import numpy as np, ml_dtypes
CORES = [23,119,17,113]
N = 4
import mx_ref
BF = ml_dtypes.bfloat16
def gcols(t, e):
    v = np.concatenate([t.reshape(8, 16, -1, 4), np.zeros((8, 16, 1, 4), BF)], axis=2)
    return np.ascontiguousarray(np.stack([v[g][:, e[g]] for g in range(8)])).reshape(128, -1)
def tile(rs):
    return np.stack(rs, axis=2).reshape(128, -1).astype(BF)
def pick(q, e):
    c = np.concatenate([q[0].reshape(128, -1, 4), np.zeros((128, 1, 4), np.uint8)], axis=1); s = np.concatenate([q[1], np.ones((16, 1), np.uint8)], axis=1)
    return (np.ascontiguousarray(c[:, e].reshape(128, -1)), np.ascontiguousarray(s[:, e]))
def join(*qs):
    return (np.concatenate([q[0] for q in qs], axis=1), np.concatenate([q[1] for q in qs], axis=1))
def put(q, e, v):
    c, s = q[0].reshape(128, -1, 4).copy(), q[1].copy(); c[:, e] = v[0].reshape(128, -1, 4); s[:, e] = v[1]
    return (c.reshape(128, -1), s)
def pk(c, s):
    return (np.ascontiguousarray(c), mx_ref.live(s))
def emit(q):
    return q[0], q[1]
def packed(v, rng):
    q = [mx_ref.quantize(np.ascontiguousarray(v[r])) for r in range(N)]
    return np.stack([a for a, b in q]), np.stack([mx_ref.plane(b, rng) for a, b in q])
def values_of_codes():
    e, c = np.zeros((128, 128, 4), np.float32), np.zeros((128, 2, 4), np.uint8)
    e[np.arange(128), np.arange(128), 0] = 1
    c[:127, :, 0] = np.arange(256).reshape(2, 128).T[:127]
    return mx_ref.matmul(mx_ref.quantize(e.reshape(128, 512).astype(BF)), (c.reshape(128, 8), np.full((16, 2), 127, np.uint8))).T.reshape(-1).astype(np.float64)
CODE_VALUE, SCALE_VALUE = values_of_codes(), 2.0 ** (np.arange(256) - 127.0)
def decode(q):
    return (CODE_VALUE[q[0]].reshape(16, 8, -1, 4) * SCALE_VALUE[q[1]][:, None, :, None] + 0.0).reshape(128, -1).astype(np.float32)
def f(rng, *shape):
    return mx_ref.flush((rng.standard_normal(shape, dtype=np.float32) * np.exp2(rng.integers(-2, 3, shape[:-1] + (1,)))).astype(BF))
def wide(rng, *shape, cols=0):
    v = rng.standard_normal(shape, dtype=np.float32) * np.exp2(rng.integers(-12, 13, shape)).astype(np.float32)
    if cols: v *= np.repeat(np.exp2(rng.integers(-cols, cols + 1, shape[:-2] + (1, shape[-1] // 4))) * (rng.random(shape[:-2] + (1, shape[-1] // 4)) > 0.0625), 4, axis=-1).astype(np.float32)
    return mx_ref.flush(v.astype(BF))
C, R, SWEEPS = 320, 2, 12
def order(p):
    return np.argsort(-(p[::16] + np.float32(0.0)), axis=1, kind="stable")
def matched(a, b):
    gap = np.abs(a.reshape(8, C // 16, 16, 1) - b.reshape(8, C // 16, 1, 16))
    l = np.arange(16)
    k = np.zeros((8, C // 16, 16), np.int64)
    for s in range(SWEEPS):
        at = (l // 2) ^ k
        here = at[:, :, :, None] == l
        best = np.argmin(np.where(here, gap, np.float32(np.inf)), axis=2)
        stays = np.take_along_axis(best, at, axis=2) == l
        k = k + ~stays
    left = np.argsort(here.any(axis=2), axis=2, kind="stable")
    turn = np.argsort(np.argsort(stays, axis=2, kind="stable"), axis=2)
    m = np.where(stays, at, np.take_along_axis(left, turn, axis=2))
    return (m + 16 * np.arange(C // 16)[:, None]).reshape(8, C)
def same(u):
    return np.stack([u] * N)
def numbers_of(rng):
    return {"x": np.array(f(rng, N, 128, 4 * C)), "u": same(np.array(f(rng, 128, 512))), "v": np.array(f(rng, N, 128, 512))}
def packed_layer(w):
    return w.reshape(N, 128, 2048)
def weights(rng, w):
    c, p = packed(packed_layer(w), rng)
    return {"wc": c, "ws": p}
def apart(rng, free):
    w = np.array(f(rng, N, 128, 2048)).reshape(N, 8, 16, 4, 8, 16, 4)
    w[:, :, ~free] = 0
    w[:, :, :, :, :, ~free] = 0
    return weights(rng, w)
def digits(n, k):
    return n[..., None] & (1 << np.arange(k))
def deciding(rng, a, b, k):
    u = np.array(f(rng, 128, 512)).reshape(128, 128, 4)
    for h, m in ((0, a), (1, b)):
        u[:, h::16] = 0
        for g in range(8): u[16 * g:16 * g + 16, 16 * g + h] = (m * k[g]).astype(np.float32).astype(BF)
    return same(u.reshape(128, 512))
def setup_inputs(rng):
    return {**numbers_of(rng), **weights(rng, f(rng, N, 128, 2048))}
def setup_inputs_ties(rng):
    d = numbers_of(rng)
    e = rng.permutation(N)
    x = d["x"].reshape(N, 8, 16, C, 4)
    for r in range(N):
        k = np.zeros(C, int) if r == e[0] else rng.permutation(C) % 3
        a = x[r][:, :8, :3].copy()
        a[:, :, 2] = 0
        x[r][:, :8] = a[:, :, k]
    x[e[1]] = 0
    u = d["u"][0].reshape(8, 16, 128, 4)
    u[:, 8:, ::16] = 0
    u[:, 8:, 1::16] = 0
    w = np.array(f(rng, N, 128, 2048)).reshape(N, 8, 16, 4, 8, 16, 4)
    w[:, :, 8:, :, :, :8] = 0
    return {"x": x.reshape(N, 128, 4 * C), "u": same(u.reshape(128, 512)), "v": d["v"], **weights(rng, w)}
def setup_inputs_near(rng):
    d = numbers_of(rng)
    x = d["x"].astype(np.float32).reshape(N, 8, 16, C, 4)
    s = digits(np.arange(C) // 2, 8) * 2.0 ** -23
    e = digits(rng.integers(0, 24, (N, 8, C)), 8) * 2.0 ** -23
    m = ((np.arange(N) + rng.integers(2)) % 2 * 2.0 - 1.0)[:, None, None]
    x[:, :, :2] = 0
    x[:, :, 0, :, 0] = rng.choice([-1.0, 1.0], (N, 8, 1))
    x[:, :, 0, :, 1] = m * 2.0 ** -9
    x[:, :, 1, :, 0] = m
    x[:, :, 2:8] = rng.integers(4, 8, (N, 8, 6, C, 4)) * rng.choice([-1.0, 1.0], (N, 8, 6, C, 4)) * 0.25
    x[:, :, 8] = s[:, :4]
    x[:, :, 9] = s[:, 4:]
    x[:, :, 10] = e[..., :4]
    x[:, :, 11] = e[..., 4:]
    x[:, :, 12:] = rng.integers(4, 8, (N, 8, 4, C, 4)) * rng.choice([-1.0, 1.0], (N, 8, 4, C, 4)) * 2.0 ** -20
    x *= np.float32(2.0 ** -7)
    a, b = np.zeros((16, 4)), np.zeros((16, 4))
    a[0, 0] = 1
    a[8:10] = 1
    b[0, 1] = 1
    b[1, 0] = 1
    b[10:12] = 1
    i = np.arange(16)
    return {"x": x.reshape(N, 128, 4 * C).astype(BF), "u": deciding(rng, a, b, np.where(rng.permutation(8) < 4, 2.0 ** -30, 1.0)), "v": d["v"], **apart(rng, (i >= 2) & (i < 8))}
def setup_inputs_jilts(rng):
    d = numbers_of(rng)
    i = np.argsort(rng.random((N, 8, C)), axis=2)
    q = 1 + np.argsort(rng.random((N, 8, C // 16, 2, 8)), axis=4)
    q[:, :, :, 0] += 8
    q = q.reshape(N, 8, C // 16, 16)
    q[:, :, 1::3] = 1 + np.argsort(rng.random((N, 8, C // 16, 16)), axis=3)[:, :, 1::3]
    q[:, :, 2::3] = 8
    m = np.take_along_axis(q.reshape(N, 8, C), i, axis=2) * ((np.arange(N) + rng.integers(2)) % 2)[:, None, None]
    x = d["x"].astype(np.float32).reshape(N, 8, 16, C, 4)
    n = rng.integers(1, 64, (N, 8, C, 32)) * rng.choice([-0.0625, 0.0625], (N, 8, C, 32))
    np.put_along_axis(n, rng.integers(0, 32, (N, 8, C, 1)), -32640.0, axis=3)
    x[:, :, :8] = n.reshape(N, 8, C, 8, 4).transpose(0, 1, 3, 2, 4)
    x[:, :, 8:] = 0
    s = digits(C - 1 - i, 12)
    for k in range(3): x[:, :, 8 + k] = s[..., 4 * k:4 * k + 4]
    s = digits(m, 8) * rng.choice([-1.0, 1.0], (N, 8, C, 1))
    for k in range(2): x[:, :, 12 + k] = s[..., 4 * k:4 * k + 4]
    a, b = np.zeros((16, 4)), np.zeros((16, 4))
    a[8:11] = 1
    b[12:14] = 1
    return {"x": x.reshape(N, 128, 4 * C).astype(BF), "u": deciding(rng, a, b, np.ones(8)), "v": d["v"], **apart(rng, np.arange(16) < 8)}
def setup_inputs_huge(rng):
    d = numbers_of(rng)
    x = 2.0 ** 30 * (0.9 + 0.1 * rng.random((N, 8, 16, C, 4)))
    c = np.stack([rng.permutation(C) % 2 * 2.0 - 1.0 for r in range(N)])
    c[rng.permutation(N) < N // 2] = 1
    x[:, :, :6] *= c[:, None, None, :, None]
    x[:, :, 6:] *= ((np.arange(N) + rng.integers(2)) % 2 * 2.0 - 1.0)[:, None, None, None, None]
    u = d["u"][0].reshape(8, 16, 128, 4)
    for h, i, j in ((0, 0, 6), (1, 6, 16)):
        a = 2.0 ** 30 * (1 - 0.05 * rng.random((8, j - i, 8, 4))) * (rng.permutation(8) % 2 * 2.0 - 1.0)[:, None]
        u[:, :, h::16] = 0
        u[:, i:j, h::16] = a.astype(np.float32).astype(BF)
    w = np.zeros((N, 128, 4, 128, 4), np.float32)
    i = np.flatnonzero(np.arange(128) % 16 >= 14)
    for b in range(4): w[:, i, b, i, b] = 8
    return {"x": x.astype(np.float32).reshape(N, 128, 4 * C).astype(BF), "u": same(u.reshape(128, 512)), "v": d["v"], **weights(rng, w.astype(BF))}
def setup_inputs_spread(rng):
    d = setup_inputs(rng)
    d["x"] = wide(rng, N, 128, 4 * C, cols=6)
    return d
def check_inputs(d):
    b = []
    for k in ("x", "u", "v"):
        a = np.abs(d[k].astype(np.float32))
        if not (np.isfinite(a).all() and ((a == 0) | (a >= 2.0 ** -30) & (a <= 2.0 ** 30)).all()): b.append("a value of " + k)
    if (d["u"].astype(np.float32) != d["u"][:1].astype(np.float32)).any(): b.append("u differs between ranks")
    if ((d["wc"] & 127) == 127).any(): b.append("a code of wc")
    return b
def reference(x, u, v, wc, ws):
    qu = mx_ref.quantize(u[0])
    lay = [pk(wc[r], ws[r]) for r in range(N)]
    now = [mx_ref.quantize(x[r]) for r in range(N)]
    for t in range(R):
        o, mark, num, wed = [], [], [], []
        for r in range(N):
            p = mx_ref.matmul(qu, now[r])
            o.append(order(p))
            mark.append(np.take_along_axis(p[1::16], o[r], axis=1))
            num.append(decode(now[r]).astype(BF))
        for r in range(N):
            e = (r + 1) % N
            w = np.zeros((8, C), np.int64)
            np.put_along_axis(w, o[r], np.take_along_axis(o[e], matched(mark[r], mark[e]), axis=1), axis=1)
            wed.append(w)
        came = [decode(mx_ref.quantize(gcols(num[r], np.argsort(wed[r], axis=1)))) for r in range(N)]
        for r in range(N):
            wives = gcols(num[(r + 1) % N], wed[r]).astype(np.float32)
            q = mx_ref.quantize(np.maximum(wives, came[(r - 1) % N]).astype(BF))
            a = num[r].astype(np.float32).reshape(128, C, 4)
            now[r] = mx_ref.quantize(tile([a[:, :, b] + mx_ref.matmul(pick(lay[r], np.arange(128 * b, 128 * b + 128)), q) * np.float32(0.03125) for b in range(4)]))
    y, ol = np.zeros((N, 128, C), np.float32), np.zeros((N, 8, C), np.float32)
    oc, osc = np.zeros((N, 128, 4 * C), np.uint8), np.zeros((N, 16, C), np.uint8)
    for r in range(N):
        y[r] = mx_ref.matmul(mx_ref.quantize(v[r]), now[r])
        ol[r] = wed[r]
        oc[r], osc[r] = emit(now[r])
    return {"y": y, "ol": ol, "oc": oc, "osc": osc}

@@ -1,0 +1,734 @@
+import math
+from concourse.mybir import dt, AluOpType, AxisListType, ActivationFunctionType
+
+A = AluOpType
+F = ActivationFunctionType
+C, NR, SW, NB = 320, 2, 12, 80
+BIG, GG = 1.0e29, 131072.0
+LN2 = math.log(2.0)
+X4, U8, BF, F32, I32, U16 = "float8_e4m3fn_x4", "uint8", "bfloat16", "float32", "int32", "uint16"
+E0, KN, WB, WQ, W1, WG, SS, FA, FB, KG, KS, NT = 0, 4, 5, 6, 10, 13, 16, 18, 19, 21, 22, 23
+SOFF, SWID = [0, 320, 576, 768, 896], [320, 256, 192, 128, 128]
+COFF, CWID = [0, 256, 512, 640, 768, 896], [256, 256, 128, 128, 128, 128]
+CZERO = [192, 128, 64, 0, 64, 0]
+PAD = 112
+QOFF = [PAD + COFF[i] + PAD * i for i in range(6)]
+
+SCRATCH, SUB = {}, {}
+
+
+def _b(names, n, d):
+    for s in names.split():
+        SCRATCH[s] = ("sbuf", [128, n], d)
+
+
+def _q(names, n):
+    for s in names.split():
+        SCRATCH[s + "c"] = ("sbuf", [128, n], X4)
+        SCRATCH[s + "s"] = ("sbuf", [128, n], U8)
+
+
+def _s(buf, names, d):
+    for i, s in enumerate(names.split()):
+        SUB[s] = (buf, 24 * i, {"uoff": 16, "al": 24, "bl": 24, "ko": 8, "so": 8}.get(s, 20))
+    _b(buf, 24 * len(names.split()), d)
+
+
+_b("xt at zt xn vp vo vg gp go", 4 * C, BF)
+_b("ut vt wt xs rt st gt zb", 512, BF)
+_b("h1 h2", 544, BF)
+_b("cb", 512 * NT, BF)
+_b("sot cot", 4096, BF)
+_b("jk", 3040, BF)
+_b("m16 k16 k01 pen m10 k10 bm mko mkn ru e16 g2", C, BF)
+_b("iot r16 r10 mk mn ms tmp sb ls sa sq orow onr wrow", C, F32)
+_b("aex d0 dd thr", 384, F32)
+_b("pkr pkb", 768, BF)
+_b("nr lsr wr", 128, BF)
+_b("ssr msr tk", 256, BF)
+_b("pb", 8, BF)
+_b("pi", 64, I32)
+_b("pf", 80, F32)
+_b("tw", 64, F32)
+_b("li", 96, I32)
+_s("sf", "rs pre cbs fx", F32)
+_s("si", "pli pni t1 t2 bo bn", I32)
+_s("of", "uoff xy al bl o32 n32 ix1 ko so", U16)
+_s("snd", "pl0 pl1 ol0 ol1 hl0 hl1", U16)
+_s("lnd", "lp0 lp1 ln0 ln1 lv0 lv1 lh0 lh1", U16)
+_q("lw", 512)
+_q("u v wt xs st s2 gt", 128)
+_q("up", 256)
+_q("x0 x1 x2 g0 g1 n0 n1 p0 p1 z", C)
+_q("c", 128 * NT)
+_q("k", 640)
+_q("so", 1024)
+_q("co", QOFF[5] + 128)
+_q("h", 528)
+for _i in range(8):
+    SCRATCH["b%d" % _i] = ("psum", [128, 512], F32)
+SEMAPHORES = ["V", "S", "P", "G", "loc"] + ["d%d" % i for i in range(28)] + \
+             [a + str(r) for r in range(NR) for a in ("an", "ap", "al", "ao", "av", "ah")]
+
+
+def emit(g, T, ops):
+    Q = {"V": g.vector, "S": g.scalar, "P": g.tensor, "G": g, "Y": g.sync}
+    lastw, readers, deps = {}, {}, []
+    for i, o in enumerate(ops):
+        d = set()
+        for k in o["R"]:
+            if k in lastw:
+                d.add(lastw[k])
+            if k.startswith("ps"):
+                d.update(j for j in readers.get(k, []) if ops[j]["e"] != o["e"])
+        for k in o["W"]:
+            if k in lastw:
+                d.add(lastw[k])
+            d.update(readers.get(k, []))
+        for k in o["R"]:
+            readers.setdefault(k, []).append(i)
+        for k in o["W"]:
+            lastw[k] = i
+            readers[k] = []
+        d.discard(i)
+        deps.append([j for j in d if ops[j]["k"] != "r" and not (o["e"] == "P" and ops[j]["e"] == "P")])
+    ev, cnt, nd, tot = [], {}, [0], {}
+    for o in ops:
+        if o["k"] == "c":
+            cnt[o["e"]] = cnt.get(o["e"], 0) + 1
+            ev.append((o["e"], cnt[o["e"]]))
+        elif o["k"] == "d":
+            ev.append(("d%d" % nd[0], 16))
+            nd[0] += 1
+        elif o["k"] == "a":
+            ev.append((o["sem"], o["n"]))
+        else:
+            ev.append(None)
+    known = {e: {} for e in Q}
+    clock, waits, need = [], [], set()
+    for i, o in enumerate(ops):
+        if o["k"] == "a":
+            clock.append({ev[i][0]: ev[i][1]})
+            waits.append([])
+            continue
+        kn, w = known[o["e"]], []
+        for j in sorted(deps[i], reverse=True):
+            s, v = ev[j]
+            if kn.get(s, 0) < v:
+                w.append(j)
+                need.add(j)
+                for s2, v2 in clock[j].items():
+                    kn[s2] = max(kn.get(s2, 0), v2)
+        waits.append(w)
+        c = dict(kn)
+        if ev[i] is not None:
+            c[ev[i][0]] = max(c.get(ev[i][0], 0), ev[i][1])
+        clock.append(c)
+    last = {}
+    for i, o in enumerate(ops):
+        if o["k"] == "c":
+            last[o["e"]] = i
+    need.update(last.values())
+    val, n = {}, {}
+    for i, o in enumerate(ops):
+        if o["k"] == "c":
+            if i in need:
+                n[o["e"]] = n.get(o["e"], 0) + 1
+                val[i] = n[o["e"]]
+        elif ev[i] is not None:
+            val[i] = ev[i][1]
+    for i, o in enumerate(ops):
+        if o["k"] == "a":
+            tot[o["sem"]] = o["n"]
+            continue
+        q = Q[o["e"]]
+        for j in waits[i]:
+            q.wait_ge(T.sem[ev[j][0]], val[j])
+        ins = o["f"](q)
+        if o["k"] == "c" and i in need:
+            ins.then_inc(T.sem[o["e"]], 1)
+            tot[o["e"]] = val[i]
+        elif o["k"] == "d":
+            ins.then_inc(T.sem[ev[i][0]], 16)
+            tot[ev[i][0]] = 16
+        elif o["k"] == "r":
+            tot["loc"] = tot.get("loc", 0) + o["n"]
+    for s, v in tot.items():
+        g.wait_ge(T.sem[s], v)
+
+
+def rank_program(g, core, T, topo):
+    rank = T.rank_of(core)
+    if rank is None:
+        return
+    n_ranks = len(T.cores)
+    nxt, prv = T.cores[(rank + 1) % n_ranks], T.cores[(rank - 1) % n_ranks]
+    ops, bgq = [], []
+
+    def op(e, f, R, W, k="c", **kw):
+        ops.append(dict(e=e, f=f, R=R.split(), W=W.split(), k=k, **kw))
+
+    def ts(out, in0, s1, s2, o0, o1, R, W):
+        if s2 is None:
+            op("V", lambda q: q.tensor_scalar(out, in0, s1, None, o0), R, W)
+        else:
+            op("V", lambda q: q.tensor_scalar(out, in0, s1, s2, o0, o1), R, W)
+
+    def tt(out, a, b, o, R, W):
+        op("V", lambda q: q.tensor_tensor(out, a, b, o), R, W)
+
+    def cp(out, a, R, W):
+        op("V", lambda q: q.tensor_copy(out, a), R, W)
+
+    def ms(out, c, W):
+        op("V", lambda q: q.memset(out, c), "", W)
+
+    def scan(out, d0, d1, init, o0, o1, R, W):
+        op("V", lambda q: q.tensor_tensor_scan(out, d0, d1, init, o0, o1), R, W)
+
+    def qz(name, a, b, src, R, W):
+        op("V", lambda q: q.quantize_mx(T[name + "c"][:, a:b], T[name + "s"][:, a:b], src), R, W)
+
+    def act(out, a, func, R, W, **kw):
+        op("S", lambda q: q.activation(out, a, func, **kw), R, W)
+
+    def af(out, a, scale, bias, R, W):
+        act(out, a, F.Identity, R, W, scale=scale, bias=bias)
+
+    def zero(buf, a, b, W, step=1):
+        act(buf[:, a:b:step], T.zb[:, 0:(b - a + step - 1) // step], F.Copy, "zb", W)
+
+    def pick(dst, a, src, b, w, off, n, R, W):
+        cp(T[dst + "c"][:, a:a + n].bitcast(dt.uint32), T[src + "c"][:, b:b + w].bitcast(dt.uint32).indirect(off), R, W + "c")
+        act(T[dst + "s"][:, a:a + n], T[src + "s"][:, b:b + w].indirect(off), F.Copy, R, W + "s")
+
+    def mm(bank, n, lhs, rhs, start, stop, R):
+        (ln, la), (rn, ra) = lhs, rhs
+        op("P", lambda q: q.matmul_mx(T["b%d" % bank][:, 0:n], T[ln + "c"][:, la:la + 128], T[ln + "s"][:, la:la + 128],
+                                      T[rn + "c"][:, ra:ra + n], T[rn + "s"][:, ra:ra + n], start, stop), R, "ps%d" % bank)
+
+    def dma(e, out, a, R, W):
+        op(e, lambda q: q.dma_start(out, a), R, W, k="d")
+
+    def iota(out, pat, base, cm, W, small=True):
+        if small:
+            op("G", lambda q: q.iota(out, pat, base, cm, allow_small_or_imprecise_dtypes=True), "", W)
+        else:
+            op("G", lambda q: q.iota(out, pat, base, cm), "", W)
+
+    def sel(out, a, pat, o, fill, base, cm, R, W):
+        op("G", lambda q: q.affine_select(out, a, pat, o, fill, base, cm), R, W)
+
+    def send(dst, out, a, sem, R):
+        rid, pid, _ = topo.addr(dst)
+        m = topo.mask(core, dst)
+        op("G", lambda q: q.remote_dma(out, a, T.sem[sem], T.sem.loc, pid, rid, m), R, "", k="r", n=len(topo.engines(core, dst)))
+
+    def send_q(dst, src, land, sem, R):
+        send(dst, T[land + "c"][:].bitcast(dt.uint8), T[src + "c"][:].bitcast(dt.uint8), sem, R)
+        send(dst, T[land + "s"][:], T[src + "s"][:], sem, R)
+
+    def arrive(src, sem, calls, W):
+        op("G", None, "", W, k="a", sem=sem, n=calls * len(topo.engines(src, core)))
+
+    def bg(n=1):
+        for _ in range(min(n, len(bgq))):
+            bgq.pop(0)()
+
+    def L(f, *a, **kw):
+        bgq.append(lambda: f(*a, **kw))
+
+    def sub(name, a=0, b=None):
+        buf, o, n = SUB[name]
+        return T[buf][:, o + a:o + (n if b is None else b)]
+
+    def ct(i):
+        return ("c", 128 * i)
+
+    def cb(i, n=1):
+        return T.cb[:, 512 * i:512 * (i + n)]
+
+    def cslot(i, t, a=0, b=128):
+        return T.cb[:, 512 * i + 4 * a + t:512 * i + 4 * b:4]
+
+    def slot(buf, t, n=NB):
+        return buf[:, t:4 * n:4]
+
+    banks = (0, 1, 3, 4)
+    ps = [T["b%d" % i] for i in range(8)]
+    pi, pf, li = T.pi, T.pf, T.li
+    SH, AND, EQ = A.logical_shift_right, A.bitwise_and, A.is_equal
+
+    def pc(i, n=1):
+        return pf[:, i:i + n]
+
+    dma("Y", T.xt[:], T.x[:], "", "xt")
+    dma("S", T.ut[:], T.u[:], "", "ut")
+    iota(pi[:, 0:1], [[0, 1]], 0, 1, "pi0", False)
+    iota(li[:, 0:16], [[1, 2], [16, 8]], 0, 0, "li0", False)
+    iota(T.r16[:], [[0, 20], [1, 16]], 0, 0, "r16")
+    iota(li[:, 16:36], [[16, 20]], 0, 0, "li1", False)
+    iota(T.wr[:], [[1, 8], [0, 16]], 0, 0, "wr")
+    iota(li[:, 36:60], [[0, 3], [10, 8]], 0, 0, "li2", False)
+    iota(T.r10[:], [[0, 32], [1, 10]], 0, 0, "r10")
+    dma("Y", T.lwc[:].bitcast(dt.uint8), T.wc[:], "", "wq")
+    dma("Y", T.lws[:], T.ws[:], "", "wsc")
+    dma("Y", T.vt[:], T.v[:], "", "vt")
+    ms(T.zb[:], 0.0, "zb")
+    for c, s, m in ((5, 0, 15), (1, 4, 7), (2, 1, 7), (3, 0, 1), (4, 3, 1), (6, 6, 1), (7, 2, 15), (8, 0, 3)):
+        ts(pi[:, c:c + 1], pi[:, 0:1], s, m, SH, AND, "pi0", "pi%d" % c)
+    cp(sub("uoff"), li[:, 0:16], "li0", "uoff")
+    cp(pc(1, 8), pi[:, 1:9], "pi1 pi2 pi3 pi4 pi5 pi6 pi7 pi8", "pf")
+    for u in range(4):
+        ms(T.sot[:, 4 * (SOFF[u] + SWID[u] - 48):4 * (SOFF[u] + SWID[u])], 0.0, "sz%d" % u)
+    ts(T.e16[:], T.r16[:], pc(5), None, EQ, None, "r16 pf", "e16")
+    ts(T.k01[:], T.r16[:], 0.0, None, A.is_gt, None, "r16", "k01")
+    zero(T.sot, 4 * SOFF[4], 4096, "sz4")
+    af(pc(10), pc(1), 1.0, 0.0, "pf", "L0")
+    af(pc(11), pc(1), 1.0, 8.0, "pf", "L1")
+    af(pc(12), pc(4), 8.0, pc(1), "pf", "L2")
+    af(pc(13), pc(2), 1.0, 0.0, "pf", "S0")
+    af(pc(14), pc(2), 1.0, 0.0, "pf", "S1")
+    af(pc(15), pc(2), 1.0, 8.0, "pf", "S2")
+    af(T.m16[:], T.e16[:], 2 * BIG, -BIG, "e16", "m16")
+    af(T.k16[:], T.k01[:], 2 * BIG, -BIG, "k01", "k16")
+    for t in range(4):
+        ts(cslot(WB, t), T.wr[:], pc(1), None, EQ, None, "wr pf", "cWB%d" % t)
+    for i in range(3):
+        qz("co", QOFF[i] - PAD, QOFF[i] - PAD + 128, T.zb[:], "zb", "coq%d" % i)
+    qz("u", 0, 128, T.ut[:], "ut", "uq")
+    pick("up", 0, "u", 0, 128, sub("uoff"), 256, "uq uoff", "up")
+    qz("x0", 0, C, T.xt[:], "xt", "x0")
+    send_q(prv, "x0", "n0", "an0", "x0")
+    for b in range(4):
+        sel(cb(E0 + b), T.zb[:], [[4, 128], [1, 4]], A.not_equal, 32.0, -b, -4, "zb", "cE%d" % b)
+    sel(cb(KN), T.zb[:], [[1, 128], [0, 4]], A.not_equal, -32.0, 0, -1, "zb", "cKN")
+
+    def consts_scalar():
+        af(T.pen[:], T.e16[:], -1049600.0, 1024.0, "e16", "pen")
+        af(pc(9), pc(5), 1023.0, 15.0 - 15360.0, "pf", "pf9")
+        af(pc(0), pc(5), 1024.0, -15360.0, "pf", "pf0")
+        af(pc(57), pc(3), -2.0, 1.0, "pf", "sp")
+        af(pc(54), pc(3), 160.0, 9.0, "pf", "f54")
+        af(pc(22, 3), pc(13, 3), 2.0, pc(3), "S0 S1 S2 pf", "sid")
+        af(pc(28, 3), pc(10, 3), 16.0, 1.0, "L0 L1 L2", "l16")
+        af(pc(55), pc(4), 80.0, pc(54), "pf f54", "f55")
+        af(pc(56), pc(2), 10.0, pc(54), "pf f54", "f56")
+        af(pc(37, 2), pc(10, 2), LN2, 0.0, "L0 L1", "bwa")
+        af(pc(39), pc(1), LN2, 8 * LN2, "pf", "bwb")
+        af(pc(64), pc(56), 1.0, 80.0, "f56", "f64")
+
+    L(qz, "c", 128 * WB, 128 * WQ, cb(WB), "cWB0 cWB1 cWB2 cWB3", "qWB")
+    L(cp, pi[:, 10:16], pc(10, 6), "L0 L1 L2 S0 S1 S2", "iL")
+    L(ms, sub("rs", 0, 1), 0.0, "rs0")
+    L(ts, pi[:, 16:22:2], pi[:, 10:13], 1, None, SH, None, "iL", "Aa")
+    L(cp, pi[:, 17:22:2], pi[:, 13:16], "iL", "Sa")
+    L(ts, pi[:, 22:28:2], pi[:, 10:13], 1, None, SH, None, "iL", "Ab")
+    L(ts, sub("cbs"), li[:, 16:36], pc(9), None, A.add, None, "li1 pf9", "cbs")
+
+    def xor(src, key, dst, dkey, mid):
+        for j in range(4):
+            L(ts, pi[:, 32 + 6 * j:38 + 6 * j], pi[:, src:src + 6], 1 << j, None, AND, None, key, "bit%d" % j)
+        mid[0]()
+        L(tt, pc(40, 12), pi[:, 32:56:2], pi[:, 33:56:2], A.subtract, "bit0 bit1 bit2 bit3", "dif")
+        mid[1]()
+        for t in range(3):
+            L(op, "V", lambda q, t=t: q.tensor_reduce(pc(dst + t), pf[:, 40 + t:52:3], AxisListType.X, A.add,
+                                                      apply_absolute_value=True), "dif", dkey + str(t))
+
+    xor(16, "Aa Sa", 16, "k",
+        [lambda: L(ts, li[:, 16:36], li[:, 16:36], pc(5), None, A.add, None, "li1 pf", "li1"),
+         lambda: L(ts, T.e16[:], T.r10[:], pc(5), None, EQ, None, "r10 pf", "e16")])
+    L(ts, sub("fx"), li[:, 16:36], -4.5, 0.1, A.add, A.mult, "li1", "fx")
+    L(ts, pi[:, 23:28:2], pc(16, 3), -1.0, 0.0, A.add, A.max, "k0 k1 k2", "Kb")
+    L(cp, li[:, 60:80], sub("fx"), "fx", "li3")
+    L(ts, pc(31, 3), pc(16, 3), 0.0, None, A.is_gt, None, "k0 k1 k2", "nz")
+    xor(22, "Ab Kb", 19, "q",
+        [lambda: L(ts, li[:, 80:88], li[:, 60:68], 6.0, None, A.mult, None, "li3", "li4"),
+         lambda: L(ts, T.mko[:], T.r10[:], 0.0, None, A.is_gt, None, "r10", "mko")])
+    L(ts, li[:, 60:80], li[:, 60:80], -319.0, None, A.mult, None, "li3", "li3")
+    L(tt, pc(25, 3), pc(13, 3), pc(28, 3), A.add, "S0 S1 S2 l16", "rkey")
+    L(tt, pc(34, 3), pc(19, 3), pc(28, 3), A.add, "q0 q1 q2 l16", "pk")
+    L(ts, pc(19, 3), pc(19, 3), 2.0, pc(3), A.mult, A.add, "q0 q1 q2 pf", "q0 q1 q2")
+    L(tt, li[:, 80:88], li[:, 80:88], li[:, 16:24], A.add, "li4 li1", "li4")
+    L(ts, pc(25, 3), pc(25, 3), pc(57), None, A.mult, None, "rkey sp", "rkey")
+    L(ts, pc(34, 3), pc(34, 3), pc(57), None, A.mult, None, "pk sp", "pk")
+    L(ts, pc(65, 3), pc(31, 3), -63.0, 63.0, A.mult, A.add, "nz", "z63")
+    L(ts, li[:, 16:36], li[:, 16:36], 32.0, None, A.mult, None, "li1", "li1")
+    L(tt, T.pb[:, 0:3], pc(34, 3), pc(31, 3), A.mult, "pk nz", "pb0")
+    L(tt, T.pb[:, 3:6], pc(19, 3), pc(65, 3), A.max, "q0 q1 q2 z63", "pb1")
+    L(tt, li[:, 60:80], li[:, 60:80], li[:, 16:36], A.add, "li3 li1", "li3")
+    for t in range(6):
+        L(dma, "Y", T.pkb[0:1, 128 * t:128 * t + 128], T.pb[:, t:t + 1], "pb0 pb1", "pk%d" % t)
+    L(ts, sub("ko"), li[:, 80:88], 127.0, None, A.min, None, "li4", "ko")
+    L(ts, sub("al", 0, 8), li[:, 36:44], pc(54), None, A.add, None, "li2 f54", "al0")
+    L(ts, sub("al", 8, 16), li[:, 44:52], pc(54), 80.0, A.add, A.add, "li2 f54", "al1")
+    L(ts, sub("al", 16, 24), li[:, 52:60], pc(55), None, A.add, None, "li2 f55", "al2")
+    L(cp, sub("xy"), li[:, 60:80], "li3", "xy")
+    L(ts, sub("bl", 0, 16), li[:, 36:52], 0.0, pc(56), A.mult, A.add, "li2 f56", "bl0")
+    L(ts, sub("bl", 16, 24), li[:, 52:60], 0.0, pc(64), A.mult, A.add, "li2 f64", "bl1")
+    L(ts, pc(52, 2), pc(31, 2), -200.0, None, A.mult, None, "nz", "b0")
+    L(ts, pc(68, 3), pc(31, 3), BIG, -BIG, A.mult, A.add, "nz", "z0")
+    L(tt, pc(52, 2), pc(52, 2), pc(37, 2), A.add, "b0 bwa", "b0")
+
+    def consts_pool2():
+        iota(T.iot[:], [[1, C]], 0, 0, "iot")
+        iota(T.bm[:], [[1, 10], [0, 32]], 0, 0, "bm")
+        iota(T.ssr[:], [[16, 2], [0, 8], [1, 16]], 0, 0, "ssr")
+        iota(T.nr[:], [[1, 128]], 0, 0, "nr")
+        for h in range(2):
+            s = 1 - 2 * h
+            iota(T.lsr[:, 64 * h:64 * h + 64], [[s, 16], [0, 4]], s, 0, "lsr%d" % h)
+            for u in range(2):
+                iota(T.msr[:, 128 * u + 64 * h:128 * u + 64 * h + 64], [[0, 16], [s, 4]], s * (4 * u + 1), 0, "msr%d%d" % (u, h))
+        for i in range(4):
+            sel(cb(WQ + i), cb(WB), [[0, 8], [1, 16], [-1, 4]], EQ, 0.0, -4 * i, 0, "cWB0 cWB1 cWB2 cWB3", "cWQ%d" % i)
+
+    def consts_court():
+        ms(T.cb[:, 512 * W1 + 3:512 * SS:4], 0.0, "cz")
+        for t in range(3):
+            ts(T.cb[:, 512 * WG + t:512 * SS:4], T.pkr[:, 0:384], pc(25 + t), GG, EQ, A.mult, "pkr rkey", "cWG%d" % t)
+            ts(T.cb[:, 512 * W1 + t:512 * WG:4], T.pkr[:, 384:768], pc(22 + t), None, EQ, None, "pkr sid", "cW1%d" % t)
+        qz("c", 128 * WG, 128 * SS, cb(WG, 3), "cWG0 cWG1 cWG2 cz", "qWG")
+        qz("c", 128 * W1, 128 * WG, cb(W1, 3), "cW10 cW11 cW12 cz", "qW1")
+
+    def consts_zero():
+        zero(T.cb, 512 * SS + 3, 512 * FB, "z1", 4)
+        for i in range(FB, NT):
+            zero(T.cb, 512 * i, 512 * i + 512, "z%d" % i)
+        for s in ("st", "gt"):
+            zero(T[s], 0, 512, s + "0 " + s + "1 " + s + "2")
+        for s in ("h1", "h2"):
+            zero(T[s], C, 544, s)
+
+    def consts_tail_scalar():
+        af(pc(28, 3), pc(10, 3), 1.0, 1.0, "L0 L1 L2", "l16")
+        af(pc(58), pc(2), 1.0, 2.0, "pf", "f58")
+        af(T.lsr[:], T.lsr[:], pc(57), 0.0, "lsr0 lsr1 sp", "lsr0 lsr1")
+        af(T.msr[:], T.msr[:], pc(57), 0.0, "msr00 msr01 msr10 msr11 sp", "msr00 msr01 msr10 msr11")
+        af(pc(71), pc(6), 16.0, pc(7), "pf", "g40")
+        af(pc(72), pc(6), 16.0, pc(8), "pf", "g41")
+        af(pc(59), pc(7), -1.0, pc(8), "pf", "th0")
+        af(pc(45), pc(7), -1.0, 0.0, "pf dif", "g45")
+        af(pc(61), pc(3), 16.0, 0.0, "pf", "h16")
+        af(pc(60), pc(59), 1.0, 4.0, "th0", "th1")
+        af(pc(46, 3), pc(10, 3), 1.0, pc(61), "L0 L1 L2 h16 dif", "g46")
+        af(pc(49, 3), pc(13, 3), 1.0, pc(61), "S0 S1 S2 h16 dif", "g49")
+        for j, c in enumerate((7.0, 8.0, 11.0, 12.0)):
+            af(pc(73 + j), pc(72), 1.0, c, "g41", "g7%d" % j)
+
+    def consts_tail():
+        L(ts, pc(42), pc(8), 0.0, None, EQ, None, "pf dif", "g42")
+        L(ts, pc(77), pc(5), 10.0, 128.0, A.is_ge, A.mult, "pf", "f77")
+        for t in range(3):
+            L(ts, T.tk[:, 0:128], T.lsr[:], pc(28 + t), -1.0, A.is_gt, A.mult, "lsr0 l16", "tk0")
+            L(ts, T.tk[:, 128:256], T.lsr[:], pc(28 + t), -64.0, EQ, A.mult, "lsr0 l16", "tk1")
+            L(ts, T.cb[:, 512 * SS + t:512 * FA:4], T.ssr[:], pc(22 + t), 0.5, EQ, A.mult, "ssr sid", "cSS%d" % t)
+            L(tt, cslot(FA, t), T.tk[:, 0:128], T.tk[:, 128:256], A.add, "tk0 tk1", "cFA%d" % t)
+        L(ts, pc(43), pc(42), 7.0, 1.0, A.mult, A.add, "g42", "g43")
+        L(ts, pc(44), pc(42), -1.0, pc(7), A.add, A.mult, "g42 pf", "g44")
+        L(ts, li[:, 88:96], li[:, 36:44], pc(5), pc(77), A.add, A.add, "li2 pf f77", "li5")
+        L(ts, T.cb[:, 512 * FB + 2:512 * KG:4], T.msr[:], pc(58), None, A.is_ge, None, "msr00 f58 z19 z20", "cFB")
+        L(qz, "c", 128 * SS, 128 * FB, cb(SS, 3), "cSS0 cSS1 cSS2 cFA0 cFA1 cFA2 z1", "qSS")
+        L(ts, sub("so"), li[:, 88:96], 127.0, None, A.min, None, "li5", "so")
+        L(ts, cslot(KG, 0, 0, 32), T.nr[:, 0:32], pc(71), pc(43), EQ, A.mult, "nr g40 g43 z21", "cKGa")
+        L(ts, cslot(KG, 1, 0, 32), T.nr[:, 0:32], pc(71), None, EQ, None, "nr g40 z21", "cKGb")
+        for u in range(2):
+            L(ts, T.tk[:, 32 * u:32 * u + 32], T.nr[:, 0:32], pc(73 + 2 * u), pc(44 + u), EQ, A.mult, "nr g70 g72 g44 g45", "tk0")
+            L(ts, T.tk[:, 128 + 32 * u:160 + 32 * u], T.nr[:, 0:32], pc(74 + 2 * u), pc(7), EQ, A.mult, "nr g71 g73 pf", "tk1")
+        for t in range(3):
+            L(ts, cslot(KS, t, 0, 32), T.nr[:, 0:32], pc(46 + t), pc(13 + t), EQ, A.mult, "nr g46 S0 S1 S2 z22", "cKSa%d" % t)
+            L(ts, cslot(KS, t, 32, 64), T.nr[:, 0:32], pc(49 + t), pc(10 + t), EQ, A.mult, "nr g49 L0 L1 L2 z22", "cKSb%d" % t)
+        for u in range(2):
+            L(tt, cslot(KG, u, 32, 64), T.tk[:, 32 * u:32 * u + 32], T.tk[:, 128 + 32 * u:160 + 32 * u], A.add, "tk0 tk1 z21", "cKG%d" % u)
+        L(qz, "c", 128 * FB, 128 * KG, cb(FB, 2), "cFB", "qFB")
+        L(qz, "c", 128 * KG, 128 * NT, cb(KG, 2), "cKGa cKGb cKG0 cKG1 cKSa0 cKSa1 cKSa2 cKSb0 cKSb1 cKSb2", "qK")
+        L(qz, "c", 128 * WQ, 128 * (WQ + 2), cb(WQ, 2), "cWQ0 cWQ1", "qWa")
+        L(qz, "c", 128 * (WQ + 2), 128 * W1, cb(WQ + 2, 2), "cWQ2 cWQ3", "qWb")
+
+    def pick32(src, skey, dst, dkey):
+        tt(T.tmp[:], src[:].indirect(sub("xy")), T.m10[:], A.min, skey + " xy m10", "tmp")
+        scan(dst[:], T.k10[:], T.tmp[:], -BIG, A.min, A.max, "k10 tmp", dkey)
+
+    def decode(name, b, bank, out, okey):
+        mm(bank, C, ct(E0 + b), (name, 0), True, True, "qE " + name)
+        act(out, ps[bank][:, 0:C], F.Copy, "ps%d" % bank, okey, scale=1.0 / 32)
+
+    def plane(buf, b):
+        return buf[:, C * b:C * b + C]
+
+    def compare(d, w, base, tile0):
+        u, t = tile0 + (d - 1) // 4, (d - 1) % 4
+        n = (w - d) * 16
+        tt(T.cot[:, 4 * COFF[u] + t:4 * (COFF[u] + n):4], T.dd[:, base:base + n], T.dd[:, base + 16 * d:base + 16 * w], A.is_le,
+           ("dd1" if tile0 == 0 else "dd2") + " cz%d" % u, "co%d%d" % (u, t))
+
+    def quant_co(u):
+        qz("co", QOFF[u], QOFF[u] + CWID[u], T.cot[:, 4 * COFF[u]:4 * (COFF[u] + CWID[u])],
+           " ".join("co%d%d" % (u, t) for t in range(4)), "coq%d" % u)
+
+    def rank_mm(u, tile0, nlam, bk, last):
+        u0 = u - tile0
+        for lam in range(nlam):
+            todo = []
+            if lam == 0 or u0 < 2:
+                todo.append((QOFF[u] + 128 * lam, 4))
+            for t in range(4):
+                d = 4 * u0 + t + 1
+                if d <= 8 * lam + 7:
+                    todo.append((QOFF[u] + 128 * lam - 16 * d, t))
+            for j, (a, k) in enumerate(todo):
+                mm(bk[lam], 128, ("co", a), ("k", 128 * k), u0 == 0 and j == 0, last and j == len(todo) - 1,
+                   "coq%d k%dc k%ds" % (u, k, k))
+
+    def list_pick(tile, a, off, mask):
+        tt(T[tile][:, 0:C], T.tw[:, a:a + 32].indirect(sub(off)), T[mask][:], A.mult, "tw %s %s" % (off, mask), tile)
+
+    def list_sum(tile, a, bank):
+        qz("h", a, a + 130, T[tile][:, 0:520], tile, "a" + tile)
+        qz("h", a + 132, a + 262, T[tile][:, 4:524], tile, "b" + tile)
+        for i in (0, 2, 1, 3):
+            mm(bank, 128, ct(WQ + i), ("h", a + 132 * (i % 2) + 2 * (i // 2)), i == 0, i == 3, "qWa qWb " + "ab"[i % 2] + tile)
+
+    def list_end(bank, base, t32, out, okey):
+        tt(sub(t32), ps[bank][:, 0:80:4], sub(base), A.add, "ps%d %s" % (bank, base), t32)
+        cp(out, sub(t32), t32, okey)
+
+    def thr(t):
+        ts(T.thr[:, 128 * t:128 * t + NB], ps[5 + t][:, 0:NB], 1.0 + 2.0 / GG, pc(68 + t), A.mult, A.add, "ps%d z0" % (5 + t), "thr%d" % t)
+
+    for r in range(NR):
+        s = str(r)
+        xq, first, final = "x" + s, r == 0, r == NR - 1
+        pl, olist, hl, lp, ln, lv, lh = (sub(a + s) for a in ("pl", "ol", "hl", "lp", "ln", "lv", "lh"))
+        mm(0, C, ("up", 0), (xq, 0), True, True, "upc ups " + xq)
+        mm(1, C, ("up", 128), (xq, 0), True, True, "upc ups " + xq)
+        if first:
+            consts_scalar()
+        act(T.mk[:], ps[1][:, 0:C], F.Copy, "ps1", "mk")
+        bg(2)
+        tt(T.sq[:], ps[0][:, 0:C], T.m16[:], A.min, "ps0 m16", "sq")
+        bg(1)
+        scan(T.sb[:], T.k16[:], T.sq[:], -BIG, A.min, A.max, "k16 sq", "sb")
+        bg(1)
+        for u in range(5):
+            for t in range(4):
+                i = 20 - 4 * u - t
+                view = T.sot[:, 4 * SOFF[u] + t:4 * (SOFF[u] + 16 * i):4]
+                key = "so%d%d" % (u, t)
+                if i == 20:
+                    tt(view, T.sb[:], ps[0][:, 0:C], A.is_ge, "sb ps0 sz0", key)
+                else:
+                    ts(view, ps[0][:, 0:16 * i], T.sb[:, 16 * i + 15:16 * i + 16], None, A.is_lt, None, "sb ps0 sz%d" % u, key)
+                    act(T.jk[:, 8 * i * (i - 1):8 * i * (i + 1)], view, F.Copy, key, "rs%d" % i, accum_out=sub("rs", i, i + 1))
+                bg(2)
+            if u == 0:
+                scan(T.ru[:], T.k01[:], T.sot[:, 0:4 * C:4], 0.0, A.mult, A.add, "k01 so00", "ru")
+            qz("so", SOFF[u], SOFF[u] + SWID[u], T.sot[:, 4 * SOFF[u]:4 * (SOFF[u] + SWID[u])],
+               " ".join("so%d%d" % (u, t) for t in range(4)), "soq%d" % u)
+            mm(2, SWID[u], ct(WB), ("so", SOFF[u]), u == 0, u == 4, "qWB soq%d" % u)
+            if u == 1:
+                tt(sub("pre"), sub("cbs"), T.ru[:, 15:C:16], A.subtract, "cbs ru", "pre")
+        tt(sub("pre"), sub("pre"), sub("rs"), A.subtract, "pre " + " ".join("rs%d" % i for i in range(20)), "pre")
+        scan(T.ls[:], T.pen[:], ps[2][:, 0:C], 0.0, A.add, A.max, "pen ps2", "ls")
+        bg(1)
+        tt(sub("pli"), T.ls[:, 15:C:16], sub("pre"), A.add, "ls pre", "pli")
+        bg(1)
+        cp(pl, sub("pli"), "pli", "pl" + s)
+        send(prv, lp, pl, "al" + s, "pl" + s)
+        bg(99)
+        if first:
+            op("G", lambda q: q.partition_broadcast(T.pkr[:], T.pkb[0:1, :], 128), "pk0 pk1 pk2 pk3 pk4 pk5", "pkr")
+            af(T.m10[:], T.e16[:], 2 * BIG, -BIG, "e16", "m10")
+            af(T.k10[:], T.mko[:], 2 * BIG, -BIG, "mko", "k10")
+            qz("c", 0, 512, cb(E0, 4), "cE0 cE1 cE2 cE3", "qE")
+        cp(T.ms[:].indirect(pl), T.mk[:], "mk pl" + s, "ms")
+        arrive(nxt, "an" + s, 2, "n" + s)
+        mm(1, C, ("up", 128), ("n" + s, 0), True, True, "upc ups n" + s)
+        act(T.mn[:], ps[1][:, 0:C], F.Copy, "ps1", "mn")
+        pick32(T.ms, "ms", T.sa, "sa")
+        for b in range(2):
+            decode(xq, b, 4 + b, slot(T.at, b, C), "at%d" % b)
+        act(T.aex[:], T.sa[:].indirect(sub("al")), F.Copy, "sa al0 al1 al2", "aex")
+        for b in range(2, 4):
+            decode(xq, b, 4 + b, slot(T.at, b, C), "at%d" % b)
+        if first:
+            for u in range(4):
+                zero(T.cot, 4 * (COFF[u] + CZERO[u]), 4 * (COFF[u] + CWID[u]), "cz%d" % u)
+        arrive(nxt, "al" + s, 1, "lp" + s)
+        cp(T.ms[:].indirect(lp), T.mn[:], "mn lp" + s, "ms")
+        pick32(T.ms, "ms", T.sa, "sa")
+        tt(T.d0[:, 0:256], T.sa[:].indirect(sub("bl", 0, 16)), T.aex[:, 0:256], A.subtract, "sa bl0 aex", "d01")
+        act(T.dd[:, 0:256], T.d0[:, 0:256], F.Abs, "d01", "dd1")
+        qz("g" + s, 0, C, T.at[:], "at0 at1 at2 at3", "g" + s)
+        send_q(nxt, "g" + s, "p" + s, "ap" + s, "g" + s)
+        if first:
+            consts_pool2()
+            qz("c", 128 * KN, 128 * WB, cb(KN), "cKN", "qKN")
+            qz("co", QOFF[3] - PAD, QOFF[3] - PAD + 128, T.zb[:], "zb", "coq3")
+            for i in range(5):
+                pick("k", 128 * i, "c", 128 * i, 128, sub("ko"), 128, "qE qKN ko", "k%d" % i)
+            for a in ("wt", "xs"):
+                zero(T[a], 0, 512, a + "0 " + a + "1 " + a + "2")
+            for u in range(4, 6):
+                zero(T.cot, 4 * (COFF[u] + CZERO[u]), 4 * (COFF[u] + CWID[u]), "cz%d" % u)
+            consts_zero()
+        for u in range(4):
+            for d in range(4 * u + 1, min(4 * u + 5, 16)):
+                compare(d, 16, 0, 0)
+            if first and u == 2:
+                consts_court()
+            quant_co(u)
+            rank_mm(u, 0, 2, (3, 4), u == 3)
+            if u < 3:
+                decode("n" + s, u, u % 2, plane(T.vp, u), "vp%d" % u)
+        for t in range(2):
+            act(slot(T.wt, t), ps[3 + t][:, 0:NB], F.Exp, "ps%d bwa" % (3 + t), "wt%d" % t, scale=-LN2 / 32, bias=pc(37 + t))
+        for t in range(2):
+            act(slot(T.xs, t), ps[3 + t][:, 0:NB], F.Exp, "ps%d b0" % (3 + t), "xs%d" % t, scale=-LN2 / 32, bias=pc(52 + t))
+        tt(T.d0[:, 256:384], T.sa[:].indirect(sub("bl", 16, 24)), T.aex[:, 256:384], A.subtract, "sa bl1 aex", "d02")
+        act(T.dd[:, 256:384], T.d0[:, 256:384], F.Abs, "d02", "dd2")
+        if first:
+            for i in (4, 5):
+                qz("co", QOFF[i] - PAD, QOFF[i] - PAD + 128, T.zb[:], "zb", "coq%d" % i)
+            ts(T.bm[:], T.bm[:], pc(5), None, EQ, None, "bm pf", "bm")
+        else:
+            ms(slot(T.xs, 2), 0.0, "xs2")
+        qz("wt", 0, 128, T.wt[:], "wt0 wt1 wt2", "wtq")
+        for t in range(2):
+            mm(5 + t, 128, ct(WG + t), ("wt", 0), True, True, "qWG wtq")
+        qz("xs", 0, 128, T.xs[:], "xs0 xs1 xs2", "xsq")
+        decode("n" + s, 3, 1, plane(T.vp, 3), "vp3")
+        thr(0)
+        thr(1)
+        for d in range(1, 6):
+            L(compare, d, 8, 256, 4)
+        L(quant_co, 4)
+        L(rank_mm, 4, 4, 1, (2,), False)
+        L(compare, 6, 8, 256, 4)
+        L(compare, 7, 8, 256, 4)
+        L(quant_co, 5)
+        L(rank_mm, 5, 4, 1, (2,), True)
+        L(act, slot(T.wt, 2), ps[2][:, 0:NB], F.Exp, "ps2 bwb", "wt2", scale=-LN2 / 32, bias=pc(39))
+        L(cp, sub("pni"), lp, "lp" + s, "pni")
+        L(ts, sub("t2"), sub("pli"), 31, None, AND, None, "pli", "t2")
+        L(ts, sub("bo"), sub("pli"), 496, None, AND, None, "pli", "bo")
+        L(qz, "wt", 0, 128, T.wt[:], "wt0 wt1 wt2", "wtq")
+        L(mm, 7, 128, ct(WG + 2), ("wt", 0), True, True, "qWG wtq")
+        L(cp, sub("o32"), sub("t2"), "t2", "o32")
+        L(ts, sub("t1"), sub("pni"), 31, None, AND, None, "pni", "t1")
+        L(thr, 2)
+        n_early = len(bgq)
+        L(ts, sub("bn"), sub("pni"), 496, None, AND, None, "pni", "bn")
+        L(cp, sub("n32"), sub("t1"), "t1", "n32")
+        if first:
+            consts_tail()
+        per = [1, 1, 1, 4, 4, 3, 5]
+        rest = len(bgq) - n_early
+        arrive(prv, "ap" + s, 2, "p" + s)
+        arrive(nxt, "ao" + s, 1, "ln" + s)
+        arrive(prv, "av" + s, 1, "lv" + s)
+        for k in range(SW - 1):
+            nt = 2 if k < 7 else 3
+            if k == 7:
+                bg(len(bgq) - rest)
+            for t in range(nt):
+                mm(5 + t, 128, ct(W1 + t), ("xs", 0), True, False, "qW1 xsq")
+                mm(5 + t, 128, ct(WG + t), ("xs", 0), False, True, "qWG xsq")
+            if k == 0:
+                act(T.mkn[:], T.bm[:].indirect(lp), F.Copy, "bm lp" + s, "mkn")
+                act(T.mko[:], T.bm[:].indirect(pl), F.Copy, "bm pl" + s, "mko")
+                if first:
+                    consts_tail_scalar()
+            if 2 <= k <= 5:
+                decode("p" + s, k - 2, banks[k - 2], plane(T.gp, k - 2), "gp%d" % (k - 2))
+            if k <= 3:
+                a, b = ((0, 6), (6, 12), (12, 16), (16, 20))[k]
+                cp(T.orow[:].indirect(sub("pl" + s, a, b)), T.iot[:, 16 * a:16 * b], "iot pl" + s, "orow")
+            if k == 4:
+                scan(T.ls[:], T.pen[:], T.orow[:], 0.0, A.add, A.max, "pen orow", "ls")
+            if k == 5:
+                ts(olist, T.ls[:, 15:C:16], pc(0), None, A.add, None, "ls pf0", "ol" + s)
+                send(prv, ln, olist, "ao" + s, "ol" + s)
+                send(nxt, lv, olist, "av" + s, "ol" + s)
+            if k >= 7:
+                b = k - 7
+                act(plane(T.vo, b), plane(T.vp, b).indirect(ln), F.Copy, "vp%d ln%s" % (b, s), "vo%d" % b)
+                act(plane(T.go, b), plane(T.gp, b).indirect(lv), F.Copy, "gp%d lv%s" % (b, s), "go%d" % b)
+            bg(per[k] if k < 7 else (rest + 3) // 4)
+            for t in range(nt):
+                tt(slot(T.rt, t), ps[5 + t][:, 0:NB], T.thr[:, 128 * t:128 * t + NB], A.is_gt, "ps%d thr%d" % (5 + t, t), "rt%d" % t)
+                if t:
+                    tt(slot(T.xs, t - 1), slot(T.rt, t - 1), slot(T.wt, t - 1), A.mult, "rt%d wt%d" % (t - 1, t - 1), "xs%d" % (t - 1))
+            t = nt - 1
+            tt(slot(T.xs, t), slot(T.rt, t), slot(T.wt, t), A.mult, "rt%d wt%d" % (t, t), "xs%d" % t)
+            qz("xs", 0, 128, T.xs[:], "xs0 xs1 xs2", "xsq")
+        for t in range(2):
+            mm(5 + t, 128, ct(SS + t), ("xs", 0), True, True, "qSS xsq")
+        bg(99)
+        for t in range(3):
+            tt(slot(T.st, t), ps[5 + t // 2][:, 0:NB], slot(T.xs, t), A.is_lt, "ps%d xs%d" % (5 + t // 2, t), "st%d" % t)
+        qz("st", 0, 128, T.st[:], "st0 st1 st2", "stq")
+        pick("s2", 0, "st", 0, 128, sub("so"), 128, "stq so", "s2")
+        for u in range(2):
+            mm(3 + u, 128, ct(FA), ("s2", 0), True, False, "qSS s2c s2s")
+            mm(3 + u, 128, ct(FB + u), ("s2", 0), False, True, "qFB s2c s2s")
+        mm(2, 128, ("s2", 0), ct(KS), True, False, "qK s2c s2s")
+        for u in range(2):
+            ts(slot(T.gt, u, 128), ps[3 + u][:, 0:128], pc(59 + u), None, A.is_ge, None, "ps%d th0 th1" % (3 + u), "gt%d" % u)
+        qz("gt", 0, 128, T.gt[:], "gt0 gt1 gt2", "gtq")
+        mm(2, 128, ("gt", 0), ct(KG), False, True, "qK gtq")
+        cp(T.tw[:], ps[2][:, 0:64], "ps2", "tw")
+        list_pick("h1", 32, "n32", "mkn")
+        list_sum("h1", 0, 5)
+        list_pick("h2", 0, "o32", "mko")
+        list_end(5, "bn", "t1", hl, "hl" + s)
+        send(nxt, lh, hl, "ah" + s, "hl" + s)
+        list_sum("h2", 264, 6)
+        H = C // 2
+        hb = (banks, (2, 5, 7, 6))
+        for hf in range(2):
+            for b in range(4):
+                if hb[hf][b] == 6:
+                    list_end(6, "bo", "t2", sub("ix1"), "ix1")
+                mm(hb[hf][b], H, ct(E0 + b), (xq, H * hf), True, False, "qE " + xq)
+        for b in (2, 3):
+            act(plane(T.vg, b), plane(T.vo, b).indirect(sub("ix1")), F.Copy, "vo%d ix1" % b, "vg%d" % b)
+        for b in (0, 1):
+            cp(plane(T.vg, b), plane(T.vo, b).indirect(sub("ix1")), "vo%d ix1" % b, "vg%d" % b)
+        if final:
+            qz("v", 0, 128, T.vt[:], "vt", "vq")
+        arrive(prv, "ah" + s, 1, "lh" + s)
+        for hf in range(2):
+            act(T.g2[:, H * hf:H * hf + H], plane(T.go, 3).indirect(sub("lh" + s, 10 * hf, 10 * hf + 10)), F.Copy, "go3 lh" + s, "g2%d" % hf)
+        if final:
+            act(T.onr[:], T.iot[:].indirect(ln), F.Copy, "iot ln" + s, "onr")
+        for hf in range(2):
+            for b in range(4):
+                a = plane(T.go, b).indirect(sub("lh" + s, 10 * hf, 10 * hf + 10)) if b < 3 else T.g2[:, H * hf:H * hf + H]
+                tt(T.zt[:, 4 * H * hf + b:4 * H * (hf + 1):4], a, T.vg[:, C * b + H * hf:C * b + H * hf + H], A.max,
+                   "vg3 g2%d" % hf if b == 3 else "go%d vg%d lh%s" % (b, b, s), "zt%d%d" % (hf, b))
+            qz("z", H * hf, H * hf + H, T.zt[:, 4 * H * hf:4 * H * (hf + 1)], " ".join("zt%d%d" % (hf, b) for b in range(4)), "zq%d" % hf)
+            for b in range(4):
+                mm(hb[hf][b], H, ("lw", 128 * b), ("z", H * hf), False, True, "wq wsc zq%d" % hf)
+        for hf in range(2):
+            for b in range(4):
+                o, bank = T.xn[:, 4 * H * hf + b:4 * H * (hf + 1):4], hb[hf][b]
+                if (hf == 1 and b % 2) or (hf == 0 and b == 3):
+                    ts(o, ps[bank][:, 0:H], 1.0 / 32, None, A.mult, None, "ps%d" % bank, "xn%d%d" % (hf, b))
+                else:
+                    act(o, ps[bank][:, 0:H], F.Copy, "ps%d" % bank, "xn%d%d" % (hf, b), scale=1.0 / 32)
+        xq = "x%d" % (r + 1)
+        qz(xq, 0, C, T.xn[:], "xn00 xn01 xn02 xn03 xn10 xn11 xn12 xn13", xq)
+        if not final:
+            send_q(prv, xq, "n%d" % (r + 1), "an%d" % (r + 1), xq)
+    mm(2, C, ("v", 0), (xq, 0), True, True, "vq " + xq)
+    act(T.wrow[:], T.onr[:].indirect(sub("ix1")), F.Copy, "onr ix1", "wrow")
+    dma("Y", T.oc[:], T[xq + "c"][:].bitcast(dt.uint8), xq, "")
+    for k in range(4):
+        dma("S", T.osc[4 * k:4 * k + 4, :], T[xq + "s"][32 * k:32 * k + 4, :], xq, "")
+    cp(T.orow[:], ps[2][:, 0:C], "ps2", "orow")
+    dma("Y", T.y[:], T.orow[:], "orow", "")
+    for k in range(8):
+        dma("YS"[k % 2], T.ol[k:k + 1, :], T.wrow[16 * k:16 * k + 1, :], "wrow", "")
+    emit(g, T, ops)

@@ -39,7 +39,7 @@ _b("ut vt wt xs rt st gt zb", 512, BF)
 _b("h1 h2", 544, BF)
 _b("cb", 512 * NT, BF)
 _b("sot cot", 4096, BF)
-_b("jk", 3040, BF)
+_b("jk", 3400, BF)
 _b("m16 k16 k01 pen m10 k10 bm mko mkn ru e16 g2", C, BF)
 _b("iot r16 r10 mk mn ms tmp sb ls sa sq orow onr wrow", C, F32)
 _b("aex d0 dd thr", 384, F32)
@@ -271,9 +271,6 @@ def rank_program(g, core, T, topo):
     iota(T.wr[:], [[1, 8], [0, 16]], 0, 0, "wr")
     iota(li[:, 36:60], [[0, 3], [10, 8]], 0, 0, "li2", False)
     iota(T.r10[:], [[0, 32], [1, 10]], 0, 0, "r10")
-    dma("Y", T.lwc[:].bitcast(dt.uint8), T.wc[:], "", "wq")
-    dma("Y", T.lws[:], T.ws[:], "", "wsc")
-    dma("Y", T.vt[:], T.v[:], "", "vt")
     ms(T.zb[:], 0.0, "zb")
     for c, s, m in ((5, 0, 15), (1, 4, 7), (2, 1, 7), (3, 0, 1), (4, 3, 1), (6, 6, 1), (7, 2, 15), (8, 0, 3)):
         ts(pi[:, c:c + 1], pi[:, 0:1], s, m, SH, AND, "pi0", "pi%d" % c)
@@ -298,25 +295,23 @@ def rank_program(g, core, T, topo):
         qz("co", QOFF[i] - PAD, QOFF[i] - PAD + 128, T.zb[:], "zb", "coq%d" % i)
     qz("u", 0, 128, T.ut[:], "ut", "uq")
     pick("up", 0, "u", 0, 128, sub("uoff"), 256, "uq uoff", "up")
+    af(T.pen[:], T.e16[:], -1049600.0, 1024.0, "e16", "pen")
+    af(pc(9), pc(5), 1023.0, 15.0 - 15360.0, "pf", "pf9")
+    af(pc(0), pc(5), 1024.0, -15360.0, "pf", "pf0")
+    af(pc(57), pc(3), -2.0, 1.0, "pf", "sp")
+    af(pc(54), pc(3), 160.0, 9.0, "pf", "f54")
+    af(pc(22, 3), pc(13, 3), 2.0, pc(3), "S0 S1 S2 pf", "sid")
+    af(pc(28, 3), pc(10, 3), 16.0, 1.0, "L0 L1 L2", "l16")
+    af(pc(55), pc(4), 80.0, pc(54), "pf f54", "f55")
+    af(pc(56), pc(2), 10.0, pc(54), "pf f54", "f56")
+    af(pc(37, 2), pc(10, 2), LN2, 0.0, "L0 L1", "bwa")
+    af(pc(39), pc(1), LN2, 8 * LN2, "pf", "bwb")
+    af(pc(64), pc(56), 1.0, 80.0, "f56", "f64")
     qz("x0", 0, C, T.xt[:], "xt", "x0")
     send_q(prv, "x0", "n0", "an0", "x0")
     for b in range(4):
         sel(cb(E0 + b), T.zb[:], [[4, 128], [1, 4]], A.not_equal, 32.0, -b, -4, "zb", "cE%d" % b)
     sel(cb(KN), T.zb[:], [[1, 128], [0, 4]], A.not_equal, -32.0, 0, -1, "zb", "cKN")
-
-    def consts_scalar():
-        af(T.pen[:], T.e16[:], -1049600.0, 1024.0, "e16", "pen")
-        af(pc(9), pc(5), 1023.0, 15.0 - 15360.0, "pf", "pf9")
-        af(pc(0), pc(5), 1024.0, -15360.0, "pf", "pf0")
-        af(pc(57), pc(3), -2.0, 1.0, "pf", "sp")
-        af(pc(54), pc(3), 160.0, 9.0, "pf", "f54")
-        af(pc(22, 3), pc(13, 3), 2.0, pc(3), "S0 S1 S2 pf", "sid")
-        af(pc(28, 3), pc(10, 3), 16.0, 1.0, "L0 L1 L2", "l16")
-        af(pc(55), pc(4), 80.0, pc(54), "pf f54", "f55")
-        af(pc(56), pc(2), 10.0, pc(54), "pf f54", "f56")
-        af(pc(37, 2), pc(10, 2), LN2, 0.0, "L0 L1", "bwa")
-        af(pc(39), pc(1), LN2, 8 * LN2, "pf", "bwb")
-        af(pc(64), pc(56), 1.0, 80.0, "f56", "f64")
 
     L(qz, "c", 128 * WB, 128 * WQ, cb(WB), "cWB0 cWB1 cWB2 cWB3", "qWB")
     L(cp, pi[:, 10:16], pc(10, 6), "L0 L1 L2 S0 S1 S2", "iL")
@@ -385,21 +380,12 @@ def rank_program(g, core, T, topo):
             sel(cb(WQ + i), cb(WB), [[0, 8], [1, 16], [-1, 4]], EQ, 0.0, -4 * i, 0, "cWB0 cWB1 cWB2 cWB3", "cWQ%d" % i)
 
     def consts_court():
-        ms(T.cb[:, 512 * W1 + 3:512 * SS:4], 0.0, "cz")
         for t in range(3):
-            ts(T.cb[:, 512 * WG + t:512 * SS:4], T.pkr[:, 0:384], pc(25 + t), GG, EQ, A.mult, "pkr rkey", "cWG%d" % t)
-            ts(T.cb[:, 512 * W1 + t:512 * WG:4], T.pkr[:, 384:768], pc(22 + t), None, EQ, None, "pkr sid", "cW1%d" % t)
-        qz("c", 128 * WG, 128 * SS, cb(WG, 3), "cWG0 cWG1 cWG2 cz", "qWG")
-        qz("c", 128 * W1, 128 * WG, cb(W1, 3), "cW10 cW11 cW12 cz", "qW1")
-
-    def consts_zero():
-        zero(T.cb, 512 * SS + 3, 512 * FB, "z1", 4)
-        for i in range(FB, NT):
-            zero(T.cb, 512 * i, 512 * i + 512, "z%d" % i)
-        for s in ("st", "gt"):
-            zero(T[s], 0, 512, s + "0 " + s + "1 " + s + "2")
-        for s in ("h1", "h2"):
-            zero(T[s], C, 544, s)
+            a = 2 * (t // 2)
+            ts(T.cb[:, 512 * (WG + a) + t:512 * SS:4], T.pkr[:, 128 * a:384], pc(25 + t), GG, EQ, A.mult, "pkr rkey", "cWG%d" % t)
+            ts(T.cb[:, 512 * (W1 + a) + t:512 * WG:4], T.pkr[:, 384 + 128 * a:768], pc(22 + t), None, EQ, None, "pkr sid", "cW1%d" % t)
+        qz("c", 128 * WG, 128 * SS, cb(WG, 3), "cWG0 cWG1 cWG2 cy1 cy3", "qWG")
+        qz("c", 128 * W1, 128 * WG, cb(W1, 3), "cW10 cW11 cW12 cy0 cy2", "qW1")
 
     def consts_tail_scalar():
         af(pc(28, 3), pc(10, 3), 1.0, 1.0, "L0 L1 L2", "l16")
@@ -416,6 +402,9 @@ def rank_program(g, core, T, topo):
         af(pc(49, 3), pc(13, 3), 1.0, pc(61), "S0 S1 S2 h16 dif", "g49")
         for j, c in enumerate((7.0, 8.0, 11.0, 12.0)):
             af(pc(73 + j), pc(72), 1.0, c, "g41", "g7%d" % j)
+        zero(T.cb, 512 * SS + 3, 512 * FB, "z1", 4)
+        for i in range(FB, NT):
+            zero(T.cb, 512 * i, 512 * i + 512, "z%d" % i)
 
     def consts_tail():
         L(ts, pc(42), pc(8), 0.0, None, EQ, None, "pf dif", "g42")
@@ -430,6 +419,7 @@ def rank_program(g, core, T, topo):
         L(ts, li[:, 88:96], li[:, 36:44], pc(5), pc(77), A.add, A.add, "li2 pf f77", "li5")
         L(ts, T.cb[:, 512 * FB + 2:512 * KG:4], T.msr[:], pc(58), None, A.is_ge, None, "msr00 f58 z19 z20", "cFB")
         L(qz, "c", 128 * SS, 128 * FB, cb(SS, 3), "cSS0 cSS1 cSS2 cFA0 cFA1 cFA2 z1", "qSS")
+        L(qz, "c", 128 * FB, 128 * KG, cb(FB, 2), "cFB", "qFB")
         L(ts, sub("so"), li[:, 88:96], 127.0, None, A.min, None, "li5", "so")
         L(ts, cslot(KG, 0, 0, 32), T.nr[:, 0:32], pc(71), pc(43), EQ, A.mult, "nr g40 g43 z21", "cKGa")
         L(ts, cslot(KG, 1, 0, 32), T.nr[:, 0:32], pc(71), None, EQ, None, "nr g40 z21", "cKGb")
@@ -441,7 +431,6 @@ def rank_program(g, core, T, topo):
             L(ts, cslot(KS, t, 32, 64), T.nr[:, 0:32], pc(49 + t), pc(10 + t), EQ, A.mult, "nr g49 L0 L1 L2 z22", "cKSb%d" % t)
         for u in range(2):
             L(tt, cslot(KG, u, 32, 64), T.tk[:, 32 * u:32 * u + 32], T.tk[:, 128 + 32 * u:160 + 32 * u], A.add, "tk0 tk1 z21", "cKG%d" % u)
-        L(qz, "c", 128 * FB, 128 * KG, cb(FB, 2), "cFB", "qFB")
         L(qz, "c", 128 * KG, 128 * NT, cb(KG, 2), "cKGa cKGb cKG0 cKG1 cKSa0 cKSa1 cKSa2 cKSb0 cKSb1 cKSb2", "qK")
         L(qz, "c", 128 * WQ, 128 * (WQ + 2), cb(WQ, 2), "cWQ0 cWQ1", "qWa")
         L(qz, "c", 128 * (WQ + 2), 128 * W1, cb(WQ + 2, 2), "cWQ2 cWQ3", "qWb")
@@ -456,6 +445,10 @@ def rank_program(g, core, T, topo):
 
     def plane(buf, b):
         return buf[:, C * b:C * b + C]
+
+    def so_view(i):
+        u, t = (20 - i) // 4, (20 - i) % 4
+        return T.sot[:, 4 * SOFF[u] + t:4 * (SOFF[u] + 16 * i):4], "so%d%d" % (u, t), T.jk[:, 8 * i * (i - 1):8 * i * (i + 1)]
 
     def compare(d, w, base, tile0):
         u, t = tile0 + (d - 1) // 4, (d - 1) % 4
@@ -495,41 +488,47 @@ def rank_program(g, core, T, topo):
         cp(out, sub(t32), t32, okey)
 
     def thr(t):
-        ts(T.thr[:, 128 * t:128 * t + NB], ps[5 + t][:, 0:NB], 1.0 + 2.0 / GG, pc(68 + t), A.mult, A.add, "ps%d z0" % (5 + t), "thr%d" % t)
+        bank = (7, 2, 7)[t]
+        ts(T.thr[:, 128 * t:128 * t + NB], ps[bank][:, 0:NB], 1.0 + 2.0 / GG, pc(68 + t), A.mult, A.add, "ps%d z0" % bank, "thr%d" % t)
 
     for r in range(NR):
         s = str(r)
         xq, first, final = "x" + s, r == 0, r == NR - 1
         pl, olist, hl, lp, ln, lv, lh = (sub(a + s) for a in ("pl", "ol", "hl", "lp", "ln", "lv", "lh"))
         mm(0, C, ("up", 0), (xq, 0), True, True, "upc ups " + xq)
+        mm(3, C, ("up", 0), (xq, 0), True, True, "upc ups " + xq)
         mm(1, C, ("up", 128), (xq, 0), True, True, "upc ups " + xq)
-        if first:
-            consts_scalar()
-        act(T.mk[:], ps[1][:, 0:C], F.Copy, "ps1", "mk")
         bg(2)
         tt(T.sq[:], ps[0][:, 0:C], T.m16[:], A.min, "ps0 m16", "sq")
         bg(1)
         scan(T.sb[:], T.k16[:], T.sq[:], -BIG, A.min, A.max, "k16 sq", "sb")
         bg(1)
+        low = 14 if first else 18
+        for i in range(19, low - 1, -1):
+            view, key, jk = so_view(i)
+            act(jk, ps[3][:, 0:16 * i], F.Sign, "sb ps3", "jk%d" % i, scale=-1.0, bias=T.sb[:, 16 * i + 15:16 * i + 16])
+            act(view, jk, F.Relu, "jk%d sz0 sz1" % i, key + " rs%d" % i, accum_out=sub("rs", i, i + 1))
+        after = {2: [0], 3: [1, 2], 4: [3, 4]} if first else {1: [0, 1], 2: [2], 3: [3], 4: [4]}
         for u in range(5):
             for t in range(4):
                 i = 20 - 4 * u - t
-                view = T.sot[:, 4 * SOFF[u] + t:4 * (SOFF[u] + 16 * i):4]
-                key = "so%d%d" % (u, t)
+                view, key, jk = so_view(i)
                 if i == 20:
                     tt(view, T.sb[:], ps[0][:, 0:C], A.is_ge, "sb ps0 sz0", key)
-                else:
+                elif i < low:
                     ts(view, ps[0][:, 0:16 * i], T.sb[:, 16 * i + 15:16 * i + 16], None, A.is_lt, None, "sb ps0 sz%d" % u, key)
-                    act(T.jk[:, 8 * i * (i - 1):8 * i * (i + 1)], view, F.Copy, key, "rs%d" % i, accum_out=sub("rs", i, i + 1))
+                    act(jk, view, F.Copy, key, "rs%d jk%d" % (i, i), accum_out=sub("rs", i, i + 1))
                 bg(2)
             if u == 0:
                 scan(T.ru[:], T.k01[:], T.sot[:, 0:4 * C:4], 0.0, A.mult, A.add, "k01 so00", "ru")
-            qz("so", SOFF[u], SOFF[u] + SWID[u], T.sot[:, 4 * SOFF[u]:4 * (SOFF[u] + SWID[u])],
-               " ".join("so%d%d" % (u, t) for t in range(4)), "soq%d" % u)
-            mm(2, SWID[u], ct(WB), ("so", SOFF[u]), u == 0, u == 4, "qWB soq%d" % u)
             if u == 1:
                 tt(sub("pre"), sub("cbs"), T.ru[:, 15:C:16], A.subtract, "cbs ru", "pre")
+            for v in after.get(u, []):
+                qz("so", SOFF[v], SOFF[v] + SWID[v], T.sot[:, 4 * SOFF[v]:4 * (SOFF[v] + SWID[v])],
+                   " ".join("so%d%d" % (v, t) for t in range(4)), "soq%d" % v)
+                mm(2, SWID[v], ct(WB), ("so", SOFF[v]), v == 0, v == 4, "qWB soq%d" % v)
         tt(sub("pre"), sub("pre"), sub("rs"), A.subtract, "pre " + " ".join("rs%d" % i for i in range(20)), "pre")
+        act(T.mk[:], ps[1][:, 0:C], F.Copy, "ps1", "mk")
         scan(T.ls[:], T.pen[:], ps[2][:, 0:C], 0.0, A.add, A.max, "pen ps2", "ls")
         bg(1)
         tt(sub("pli"), T.ls[:, 15:C:16], sub("pre"), A.add, "ls pre", "pli")
@@ -546,15 +545,15 @@ def rank_program(g, core, T, topo):
         arrive(nxt, "an" + s, 2, "n" + s)
         mm(1, C, ("up", 128), ("n" + s, 0), True, True, "upc ups n" + s)
         act(T.mn[:], ps[1][:, 0:C], F.Copy, "ps1", "mn")
+        if first:
+            for u in range(4):
+                zero(T.cot, 4 * (COFF[u] + CZERO[u]), 4 * (COFF[u] + CWID[u]), "cz%d" % u)
         pick32(T.ms, "ms", T.sa, "sa")
         for b in range(2):
             decode(xq, b, 4 + b, slot(T.at, b, C), "at%d" % b)
         act(T.aex[:], T.sa[:].indirect(sub("al")), F.Copy, "sa al0 al1 al2", "aex")
         for b in range(2, 4):
             decode(xq, b, 4 + b, slot(T.at, b, C), "at%d" % b)
-        if first:
-            for u in range(4):
-                zero(T.cot, 4 * (COFF[u] + CZERO[u]), 4 * (COFF[u] + CWID[u]), "cz%d" % u)
         arrive(nxt, "al" + s, 1, "lp" + s)
         cp(T.ms[:].indirect(lp), T.mn[:], "mn lp" + s, "ms")
         pick32(T.ms, "ms", T.sa, "sa")
@@ -568,11 +567,15 @@ def rank_program(g, core, T, topo):
             qz("co", QOFF[3] - PAD, QOFF[3] - PAD + 128, T.zb[:], "zb", "coq3")
             for i in range(5):
                 pick("k", 128 * i, "c", 128 * i, 128, sub("ko"), 128, "qE qKN ko", "k%d" % i)
+            for j, i in enumerate((W1, WG)):
+                zero(T.cb, 512 * i + 3, 512 * (i + 3), "cy%d" % j, 4)
+                zero(T.cb, 512 * i + 2, 512 * (i + 2), "cy%d" % (j + 2), 4)
             for a in ("wt", "xs"):
                 zero(T[a], 0, 512, a + "0 " + a + "1 " + a + "2")
             for u in range(4, 6):
                 zero(T.cot, 4 * (COFF[u] + CZERO[u]), 4 * (COFF[u] + CWID[u]), "cz%d" % u)
-            consts_zero()
+        for b in range(4):
+            decode("n" + s, b, (0, 1, 5, 6)[b], plane(T.vp, b), "vp%d" % b)
         for u in range(4):
             for d in range(4 * u + 1, min(4 * u + 5, 16)):
                 compare(d, 16, 0, 0)
@@ -580,8 +583,6 @@ def rank_program(g, core, T, topo):
                 consts_court()
             quant_co(u)
             rank_mm(u, 0, 2, (3, 4), u == 3)
-            if u < 3:
-                decode("n" + s, u, u % 2, plane(T.vp, u), "vp%d" % u)
         for t in range(2):
             act(slot(T.wt, t), ps[3 + t][:, 0:NB], F.Exp, "ps%d bwa" % (3 + t), "wt%d" % t, scale=-LN2 / 32, bias=pc(37 + t))
         for t in range(2):
@@ -596,9 +597,8 @@ def rank_program(g, core, T, topo):
             ms(slot(T.xs, 2), 0.0, "xs2")
         qz("wt", 0, 128, T.wt[:], "wt0 wt1 wt2", "wtq")
         for t in range(2):
-            mm(5 + t, 128, ct(WG + t), ("wt", 0), True, True, "qWG wtq")
+            mm((7, 2)[t], 128, ct(WG + t), ("wt", 0), True, True, "qWG wtq")
         qz("xs", 0, 128, T.xs[:], "xs0 xs1 xs2", "xsq")
-        decode("n" + s, 3, 1, plane(T.vp, 3), "vp3")
         thr(0)
         thr(1)
         for d in range(1, 6):
@@ -636,10 +636,19 @@ def rank_program(g, core, T, topo):
                 mm(5 + t, 128, ct(W1 + t), ("xs", 0), True, False, "qW1 xsq")
                 mm(5 + t, 128, ct(WG + t), ("xs", 0), False, True, "qWG xsq")
             if k == 0:
+                if first:
+                    dma("Y", T.lwc[:].bitcast(dt.uint8), T.wc[:], "thr1", "wq")
+                    dma("Y", T.lws[:], T.ws[:], "", "wsc")
+                    dma("Y", T.vt[:], T.v[:], "", "vt")
                 act(T.mkn[:], T.bm[:].indirect(lp), F.Copy, "bm lp" + s, "mkn")
                 act(T.mko[:], T.bm[:].indirect(pl), F.Copy, "bm pl" + s, "mko")
                 if first:
                     consts_tail_scalar()
+            if k == 6 and first:
+                for a in ("st", "gt"):
+                    zero(T[a], 0, 512, a + "0 " + a + "1 " + a + "2")
+                for a in ("h1", "h2"):
+                    zero(T[a], C, 544, a)
             if 2 <= k <= 5:
                 decode("p" + s, k - 2, banks[k - 2], plane(T.gp, k - 2), "gp%d" % (k - 2))
             if k <= 3:
@@ -655,7 +664,7 @@ def rank_program(g, core, T, topo):
                 b = k - 7
                 act(plane(T.vo, b), plane(T.vp, b).indirect(ln), F.Copy, "vp%d ln%s" % (b, s), "vo%d" % b)
                 act(plane(T.go, b), plane(T.gp, b).indirect(lv), F.Copy, "gp%d lv%s" % (b, s), "go%d" % b)
-            bg(per[k] if k < 7 else (rest + 3) // 4)
+            bg(per[k] if k < 7 else 6 if first else 1)
             for t in range(nt):
                 tt(slot(T.rt, t), ps[5 + t][:, 0:NB], T.thr[:, 128 * t:128 * t + NB], A.is_gt, "ps%d thr%d" % (5 + t, t), "rt%d" % t)
                 if t:
@@ -665,7 +674,7 @@ def rank_program(g, core, T, topo):
             qz("xs", 0, 128, T.xs[:], "xs0 xs1 xs2", "xsq")
         for t in range(2):
             mm(5 + t, 128, ct(SS + t), ("xs", 0), True, True, "qSS xsq")
-        bg(99)
+        bg(5)
         for t in range(3):
             tt(slot(T.st, t), ps[5 + t // 2][:, 0:NB], slot(T.xs, t), A.is_lt, "ps%d xs%d" % (5 + t // 2, t), "st%d" % t)
         qz("st", 0, 128, T.st[:], "st0 st1 st2", "stq")
@@ -673,11 +682,16 @@ def rank_program(g, core, T, topo):
         for u in range(2):
             mm(3 + u, 128, ct(FA), ("s2", 0), True, False, "qSS s2c s2s")
             mm(3 + u, 128, ct(FB + u), ("s2", 0), False, True, "qFB s2c s2s")
-        mm(2, 128, ("s2", 0), ct(KS), True, False, "qK s2c s2s")
+        bg(len(bgq) - 3)
         for u in range(2):
             ts(slot(T.gt, u, 128), ps[3 + u][:, 0:128], pc(59 + u), None, A.is_ge, None, "ps%d th0 th1" % (3 + u), "gt%d" % u)
+        bg(1)
         qz("gt", 0, 128, T.gt[:], "gt0 gt1 gt2", "gtq")
+        mm(2, 128, ("s2", 0), ct(KS), True, False, "qK s2c s2s")
         mm(2, 128, ("gt", 0), ct(KG), False, True, "qK gtq")
+        bg(2)
+        if final:
+            act(T.onr[:], T.iot[:].indirect(ln), F.Copy, "iot ln" + s, "onr")
         cp(T.tw[:], ps[2][:, 0:64], "ps2", "tw")
         list_pick("h1", 32, "n32", "mkn")
         list_sum("h1", 0, 5)
@@ -698,11 +712,12 @@ def rank_program(g, core, T, topo):
             cp(plane(T.vg, b), plane(T.vo, b).indirect(sub("ix1")), "vo%d ix1" % b, "vg%d" % b)
         if final:
             qz("v", 0, 128, T.vt[:], "vt", "vq")
+            act(T.wrow[:], T.onr[:].indirect(sub("ix1")), F.Copy, "onr ix1", "wrow")
+            for k in range(8):
+                dma("Y", T.ol[k:k + 1, :], T.wrow[16 * k:16 * k + 1, :], "wrow", "")
         arrive(prv, "ah" + s, 1, "lh" + s)
         for hf in range(2):
             act(T.g2[:, H * hf:H * hf + H], plane(T.go, 3).indirect(sub("lh" + s, 10 * hf, 10 * hf + 10)), F.Copy, "go3 lh" + s, "g2%d" % hf)
-        if final:
-            act(T.onr[:], T.iot[:].indirect(ln), F.Copy, "iot ln" + s, "onr")
         for hf in range(2):
             for b in range(4):
                 a = plane(T.go, b).indirect(sub("lh" + s, 10 * hf, 10 * hf + 10)) if b < 3 else T.g2[:, H * hf:H * hf + H]
@@ -711,6 +726,7 @@ def rank_program(g, core, T, topo):
             qz("z", H * hf, H * hf + H, T.zt[:, 4 * H * hf:4 * H * (hf + 1)], " ".join("zt%d%d" % (hf, b) for b in range(4)), "zq%d" % hf)
             for b in range(4):
                 mm(hb[hf][b], H, ("lw", 128 * b), ("z", H * hf), False, True, "wq wsc zq%d" % hf)
+        xq = "x%d" % (r + 1)
         for hf in range(2):
             for b in range(4):
                 o, bank = T.xn[:, 4 * H * hf + b:4 * H * (hf + 1):4], hb[hf][b]
@@ -718,17 +734,13 @@ def rank_program(g, core, T, topo):
                     ts(o, ps[bank][:, 0:H], 1.0 / 32, None, A.mult, None, "ps%d" % bank, "xn%d%d" % (hf, b))
                 else:
                     act(o, ps[bank][:, 0:H], F.Copy, "ps%d" % bank, "xn%d%d" % (hf, b), scale=1.0 / 32)
-        xq = "x%d" % (r + 1)
-        qz(xq, 0, C, T.xn[:], "xn00 xn01 xn02 xn03 xn10 xn11 xn12 xn13", xq)
+            qz(xq, H * hf, H * hf + H, T.xn[:, 4 * H * hf:4 * H * (hf + 1)], " ".join("xn%d%d" % (hf, b) for b in range(4)), xq)
         if not final:
             send_q(prv, xq, "n%d" % (r + 1), "an%d" % (r + 1), xq)
     mm(2, C, ("v", 0), (xq, 0), True, True, "vq " + xq)
-    act(T.wrow[:], T.onr[:].indirect(sub("ix1")), F.Copy, "onr ix1", "wrow")
     dma("Y", T.oc[:], T[xq + "c"][:].bitcast(dt.uint8), xq, "")
     for k in range(4):
         dma("S", T.osc[4 * k:4 * k + 4, :], T[xq + "s"][32 * k:32 * k + 4, :], xq, "")
     cp(T.orow[:], ps[2][:, 0:C], "ps2", "orow")
     dma("Y", T.y[:], T.orow[:], "orow", "")
-    for k in range(8):
-        dma("YS"[k % 2], T.ol[k:k + 1, :], T.wrow[16 * k:16 * k + 1, :], "wrow", "")
     emit(g, T, ops)

@@ -3,16 +3,17 @@ from concourse.mybir import dt, AluOpType, AxisListType, ActivationFunctionType
 
 A = AluOpType
 F = ActivationFunctionType
-C, NR, SW, NB = 320, 2, 12, 80
-BIG, GG = 1.0e29, 131072.0
+C, NR, SW, NB = 320, 2, 12, 160
+BIG = 1.0e29
+CW, GW, SIG = 2.0 ** 13, 2.0 ** 16, 16.0
 LN2 = math.log(2.0)
 X4, U8, BF, F32, I32, U16 = "float8_e4m3fn_x4", "uint8", "bfloat16", "float32", "int32", "uint16"
-E0, KN, WB, WQ, W1, WG, SS, FA, FB, KG, KS, NT = 0, 4, 5, 6, 10, 13, 16, 18, 19, 21, 22, 23
+WB, E0, K0, KN, MX, PG, PO, SS, MU, FA, MI, NT = 0, 1, 5, 9, 10, 12, 14, 16, 18, 19, 20, 21
+SLOT = (0, 2, 1, 3)
 SOFF, SWID = [0, 320, 576, 768, 896], [320, 256, 192, 128, 128]
-COFF, CWID = [0, 256, 512, 640, 768, 896], [256, 256, 128, 128, 128, 128]
-CZERO = [192, 128, 64, 0, 64, 0]
-PAD = 112
-QOFF = [PAD + COFF[i] + PAD * i for i in range(6)]
+DL, DU = ((15, 14, 13, 12), (11, 10, 9, 8), (7, 6, 5, 4), (3, 2, 1)), ((7, 6, 5, 4), (3, 2, 1))
+LOW, FEW = [18, 19], [4, 4]
+LB, UB, HB = (5, 6), (7, 0), ((0, 1, 4, 5), (6, 7, 2, 3))
 
 SCRATCH, SUB = {}, {}
 
@@ -30,44 +31,46 @@ def _q(names, n):
 
 def _s(buf, names, d):
     for i, s in enumerate(names.split()):
-        SUB[s] = (buf, 24 * i, {"uoff": 16, "al": 24, "bl": 24, "ko": 8, "so": 8}.get(s, 20))
-    _b(buf, 24 * len(names.split()), d)
+        SUB[s] = (buf, 32 * i, {"uoff": 16, "al": 24, "bl": 24, "ky": 16, "tl": 2}.get(s, 20))
+    _b(buf, 32 * len(names.split()), d)
 
 
-_b("xt at zt xn vp vo vg gp go", 4 * C, BF)
-_b("ut vt wt xs rt st gt zb", 512, BF)
-_b("h1 h2", 544, BF)
-_b("cb", 512 * NT, BF)
-_b("sot cot", 4096, BF)
+_b("xt at zt xn vp vo vq gp go zp", 4 * C, BF)
+_b("ut vt wb", 512, BF)
+_b("kn", 520, BF)
+_b("zb", 1024, BF)
+_b("wt xs st", 4 * NB, BF)
+_b("sg", 2064, BF)
+_b("sot", 4096, BF)
+_b("cot", 5120, BF)
 _b("jk", 3400, BF)
-_b("m16 k16 k01 pen m10 k10 bm mko mkn ru e16 g2", C, BF)
-_b("iot r16 r10 mk mn ms tmp sb ls sa sq orow onr wrow", C, F32)
-_b("aex d0 dd thr", 384, F32)
-_b("pkr pkb", 768, BF)
-_b("nr lsr wr", 128, BF)
-_b("ssr msr tk", 256, BF)
-_b("pb", 8, BF)
-_b("pi", 64, I32)
-_b("pf", 80, F32)
-_b("tw", 64, F32)
+_b("m16 k16 k01 pen m10 k10 e10 ru e16 r16 r10 wp gq vg", C, BF)
+_b("iot mk mn ms tmp sb ls sa sq orow onr wrow wro2 yb", C, F32)
+_b("aex d0 dd", 384, F32)
+_b("wr r8 lr", 128, BF)
+_b("psr pir a1 a2 b1t b2t", 256, BF)
+_b("fa", 640, BF)
+_b("bs mt mt2", NB, F32)
+_b("pi", 8, I32)
+_b("pf", 64, F32)
 _b("li", 96, I32)
+_b("kf", 128, F32)
 _s("sf", "rs pre cbs fx", F32)
-_s("si", "pli pni t1 t2 bo bn", I32)
-_s("of", "uoff xy al bl o32 n32 ix1 ko so", U16)
+_s("si", "pli j32 j10", I32)
+_s("of", "uoff xy al bl ky tl mu", U16)
 _s("snd", "pl0 pl1 ol0 ol1 hl0 hl1", U16)
 _s("lnd", "lp0 lp1 ln0 ln1 lv0 lv1 lh0 lh1", U16)
 _q("lw", 512)
-_q("u v wt xs st s2 gt", 128)
+_q("u v", 128)
+_q("wt w2 xs st s2", NB)
 _q("up", 256)
 _q("x0 x1 x2 g0 g1 n0 n1 p0 p1 z", C)
 _q("c", 128 * NT)
-_q("k", 640)
 _q("so", 1024)
-_q("co", QOFF[5] + 128)
-_q("h", 528)
+_q("co", 1664)
 for _i in range(8):
     SCRATCH["b%d" % _i] = ("psum", [128, 512], F32)
-SEMAPHORES = ["V", "S", "P", "G", "loc"] + ["d%d" % i for i in range(28)] + \
+SEMAPHORES = ["V", "S", "P", "G", "loc"] + ["d%d" % i for i in range(40)] + \
              [a + str(r) for r in range(NR) for a in ("an", "ap", "al", "ao", "av", "ah")]
 
 
@@ -195,12 +198,15 @@ def rank_program(g, core, T, topo):
     def af(out, a, scale, bias, R, W):
         act(out, a, F.Identity, R, W, scale=scale, bias=bias)
 
+    def sc(out, a, R, W):
+        act(out, a, F.Copy, R, W)
+
     def zero(buf, a, b, W, step=1):
-        act(buf[:, a:b:step], T.zb[:, 0:(b - a + step - 1) // step], F.Copy, "zb", W)
+        sc(buf[:, a:b:step], T.zb[:, 0:(b - a + step - 1) // step], "zb", W)
 
     def pick(dst, a, src, b, w, off, n, R, W):
         cp(T[dst + "c"][:, a:a + n].bitcast(dt.uint32), T[src + "c"][:, b:b + w].bitcast(dt.uint32).indirect(off), R, W + "c")
-        act(T[dst + "s"][:, a:a + n], T[src + "s"][:, b:b + w].indirect(off), F.Copy, R, W + "s")
+        sc(T[dst + "s"][:, a:a + n], T[src + "s"][:, b:b + w].indirect(off), R, W + "s")
 
     def mm(bank, n, lhs, rhs, start, stop, R):
         (ln, la), (rn, ra) = lhs, rhs
@@ -245,270 +251,255 @@ def rank_program(g, core, T, topo):
     def ct(i):
         return ("c", 128 * i)
 
-    def cb(i, n=1):
-        return T.cb[:, 512 * i:512 * (i + n)]
+    def sg(i, t, n=128):
+        return T.sg[:, 512 * i + t:512 * i + 4 * n:4]
 
-    def cslot(i, t, a=0, b=128):
-        return T.cb[:, 512 * i + 4 * a + t:512 * i + 4 * b:4]
+    def qc(i, j, n, R, W):
+        qz("c", 128 * i, 128 * (i + n), T.sg[:, 512 * j:512 * (j + n)], R, W)
 
-    def slot(buf, t, n=NB):
-        return buf[:, t:4 * n:4]
+    def slot(buf, t, a=0, b=NB):
+        return buf[:, 4 * a + t:4 * b:4]
 
-    banks = (0, 1, 3, 4)
+    def plane(buf, b, lo=0, hi=C):
+        return buf[:, C * b + lo:C * b + hi]
+
     ps = [T["b%d" % i] for i in range(8)]
-    pi, pf, li = T.pi, T.pf, T.li
-    SH, AND, EQ = A.logical_shift_right, A.bitwise_and, A.is_equal
+    pi, pf, li, kf = T.pi, T.pf, T.li, T.kf
+    SH, AND, EQ, MUL, ADD = A.logical_shift_right, A.bitwise_and, A.is_equal, A.mult, A.add
+    H = C // 2
 
-    def pc(i, n=1):
+    names = ("p g l8 p3 p1 q s hb s4 s2 c1 c2 c3 lB sB iA iB z nz nnz co s16 vl vu alo blo alu blu tl t0 t1 t2 cb o0 fx "
+             "bw bx u0 u1 u2 u3 th fl fu fs").split()
+
+    def pc(name, n=1):
+        i = names.index(name)
         return pf[:, i:i + n]
+
+    def lin(name, src, k, add, e="S"):
+        a, R = (pc(add), "_%s _%s" % (src, add)) if isinstance(add, str) else (float(add), "_" + src)
+        if e == "S":
+            af(pc(name), pc(src), float(k), a, R, "_" + name)
+        else:
+            ts(pc(name), pc(src), float(k), a, MUL, ADD, R, "_" + name)
 
     dma("Y", T.xt[:], T.x[:], "", "xt")
     dma("S", T.ut[:], T.u[:], "", "ut")
     iota(pi[:, 0:1], [[0, 1]], 0, 1, "pi0", False)
-    iota(li[:, 0:16], [[1, 2], [16, 8]], 0, 0, "li0", False)
     iota(T.r16[:], [[0, 20], [1, 16]], 0, 0, "r16")
-    iota(li[:, 16:36], [[16, 20]], 0, 0, "li1", False)
     iota(T.wr[:], [[1, 8], [0, 16]], 0, 0, "wr")
-    iota(li[:, 36:60], [[0, 3], [10, 8]], 0, 0, "li2", False)
-    iota(T.r10[:], [[0, 32], [1, 10]], 0, 0, "r10")
+    iota(li[:, 0:16], [[1, 2], [16, 8]], 0, 0, "li0", False)
+    iota(li[:, 16:36], [[16, 20]], 0, 0, "li1", False)
     ms(T.zb[:], 0.0, "zb")
-    for c, s, m in ((5, 0, 15), (1, 4, 7), (2, 1, 7), (3, 0, 1), (4, 3, 1), (6, 6, 1), (7, 2, 15), (8, 0, 3)):
+    for c, s, m in ((1, 4, 7), (2, 3, 15), (3, 0, 3), (4, 0, 1), (5, 0, 15)):
         ts(pi[:, c:c + 1], pi[:, 0:1], s, m, SH, AND, "pi0", "pi%d" % c)
-    cp(sub("uoff"), li[:, 0:16], "li0", "uoff")
-    cp(pc(1, 8), pi[:, 1:9], "pi1 pi2 pi3 pi4 pi5 pi6 pi7 pi8", "pf")
+    qz("co", 0, 128, T.zb[:, 0:512], "zb", "coz")
+    cp(pc("p", 6), pi[:, 0:6], "pi0 pi1 pi2 pi3 pi4 pi5", "_p _g _l8 _p3 _p1 _q")
     for u in range(4):
-        ms(T.sot[:, 4 * (SOFF[u] + SWID[u] - 48):4 * (SOFF[u] + SWID[u])], 0.0, "sz%d" % u)
-    ts(T.e16[:], T.r16[:], pc(5), None, EQ, None, "r16 pf", "e16")
-    ts(T.k01[:], T.r16[:], 0.0, None, A.is_gt, None, "r16", "k01")
+        zero(T.sot, 4 * (SOFF[u] + SWID[u] - 48), 4 * (SOFF[u] + SWID[u]), "sz%d" % u)
     zero(T.sot, 4 * SOFF[4], 4096, "sz4")
-    af(pc(10), pc(1), 1.0, 0.0, "pf", "L0")
-    af(pc(11), pc(1), 1.0, 8.0, "pf", "L1")
-    af(pc(12), pc(4), 8.0, pc(1), "pf", "L2")
-    af(pc(13), pc(2), 1.0, 0.0, "pf", "S0")
-    af(pc(14), pc(2), 1.0, 0.0, "pf", "S1")
-    af(pc(15), pc(2), 1.0, 8.0, "pf", "S2")
+    ts(T.e16[:], T.r16[:], pc("q"), None, EQ, None, "r16 _q", "e16")
+    ts(T.k01[:], T.r16[:], 0.0, None, A.is_gt, None, "r16", "k01")
+    for t in range(4):
+        ts(T.wb[:, t:512:4], T.wr[:], pc("g"), None, EQ, None, "wr _g", "wb%d" % t)
+    cp(sub("uoff"), li[:, 0:16], "li0", "uoff")
     af(T.m16[:], T.e16[:], 2 * BIG, -BIG, "e16", "m16")
     af(T.k16[:], T.k01[:], 2 * BIG, -BIG, "k01", "k16")
-    for t in range(4):
-        ts(cslot(WB, t), T.wr[:], pc(1), None, EQ, None, "wr pf", "cWB%d" % t)
-    for i in range(3):
-        qz("co", QOFF[i] - PAD, QOFF[i] - PAD + 128, T.zb[:], "zb", "coq%d" % i)
-    qz("u", 0, 128, T.ut[:], "ut", "uq")
-    pick("up", 0, "u", 0, 128, sub("uoff"), 256, "uq uoff", "up")
     af(T.pen[:], T.e16[:], -1049600.0, 1024.0, "e16", "pen")
-    af(pc(9), pc(5), 1023.0, 15.0 - 15360.0, "pf", "pf9")
-    af(pc(0), pc(5), 1024.0, -15360.0, "pf", "pf0")
-    af(pc(57), pc(3), -2.0, 1.0, "pf", "sp")
-    af(pc(54), pc(3), 160.0, 9.0, "pf", "f54")
-    af(pc(22, 3), pc(13, 3), 2.0, pc(3), "S0 S1 S2 pf", "sid")
-    af(pc(28, 3), pc(10, 3), 16.0, 1.0, "L0 L1 L2", "l16")
-    af(pc(55), pc(4), 80.0, pc(54), "pf f54", "f55")
-    af(pc(56), pc(2), 10.0, pc(54), "pf f54", "f56")
-    af(pc(37, 2), pc(10, 2), LN2, 0.0, "L0 L1", "bwa")
-    af(pc(39), pc(1), LN2, 8 * LN2, "pf", "bwb")
-    af(pc(64), pc(56), 1.0, 80.0, "f56", "f64")
-    qz("x0", 0, C, T.xt[:], "xt", "x0")
-    send_q(prv, "x0", "n0", "an0", "x0")
+    qz("c", 128 * WB, 128 * E0, T.wb[:], "wb0 wb1 wb2 wb3", "qWB")
+    for n, s, k, a in (("s", "l8", -8, "p"), ("hb", "g", -2, "l8"), ("s2", "p1", -1, "p3"), ("cb", "q", 1023, 15 - 15360),
+                       ("fx", "q", 1, -4.5), ("o0", "q", 1024, -15360), ("s4", "p3", -1, "s"), ("alo", "hb", 10, 9),
+                       ("blo", "s", 10, 9), ("t0", "hb", 160, 9), ("c1", "s2", -2, 2), ("t1", "s", -30, 249)):
+        lin(n, s, k, a, "V")
+    qz("u", 0, 128, T.ut[:], "ut", "uq")
+    for n, s, k, a in (("t2", "p1", -2, "s"), ("s16", "s", 16, 0), ("sB", "s", 1, 8), ("iA", "l8", 16, "s")):
+        lin(n, s, k, a, "V")
+    pick("up", 0, "u", 0, 128, sub("uoff", 0, 8), 128, "uq uoff", "up0")
+    pick("up", 128, "u", 0, 128, sub("uoff", 8, 16), 128, "uq uoff", "up1")
+    for n, s, k, a in (("alu", "s4", 20, "t0"), ("blu", "s", 10, "t0"), ("c2", "s4", -2, 4), ("lB", "s4", 2, "g"),
+                       ("c3", "hb", -16, "t1"), ("vl", "hb", 16, "t2"), ("vu", "s4", 32, "t2"), ("iB", "lB", 16, "sB")):
+        lin(n, s, k, a, "S")
+    iota(li[:, 52:60], [[0, 4], [1, 2]], 0, 0, "li3", False)
+    iota(li[:, 60:68], [[0, 2], [1, 2], [0, 2]], 0, 0, "li4", False)
+    iota(li[:, 68:76], [[0, 2], [1, 4]], 0, 0, "li5", False)
+    iota(li[:, 76:84], [[1, 4], [0, 2]], 0, 0, "li6", False)
+    iota(li[:, 36:52], [[160, 2], [0, 8]], 0, 0, "li2", False)
+    iota(T.r10[:], [[0, 32], [1, 10]], 0, 0, "r10")
     for b in range(4):
-        sel(cb(E0 + b), T.zb[:], [[4, 128], [1, 4]], A.not_equal, 32.0, -b, -4, "zb", "cE%d" % b)
-    sel(cb(KN), T.zb[:], [[1, 128], [0, 4]], A.not_equal, -32.0, 0, -1, "zb", "cKN")
+        if b == 1:
+            qz("x0", 0, C, T.xt[:], "xt", "x0a x0b")
+            send_q(prv, "x0", "n0", "an0", "x0a x0b")
+        sel(T.sg[:, 512 * b:512 * b + 512], T.zb[:, 0:512], [[4, 128], [1, 4]], A.not_equal, 32.0, -SLOT[b], -4, "zb", "sg%d" % b)
+    for a in (640, 1280):
+        dma("Y", T.coc[:, a:a + 128].bitcast(dt.uint8), T.coc[:, 0:128].bitcast(dt.uint8), "coz xt", "cy%dc" % a)
+        dma("Y", T.cos[:, a:a + 128], T.cos[:, 0:128], "coz", "cy%ds" % a)
+    for i in range(5):
+        tiles = ["%d%d" % (i // 2, 2 * (i % 2) + j) for j in range(2)]
+        dma("Y", T.cot[:, 1024 * i:1024 * i + 1024], T.zb[:], "zb", " ".join("cz%s co%s3" % (a, a) for a in tiles))
+    for a in ("wt", "xs", "st"):
+        dma("Y", T[a][:], T.zb[:, 0:4 * NB], "zb", " ".join(a + t for t in ("0", "00", "01", "1", "2", "3")))
+    iota(T.iot[:], [[1, C]], 0, 0, "iot")
 
-    L(qz, "c", 128 * WB, 128 * WQ, cb(WB), "cWB0 cWB1 cWB2 cWB3", "qWB")
-    L(cp, pi[:, 10:16], pc(10, 6), "L0 L1 L2 S0 S1 S2", "iL")
+    L(ts, sub("cbs"), li[:, 16:36], pc("cb"), None, ADD, None, "li1 _cb", "cbs")
     L(ms, sub("rs", 0, 1), 0.0, "rs0")
-    L(ts, pi[:, 16:22:2], pi[:, 10:13], 1, None, SH, None, "iL", "Aa")
-    L(cp, pi[:, 17:22:2], pi[:, 13:16], "iL", "Sa")
-    L(ts, pi[:, 22:28:2], pi[:, 10:13], 1, None, SH, None, "iL", "Ab")
-    L(ts, sub("cbs"), li[:, 16:36], pc(9), None, A.add, None, "li1 pf9", "cbs")
+    L(ts, sub("fx"), li[:, 16:36], pc("fx"), 0.1, ADD, MUL, "li1 _fx", "fx")
+    L(ts, sub("j32"), li[:, 16:36], pc("q"), 32.0, ADD, MUL, "li1 _q", "j32")
+    L(cp, sub("j10"), sub("fx"), "fx", "j10")
+    L(ts, sub("al", 0, 16), li[:, 16:32], 1.25, pc("alo"), MUL, ADD, "li1 _alo", "al0")
+    L(ts, sub("j10"), sub("j10"), -319.0, None, MUL, None, "j10", "j10")
+    L(ts, sub("al", 16, 24), li[:, 16:24], 0.625, pc("alu"), MUL, ADD, "li1 _alu", "al1")
+    L(tt, sub("j32"), sub("j32"), sub("j10"), ADD, "j32 j10", "j32")
+    L(ts, T.e10[:], T.r10[:], pc("q"), None, EQ, None, "r10 _q", "e10")
+    L(cp, sub("xy"), sub("j32"), "j32", "xy")
+    L(ts, T.k10[:], T.r10[:], 0.5, None, A.is_gt, None, "r10", "k10")
+    L(ts, sub("bl", 0, 16), li[:, 36:52], pc("blo"), None, ADD, None, "li2 _blo", "bl0")
+    L(ts, sub("bl", 16, 24), li[:, 36:44], pc("blu"), 80.0, ADD, ADD, "li2 _blu", "bl1")
 
-    def xor(src, key, dst, dkey, mid):
-        for j in range(4):
-            L(ts, pi[:, 32 + 6 * j:38 + 6 * j], pi[:, src:src + 6], 1 << j, None, AND, None, key, "bit%d" % j)
-        mid[0]()
-        L(tt, pc(40, 12), pi[:, 32:56:2], pi[:, 33:56:2], A.subtract, "bit0 bit1 bit2 bit3", "dif")
-        mid[1]()
-        for t in range(3):
-            L(op, "V", lambda q, t=t: q.tensor_reduce(pc(dst + t), pf[:, 40 + t:52:3], AxisListType.X, A.add,
-                                                      apply_absolute_value=True), "dif", dkey + str(t))
+    def consts_keys():
+        ts(kf[:, 0:16], li[:, 52:68], pc("p1"), pc("c1"), EQ, MUL, "li3 li4 _p1 _c1", "k0")
+        ts(kf[:, 16:32], li[:, 68:84], pc("p3"), pc("c2"), EQ, MUL, "li5 li6 _p3 _c2", "k1")
+        ts(kf[:, 32:40], li[:, 16:24], pc("s16"), pc("c3"), EQ, MUL, "li1 _s16 _c3", "k2")
+        ts(kf[:, 40:48], li[:, 76:84], pc("p3"), 8.0, A.not_equal, MUL, "li6 _p3", "k3")
+        ts(kf[:, 48:56], li[:, 16:24], 2.0, pc("vl"), MUL, ADD, "li1 _vl", "k4")
+        ts(kf[:, 56:64], li[:, 16:24], pc("vu"), None, ADD, None, "li1 _vu", "k5")
+        tt(kf[:, 64:96], kf[:, 0:32], kf[:, 32:64], ADD, "k0 k1 k2 k3 k4 k5", "k6")
+        ts(pc("z"), pc("g"), pc("s"), None, EQ, None, "_g _s", "_z")
+        tt(kf[:, 96:112], kf[:, 64:80], kf[:, 80:96], ADD, "k6", "k7")
 
-    xor(16, "Aa Sa", 16, "k",
-        [lambda: L(ts, li[:, 16:36], li[:, 16:36], pc(5), None, A.add, None, "li1 pf", "li1"),
-         lambda: L(ts, T.e16[:], T.r10[:], pc(5), None, EQ, None, "r10 pf", "e16")])
-    L(ts, sub("fx"), li[:, 16:36], -4.5, 0.1, A.add, A.mult, "li1", "fx")
-    L(ts, pi[:, 23:28:2], pc(16, 3), -1.0, 0.0, A.add, A.max, "k0 k1 k2", "Kb")
-    L(cp, li[:, 60:80], sub("fx"), "fx", "li3")
-    L(ts, pc(31, 3), pc(16, 3), 0.0, None, A.is_gt, None, "k0 k1 k2", "nz")
-    xor(22, "Ab Kb", 19, "q",
-        [lambda: L(ts, li[:, 80:88], li[:, 60:68], 6.0, None, A.mult, None, "li3", "li4"),
-         lambda: L(ts, T.mko[:], T.r10[:], 0.0, None, A.is_gt, None, "r10", "mko")])
-    L(ts, li[:, 60:80], li[:, 60:80], -319.0, None, A.mult, None, "li3", "li3")
-    L(tt, pc(25, 3), pc(13, 3), pc(28, 3), A.add, "S0 S1 S2 l16", "rkey")
-    L(tt, pc(34, 3), pc(19, 3), pc(28, 3), A.add, "q0 q1 q2 l16", "pk")
-    L(ts, pc(19, 3), pc(19, 3), 2.0, pc(3), A.mult, A.add, "q0 q1 q2 pf", "q0 q1 q2")
-    L(tt, li[:, 80:88], li[:, 80:88], li[:, 16:24], A.add, "li4 li1", "li4")
-    L(ts, pc(25, 3), pc(25, 3), pc(57), None, A.mult, None, "rkey sp", "rkey")
-    L(ts, pc(34, 3), pc(34, 3), pc(57), None, A.mult, None, "pk sp", "pk")
-    L(ts, pc(65, 3), pc(31, 3), -63.0, 63.0, A.mult, A.add, "nz", "z63")
-    L(ts, li[:, 16:36], li[:, 16:36], 32.0, None, A.mult, None, "li1", "li1")
-    L(tt, T.pb[:, 0:3], pc(34, 3), pc(31, 3), A.mult, "pk nz", "pb0")
-    L(tt, T.pb[:, 3:6], pc(19, 3), pc(65, 3), A.max, "q0 q1 q2 z63", "pb1")
-    L(tt, li[:, 60:80], li[:, 60:80], li[:, 16:36], A.add, "li3 li1", "li3")
-    for t in range(6):
-        L(dma, "Y", T.pkb[0:1, 128 * t:128 * t + 128], T.pb[:, t:t + 1], "pb0 pb1", "pk%d" % t)
-    L(ts, sub("ko"), li[:, 80:88], 127.0, None, A.min, None, "li4", "ko")
-    L(ts, sub("al", 0, 8), li[:, 36:44], pc(54), None, A.add, None, "li2 f54", "al0")
-    L(ts, sub("al", 8, 16), li[:, 44:52], pc(54), 80.0, A.add, A.add, "li2 f54", "al1")
-    L(ts, sub("al", 16, 24), li[:, 52:60], pc(55), None, A.add, None, "li2 f55", "al2")
-    L(cp, sub("xy"), li[:, 60:80], "li3", "xy")
-    L(ts, sub("bl", 0, 16), li[:, 36:52], 0.0, pc(56), A.mult, A.add, "li2 f56", "bl0")
-    L(ts, sub("bl", 16, 24), li[:, 52:60], 0.0, pc(64), A.mult, A.add, "li2 f64", "bl1")
-    L(ts, pc(52, 2), pc(31, 2), -200.0, None, A.mult, None, "nz", "b0")
-    L(ts, pc(68, 3), pc(31, 3), BIG, -BIG, A.mult, A.add, "nz", "z0")
-    L(tt, pc(52, 2), pc(52, 2), pc(37, 2), A.add, "b0 bwa", "b0")
-
-    def consts_pool2():
-        iota(T.iot[:], [[1, C]], 0, 0, "iot")
-        iota(T.bm[:], [[1, 10], [0, 32]], 0, 0, "bm")
-        iota(T.ssr[:], [[16, 2], [0, 8], [1, 16]], 0, 0, "ssr")
-        iota(T.nr[:], [[1, 128]], 0, 0, "nr")
-        for h in range(2):
-            s = 1 - 2 * h
-            iota(T.lsr[:, 64 * h:64 * h + 64], [[s, 16], [0, 4]], s, 0, "lsr%d" % h)
-            for u in range(2):
-                iota(T.msr[:, 128 * u + 64 * h:128 * u + 64 * h + 64], [[0, 16], [s, 4]], s * (4 * u + 1), 0, "msr%d%d" % (u, h))
-        for i in range(4):
-            sel(cb(WQ + i), cb(WB), [[0, 8], [1, 16], [-1, 4]], EQ, 0.0, -4 * i, 0, "cWB0 cWB1 cWB2 cWB3", "cWQ%d" % i)
+    def consts_rows():
+        ts(sub("ky"), kf[:, 96:112], 1.0, None, ADD, None, "k7", "ky")
+        lin("nz", "z", -1, 1)
+        lin("nnz", "z", 1, -1)
+        lin("co", "z", -1 / GW, -1.5 / GW)
+        sc(T.psr[:], T.r16[:].indirect(sub("ky")), "r16 ky", "psr")
+        sc(T.pir[:], T.iot[:].indirect(sub("ky")), "iot ky", "pir")
 
     def consts_court():
-        for t in range(3):
-            a = 2 * (t // 2)
-            ts(T.cb[:, 512 * (WG + a) + t:512 * SS:4], T.pkr[:, 128 * a:384], pc(25 + t), GG, EQ, A.mult, "pkr rkey", "cWG%d" % t)
-            ts(T.cb[:, 512 * (W1 + a) + t:512 * WG:4], T.pkr[:, 384 + 128 * a:768], pc(22 + t), None, EQ, None, "pkr sid", "cW1%d" % t)
-        qz("c", 128 * WG, 128 * SS, cb(WG, 3), "cWG0 cWG1 cWG2 cy1 cy3", "qWG")
-        qz("c", 128 * W1, 128 * WG, cb(W1, 3), "cW10 cW11 cW12 cy0 cy2", "qW1")
+        L(qc, K0, 0, 4, "sg0 sg1 sg2 sg3", "qK")
+        L(qz, "c", 128 * KN, 128 * MX, T.kn[:, 0:512], "kn", "qKN")
+        L(ts, T.a1[:], T.psr[:], pc("s"), CW, EQ, MUL, "psr _s", "a1")
+        L(ts, T.a2[:], T.pir[:], pc("iA"), CW * GW, EQ, MUL, "pir _iA", "a2")
+        L(ms, sg(2, 1), 0.0, "sg2")
+        L(ms, sg(3, 3), 0.0, "sg3")
+        L(af, T.b1t[:], T.a1[:], pc("z"), 0.0, "a1 _z", "b1t")
+        L(af, T.b2t[:], T.a2[:], pc("co"), 0.0, "a2 _co", "b2t")
+        L(af, sg(2, 0, 256), T.a2[:], pc("nnz"), 0.0, "a2 _nnz", "sg2 sg3")
+        L(tt, T.fa[:, 0:256], T.a1[:], T.a2[:], ADD, "a1 a2", "fa0")
+        L(af, sg(0, 0, 256), T.fa[:, 0:256], pc("nz"), 0.0, "fa0 _nz", "sg0 sg1")
+        L(ts, T.fa[:, 256:384], T.psr[:, 128:256], pc("sB"), CW, EQ, MUL, "psr _sB", "fa1")
+        L(ts, T.fa[:, 384:512], T.pir[:, 128:256], pc("iB"), CW * GW, EQ, MUL, "pir _iB", "fa2")
+        L(af, sg(3, 2), T.fa[:, 384:512], -1.0, 0.0, "fa2", "sg3")
+        L(tt, sg(1, 2), T.fa[:, 256:384], T.fa[:, 384:512], ADD, "fa1 fa2", "sg1")
+        L(qc, PG, 2, 2, "sg2 sg3", "qPG")
+        L(qc, MX, 0, 2, "sg0 sg1", "qMX")
+        L(af, sg(3, 2), T.fa[:, 384:512], -1.5 / GW, 0.0, "fa2", "sg3")
+        L(tt, sg(2, 0, 256), T.b1t[:], T.b2t[:], ADD, "b1t b2t", "sg2 sg3")
+        L(qc, PO, 2, 2, "sg2 sg3", "qPO")
+
+    def consts_weights():
+        for n, s, k, a in (("bw", "l8", LN2, 0), ("bx", "l8", LN2, -math.log(SIG)), ("t0", "g", LN2, 8 * LN2),
+                           ("t1", "g", LN2, 8 * LN2 - 200), ("u0", "hb", -200, "t0"), ("u1", "hb", 200, "t1"),
+                           ("u2", "u0", 1, -math.log(SIG)), ("u3", "u1", 1, -math.log(SIG))):
+            lin(n, s, k, a)
+
+    def consts_tail_numbers():
+        for n, s, k, a in (("fl", "l8", -3, 1), ("fu", "lB", -3, 1), ("fs", "s", -2, 2), ("t0", "s", 4, 0), ("t1", "q", 0.5, 0),
+                           ("th", "l8", -4, "t0"), ("t2", "g", 10, "t1"), ("tl", "p1", 79.5, "t2")):
+            lin(n, s, k, a)
 
     def consts_tail_scalar():
-        af(pc(28, 3), pc(10, 3), 1.0, 1.0, "L0 L1 L2", "l16")
-        af(pc(58), pc(2), 1.0, 2.0, "pf", "f58")
-        af(T.lsr[:], T.lsr[:], pc(57), 0.0, "lsr0 lsr1 sp", "lsr0 lsr1")
-        af(T.msr[:], T.msr[:], pc(57), 0.0, "msr00 msr01 msr10 msr11 sp", "msr00 msr01 msr10 msr11")
-        af(pc(71), pc(6), 16.0, pc(7), "pf", "g40")
-        af(pc(72), pc(6), 16.0, pc(8), "pf", "g41")
-        af(pc(59), pc(7), -1.0, pc(8), "pf", "th0")
-        af(pc(45), pc(7), -1.0, 0.0, "pf dif", "g45")
-        af(pc(61), pc(3), 16.0, 0.0, "pf", "h16")
-        af(pc(60), pc(59), 1.0, 4.0, "th0", "th1")
-        af(pc(46, 3), pc(10, 3), 1.0, pc(61), "L0 L1 L2 h16 dif", "g46")
-        af(pc(49, 3), pc(13, 3), 1.0, pc(61), "S0 S1 S2 h16 dif", "g49")
-        for j, c in enumerate((7.0, 8.0, 11.0, 12.0)):
-            af(pc(73 + j), pc(72), 1.0, c, "g41", "g7%d" % j)
-        zero(T.cb, 512 * SS + 3, 512 * FB, "z1", 4)
-        for i in range(FB, NT):
-            zero(T.cb, 512 * i, 512 * i + 512, "z%d" % i)
+        for j, (row, k, b) in enumerate(((T.lr, 3.0, "fl"), (T.lr, 3.0, "fu"), (T.r8, 2.0, "fs"))):
+            act(T.fa[:, 512:640], row[:], F.Relu, "lr r8 _" + b, "fa3", scale=k, bias=pc(b))
+            act(T.fa[:, 128 * j:128 * j + 128], T.fa[:, 512:640], F.Relu, "fa3", "fa0 fa1", scale=-1.0, bias=4.0)
+        af(sg(1, 0), T.fa[:, 0:128], 1.0, -4.0, "fa0", "sg1")
 
     def consts_tail():
-        L(ts, pc(42), pc(8), 0.0, None, EQ, None, "pf dif", "g42")
-        L(ts, pc(77), pc(5), 10.0, 128.0, A.is_ge, A.mult, "pf", "f77")
-        for t in range(3):
-            L(ts, T.tk[:, 0:128], T.lsr[:], pc(28 + t), -1.0, A.is_gt, A.mult, "lsr0 l16", "tk0")
-            L(ts, T.tk[:, 128:256], T.lsr[:], pc(28 + t), -64.0, EQ, A.mult, "lsr0 l16", "tk1")
-            L(ts, T.cb[:, 512 * SS + t:512 * FA:4], T.ssr[:], pc(22 + t), 0.5, EQ, A.mult, "ssr sid", "cSS%d" % t)
-            L(tt, cslot(FA, t), T.tk[:, 0:128], T.tk[:, 128:256], A.add, "tk0 tk1", "cFA%d" % t)
-        L(ts, pc(43), pc(42), 7.0, 1.0, A.mult, A.add, "g42", "g43")
-        L(ts, pc(44), pc(42), -1.0, pc(7), A.add, A.mult, "g42 pf", "g44")
-        L(ts, li[:, 88:96], li[:, 36:44], pc(5), pc(77), A.add, A.add, "li2 pf f77", "li5")
-        L(ts, T.cb[:, 512 * FB + 2:512 * KG:4], T.msr[:], pc(58), None, A.is_ge, None, "msr00 f58 z19 z20", "cFB")
-        L(qz, "c", 128 * SS, 128 * FB, cb(SS, 3), "cSS0 cSS1 cSS2 cFA0 cFA1 cFA2 z1", "qSS")
-        L(qz, "c", 128 * FB, 128 * KG, cb(FB, 2), "cFB", "qFB")
-        L(ts, sub("so"), li[:, 88:96], 127.0, None, A.min, None, "li5", "so")
-        L(ts, cslot(KG, 0, 0, 32), T.nr[:, 0:32], pc(71), pc(43), EQ, A.mult, "nr g40 g43 z21", "cKGa")
-        L(ts, cslot(KG, 1, 0, 32), T.nr[:, 0:32], pc(71), None, EQ, None, "nr g40 z21", "cKGb")
-        for u in range(2):
-            L(ts, T.tk[:, 32 * u:32 * u + 32], T.nr[:, 0:32], pc(73 + 2 * u), pc(44 + u), EQ, A.mult, "nr g70 g72 g44 g45", "tk0")
-            L(ts, T.tk[:, 128 + 32 * u:160 + 32 * u], T.nr[:, 0:32], pc(74 + 2 * u), pc(7), EQ, A.mult, "nr g71 g73 pf", "tk1")
-        for t in range(3):
-            L(ts, cslot(KS, t, 0, 32), T.nr[:, 0:32], pc(46 + t), pc(13 + t), EQ, A.mult, "nr g46 S0 S1 S2 z22", "cKSa%d" % t)
-            L(ts, cslot(KS, t, 32, 64), T.nr[:, 0:32], pc(49 + t), pc(10 + t), EQ, A.mult, "nr g49 L0 L1 L2 z22", "cKSb%d" % t)
-        for u in range(2):
-            L(tt, cslot(KG, u, 32, 64), T.tk[:, 32 * u:32 * u + 32], T.tk[:, 128 + 32 * u:160 + 32 * u], A.add, "tk0 tk1 z21", "cKG%d" % u)
-        L(qz, "c", 128 * KG, 128 * NT, cb(KG, 2), "cKGa cKGb cKG0 cKG1 cKSa0 cKSa1 cKSa2 cKSb0 cKSb1 cKSb2", "qK")
-        L(qz, "c", 128 * WQ, 128 * (WQ + 2), cb(WQ, 2), "cWQ0 cWQ1", "qWa")
-        L(qz, "c", 128 * (WQ + 2), 128 * W1, cb(WQ + 2, 2), "cWQ2 cWQ3", "qWb")
+        L(ms, sg(3, 0), 0.0, "sg3")
+        L(ts, sg(2, 0), T.r8[:], pc("s"), 0.5, EQ, MUL, "r8 _s", "sg2")
+        L(ts, sg(3, 2), T.r8[:], pc("s"), 0.5, EQ, MUL, "r8 _s", "sg3")
+        for t, (a, b) in enumerate((("l8", "s"), ("l8", "sB"), ("lB", "sB"))):
+            L(ts, sg(0, t), T.r16[:, 0:128], pc(a), pc(b), EQ, MUL, "r16 _%s _%s" % (a, b), "sg0")
+        L(qc, SS, 2, 2, "sg2 sg3", "qSS")
+        L(tt, sg(1, 2), T.fa[:, 128:256], T.fa[:, 256:384], A.subtract, "fa0 fa1", "sg1")
+        for t, (a, b) in enumerate((("s", "l8"), ("sB", "l8"), ("sB", "lB"))):
+            L(ts, sg(2, t), T.r16[:, 0:128], pc(a), pc(b), EQ, MUL, "r16 _%s _%s" % (a, b), "sg2")
+        L(qc, MU, 0, 2, "sg0 sg1", "qMU")
+        L(ts, kf[:, 112:114], li[:, 16:18], 0.5, pc("tl"), MUL, ADD, "li1 _tl", "k8")
+        L(qc, MI, 2, 1, "sg2", "qMI")
+        L(ts, sub("tl"), kf[:, 112:114], NB - 1.0, None, A.min, None, "k8", "tl")
 
     def pick32(src, skey, dst, dkey):
-        tt(T.tmp[:], src[:].indirect(sub("xy")), T.m10[:], A.min, skey + " xy m10", "tmp")
-        scan(dst[:], T.k10[:], T.tmp[:], -BIG, A.min, A.max, "k10 tmp", dkey)
+        tt(T.tmp[:], src[:].indirect(sub("xy")), T.e10[:], MUL, skey + " xy e10", "tmp")
+        scan(dst[:], T.k10[:], T.tmp[:], 0.0, MUL, ADD, "k10 tmp", dkey)
 
-    def decode(name, b, bank, out, okey):
-        mm(bank, C, ct(E0 + b), (name, 0), True, True, "qE " + name)
+    def et(b):
+        return ct(E0 + SLOT.index(b))
+
+    def decode(name, key, b, bank, out, okey):
+        mm(bank, C, et(b), (name, 0), True, True, "qE " + key)
         act(out, ps[bank][:, 0:C], F.Copy, "ps%d" % bank, okey, scale=1.0 / 32)
-
-    def plane(buf, b):
-        return buf[:, C * b:C * b + C]
 
     def so_view(i):
         u, t = (20 - i) // 4, (20 - i) % 4
         return T.sot[:, 4 * SOFF[u] + t:4 * (SOFF[u] + 16 * i):4], "so%d%d" % (u, t), T.jk[:, 8 * i * (i - 1):8 * i * (i + 1)]
 
-    def compare(d, w, base, tile0):
-        u, t = tile0 + (d - 1) // 4, (d - 1) % 4
-        n = (w - d) * 16
-        tt(T.cot[:, 4 * COFF[u] + t:4 * (COFF[u] + n):4], T.dd[:, base:base + n], T.dd[:, base + 16 * d:base + 16 * w], A.is_le,
-           ("dd1" if tile0 == 0 else "dd2") + " cz%d" % u, "co%d%d" % (u, t))
+    def shifts(h):
+        return (DL, 8) if h < 2 else (DU, 16)
 
-    def quant_co(u):
-        qz("co", QOFF[u], QOFF[u] + CWID[u], T.cot[:, 4 * COFF[u]:4 * (COFF[u] + CWID[u])],
-           " ".join("co%d%d" % (u, t) for t in range(4)), "coq%d" % u)
+    def compare(h, u, t):
+        D, w = shifts(h)
+        d, a = D[u][t], 2048 * h + 512 * u
+        n = 128 - w * d
+        tt(T.cot[:, a + t:a + 4 * n:4], T.dd[:, 128 * h:128 * h + n], T.dd[:, 128 * h + w * d:128 * h + 128], A.is_le,
+           "dd%d cz%d%d" % (h, h, u), "co%d%d%d" % (h, u, t))
 
-    def rank_mm(u, tile0, nlam, bk, last):
-        u0 = u - tile0
-        for lam in range(nlam):
-            todo = []
-            if lam == 0 or u0 < 2:
-                todo.append((QOFF[u] + 128 * lam, 4))
-            for t in range(4):
-                d = 4 * u0 + t + 1
-                if d <= 8 * lam + 7:
-                    todo.append((QOFF[u] + 128 * lam - 16 * d, t))
-            for j, (a, k) in enumerate(todo):
-                mm(bk[lam], 128, ("co", a), ("k", 128 * k), u0 == 0 and j == 0, last and j == len(todo) - 1,
-                   "coq%d k%dc k%ds" % (u, k, k))
+    def quant_co(h, u, n):
+        a, b = 128 + 640 * h + 128 * u, 2048 * h + 512 * u
+        qz("co", a, a + 128 * n, T.cot[:, b:b + 512 * n], " ".join("co%d%d%d" % (h, v, t) for v in range(u, u + n) for t in range(4)),
+           " ".join("cq%d%d" % (h, v) for v in range(u, u + n)))
 
-    def list_pick(tile, a, off, mask):
-        tt(T[tile][:, 0:C], T.tw[:, a:a + 32].indirect(sub(off)), T[mask][:], A.mult, "tw %s %s" % (off, mask), tile)
+    def rank_mm(h, u, bank):
+        D, w = shifts(h)
+        a = 128 + 640 * h + 128 * u
+        before = "cq%d%d" % (h, u - 1) if u else ("coz", "cy640c cy640s", "cy1280c cy1280s")[h]
+        mm(bank, 128, ("co", a), ct(KN), u == 0, False, "cq%d%d qKN" % (h, u))
+        for t, d in enumerate(D[u]):
+            mm(bank, 128, ("co", a - w * d), ct(K0 + SLOT.index(t)), False, u == len(D) - 1 and t == len(D[u]) - 1,
+               "cq%d%d qK %s" % (h, u, before))
 
-    def list_sum(tile, a, bank):
-        qz("h", a, a + 130, T[tile][:, 0:520], tile, "a" + tile)
-        qz("h", a + 132, a + 262, T[tile][:, 4:524], tile, "b" + tile)
-        for i in (0, 2, 1, 3):
-            mm(bank, 128, ct(WQ + i), ("h", a + 132 * (i % 2) + 2 * (i // 2)), i == 0, i == 3, "qWa qWb " + "ab"[i % 2] + tile)
+    def weigh(out, bank, bias, W):
+        act(out, ps[bank][:, 0:NB // 2], F.Exp, "ps%d _%s" % (bank, bias), W, scale=-LN2 / 32, bias=pc(bias))
 
-    def list_end(bank, base, t32, out, okey):
-        tt(sub(t32), ps[bank][:, 0:80:4], sub(base), A.add, "ps%d %s" % (bank, base), t32)
-        cp(out, sub(t32), t32, okey)
+    def preload(k):
+        mm(LB[k % 2], NB, ct(PG), ("wt", 0), True, False, "qPG wtq")
+        mm(LB[k % 2], NB, ct(PO), ("wt", 0), False, k == 0, "qPO wtq")
+        if k >= 7:
+            mm(UB[k % 2], NB, ct(PG + 1), ("w2", 0), True, False, "qPG w2q")
+            mm(UB[k % 2], NB, ct(PO + 1), ("w2", 0), False, False, "qPO w2q")
 
-    def thr(t):
-        bank = (7, 2, 7)[t]
-        ts(T.thr[:, 128 * t:128 * t + NB], ps[bank][:, 0:NB], 1.0 + 2.0 / GG, pc(68 + t), A.mult, A.add, "ps%d z0" % bank, "thr%d" % t)
+    def places(tile, bank, mid, out, okey):
+        mm(bank, NB, ct(tile), ("s2", 0), True, True, "qMU qMI s2q")
+        tt(T[mid][:], ps[bank][:, 0:NB], T.bs[:], ADD, "ps%d bs" % bank, mid)
+        cp(out, T[mid][:].indirect(sub("tl")), mid + " tl", okey)
 
     for r in range(NR):
         s = str(r)
         xq, first, final = "x" + s, r == 0, r == NR - 1
+        xk = "%sa %sb" % (xq, xq)
         pl, olist, hl, lp, ln, lv, lh = (sub(a + s) for a in ("pl", "ol", "hl", "lp", "ln", "lv", "lh"))
-        mm(0, C, ("up", 0), (xq, 0), True, True, "upc ups " + xq)
-        mm(3, C, ("up", 0), (xq, 0), True, True, "upc ups " + xq)
-        mm(1, C, ("up", 128), (xq, 0), True, True, "upc ups " + xq)
-        bg(2)
+        mm(0, C, ("up", 0), (xq, 0), True, True, "up0c up0s " + xk)
+        mm(3, C, ("up", 0), (xq, 0), True, True, "up0c up0s " + xk)
+        bg(1)
         tt(T.sq[:], ps[0][:, 0:C], T.m16[:], A.min, "ps0 m16", "sq")
         bg(1)
         scan(T.sb[:], T.k16[:], T.sq[:], -BIG, A.min, A.max, "k16 sq", "sb")
         bg(1)
-        low = 14 if first else 18
+        mm(1, C, ("up", 128), (xq, 0), True, True, "up1c up1s " + xk)
+        low, few = LOW[r], FEW[r]
         for i in range(19, low - 1, -1):
             view, key, jk = so_view(i)
             act(jk, ps[3][:, 0:16 * i], F.Sign, "sb ps3", "jk%d" % i, scale=-1.0, bias=T.sb[:, 16 * i + 15:16 * i + 16])
             act(view, jk, F.Relu, "jk%d sz0 sz1" % i, key + " rs%d" % i, accum_out=sub("rs", i, i + 1))
-        after = {2: [0], 3: [1, 2], 4: [3, 4]} if first else {1: [0, 1], 2: [2], 3: [3], 4: [4]}
+        after = {1: [0, 1], 2: [2], 3: [3], 4: [4]}
         for u in range(5):
             for t in range(4):
                 i = 20 - 4 * u - t
@@ -517,10 +508,14 @@ def rank_program(g, core, T, topo):
                     tt(view, T.sb[:], ps[0][:, 0:C], A.is_ge, "sb ps0 sz0", key)
                 elif i < low:
                     ts(view, ps[0][:, 0:16 * i], T.sb[:, 16 * i + 15:16 * i + 16], None, A.is_lt, None, "sb ps0 sz%d" % u, key)
-                    act(jk, view, F.Copy, key, "rs%d jk%d" % (i, i), accum_out=sub("rs", i, i + 1))
-                bg(2)
+                    if i > few:
+                        act(jk, view, F.Copy, key, "rs%d jk%d" % (i, i), accum_out=sub("rs", i, i + 1))
+                    bg(1)
+            for i in range(min(few, 20 - 4 * u), max(0, 16 - 4 * u), -1):
+                view, key, jk = so_view(i)
+                op("V", lambda q, i=i, view=view: q.tensor_reduce(sub("rs", i, i + 1), view, AxisListType.X, ADD), key, "rs%d" % i)
             if u == 0:
-                scan(T.ru[:], T.k01[:], T.sot[:, 0:4 * C:4], 0.0, A.mult, A.add, "k01 so00", "ru")
+                scan(T.ru[:], T.k01[:], T.sot[:, 0:4 * C:4], 0.0, MUL, ADD, "k01 so00", "ru")
             if u == 1:
                 tt(sub("pre"), sub("cbs"), T.ru[:, 15:C:16], A.subtract, "cbs ru", "pre")
             for v in after.get(u, []):
@@ -528,219 +523,196 @@ def rank_program(g, core, T, topo):
                    " ".join("so%d%d" % (v, t) for t in range(4)), "soq%d" % v)
                 mm(2, SWID[v], ct(WB), ("so", SOFF[v]), v == 0, v == 4, "qWB soq%d" % v)
         tt(sub("pre"), sub("pre"), sub("rs"), A.subtract, "pre " + " ".join("rs%d" % i for i in range(20)), "pre")
-        act(T.mk[:], ps[1][:, 0:C], F.Copy, "ps1", "mk")
-        scan(T.ls[:], T.pen[:], ps[2][:, 0:C], 0.0, A.add, A.max, "pen ps2", "ls")
-        bg(1)
-        tt(sub("pli"), T.ls[:, 15:C:16], sub("pre"), A.add, "ls pre", "pli")
-        bg(1)
+        sc(T.mk[:], ps[1][:, 0:C], "ps1", "mk")
+        scan(T.ls[:], T.pen[:], ps[2][:, 0:C], 0.0, ADD, A.max, "pen ps2", "ls")
+        tt(sub("pli"), T.ls[:, 15:C:16], sub("pre"), ADD, "ls pre", "pli")
         cp(pl, sub("pli"), "pli", "pl" + s)
         send(prv, lp, pl, "al" + s, "pl" + s)
         bg(99)
         if first:
-            op("G", lambda q: q.partition_broadcast(T.pkr[:], T.pkb[0:1, :], 128), "pk0 pk1 pk2 pk3 pk4 pk5", "pkr")
-            af(T.m10[:], T.e16[:], 2 * BIG, -BIG, "e16", "m10")
-            af(T.k10[:], T.mko[:], 2 * BIG, -BIG, "mko", "k10")
-            qz("c", 0, 512, cb(E0, 4), "cE0 cE1 cE2 cE3", "qE")
+            qc(E0, 0, 4, "sg0 sg1 sg2 sg3", "qE")
+            for i in range(4):
+                sel(T.sg[:, 512 * i + SLOT[i]:512 * i + 520:4], T.zb[:, 0:130], [[-16, 13], [-1, 10]], A.not_equal, 32.0, 0, 1,
+                    "zb", "sg%d sg%d" % (i, i + 1))
+            sel(T.kn[:], T.zb[:, 0:520], [[-16, 13], [-1, 10], [0, 4]], A.not_equal, -32.0, 0, 1, "zb", "kn")
         cp(T.ms[:].indirect(pl), T.mk[:], "mk pl" + s, "ms")
         arrive(nxt, "an" + s, 2, "n" + s)
-        mm(1, C, ("up", 128), ("n" + s, 0), True, True, "upc ups n" + s)
-        act(T.mn[:], ps[1][:, 0:C], F.Copy, "ps1", "mn")
-        if first:
-            for u in range(4):
-                zero(T.cot, 4 * (COFF[u] + CZERO[u]), 4 * (COFF[u] + CWID[u]), "cz%d" % u)
+        mm(1, C, ("up", 128), ("n" + s, 0), True, True, "up1c up1s n" + s)
+        sc(T.mn[:], ps[1][:, 0:C], "ps1", "mn")
         pick32(T.ms, "ms", T.sa, "sa")
         for b in range(2):
-            decode(xq, b, 4 + b, slot(T.at, b, C), "at%d" % b)
-        act(T.aex[:], T.sa[:].indirect(sub("al")), F.Copy, "sa al0 al1 al2", "aex")
+            decode(xq, xk, b, 4 + b, slot(T.at, b, 0, C), "at%d" % b)
+        sc(T.aex[:], T.sa[:].indirect(sub("al")), "sa al0 al1", "aex")
         for b in range(2, 4):
-            decode(xq, b, 4 + b, slot(T.at, b, C), "at%d" % b)
+            decode(xq, xk, b, 4 + b, slot(T.at, b, 0, C), "at%d" % b)
+        if first:
+            consts_keys()
         arrive(nxt, "al" + s, 1, "lp" + s)
         cp(T.ms[:].indirect(lp), T.mn[:], "mn lp" + s, "ms")
+        if first:
+            consts_rows()
         pick32(T.ms, "ms", T.sa, "sa")
         tt(T.d0[:, 0:256], T.sa[:].indirect(sub("bl", 0, 16)), T.aex[:, 0:256], A.subtract, "sa bl0 aex", "d01")
-        act(T.dd[:, 0:256], T.d0[:, 0:256], F.Abs, "d01", "dd1")
+        for h in range(2):
+            act(T.dd[:, 128 * h:128 * h + 128], T.d0[:, 128 * h:128 * h + 128], F.Abs, "d01", "dd%d" % h)
         qz("g" + s, 0, C, T.at[:], "at0 at1 at2 at3", "g" + s)
         send_q(nxt, "g" + s, "p" + s, "ap" + s, "g" + s)
         if first:
-            consts_pool2()
-            qz("c", 128 * KN, 128 * WB, cb(KN), "cKN", "qKN")
-            qz("co", QOFF[3] - PAD, QOFF[3] - PAD + 128, T.zb[:], "zb", "coq3")
-            for i in range(5):
-                pick("k", 128 * i, "c", 128 * i, 128, sub("ko"), 128, "qE qKN ko", "k%d" % i)
-            for j, i in enumerate((W1, WG)):
-                zero(T.cb, 512 * i + 3, 512 * (i + 3), "cy%d" % j, 4)
-                zero(T.cb, 512 * i + 2, 512 * (i + 2), "cy%d" % (j + 2), 4)
-            for a in ("wt", "xs"):
-                zero(T[a], 0, 512, a + "0 " + a + "1 " + a + "2")
-            for u in range(4, 6):
-                zero(T.cot, 4 * (COFF[u] + CZERO[u]), 4 * (COFF[u] + CWID[u]), "cz%d" % u)
-        for b in range(4):
-            decode("n" + s, b, (0, 1, 5, 6)[b], plane(T.vp, b), "vp%d" % b)
-        for u in range(4):
-            for d in range(4 * u + 1, min(4 * u + 5, 16)):
-                compare(d, 16, 0, 0)
-            if first and u == 2:
-                consts_court()
-            quant_co(u)
-            rank_mm(u, 0, 2, (3, 4), u == 3)
-        for t in range(2):
-            act(slot(T.wt, t), ps[3 + t][:, 0:NB], F.Exp, "ps%d bwa" % (3 + t), "wt%d" % t, scale=-LN2 / 32, bias=pc(37 + t))
-        for t in range(2):
-            act(slot(T.xs, t), ps[3 + t][:, 0:NB], F.Exp, "ps%d b0" % (3 + t), "xs%d" % t, scale=-LN2 / 32, bias=pc(52 + t))
-        tt(T.d0[:, 256:384], T.sa[:].indirect(sub("bl", 16, 24)), T.aex[:, 256:384], A.subtract, "sa bl1 aex", "d02")
-        act(T.dd[:, 256:384], T.d0[:, 256:384], F.Abs, "d02", "dd2")
-        if first:
-            for i in (4, 5):
-                qz("co", QOFF[i] - PAD, QOFF[i] - PAD + 128, T.zb[:], "zb", "coq%d" % i)
-            ts(T.bm[:], T.bm[:], pc(5), None, EQ, None, "bm pf", "bm")
+            iota(T.r8[:], [[0, 16], [1, 8]], 0, 0, "r8")
+            iota(T.lr[:], [[1, 16], [0, 8]], 0, 0, "lr")
+            iota(T.bs[:], [[16, 2], [0, 8], [32, 10]], 0, 0, "bs")
+            consts_weights()
+            consts_court()
+            bg(2)
         else:
-            ms(slot(T.xs, 2), 0.0, "xs2")
-        qz("wt", 0, 128, T.wt[:], "wt0 wt1 wt2", "wtq")
-        for t in range(2):
-            mm((7, 2)[t], 128, ct(WG + t), ("wt", 0), True, True, "qWG wtq")
-        qz("xs", 0, 128, T.xs[:], "xs0 xs1 xs2", "xsq")
-        thr(0)
-        thr(1)
-        for d in range(1, 6):
-            L(compare, d, 8, 256, 4)
-        L(quant_co, 4)
-        L(rank_mm, 4, 4, 1, (2,), False)
-        L(compare, 6, 8, 256, 4)
-        L(compare, 7, 8, 256, 4)
-        L(quant_co, 5)
-        L(rank_mm, 5, 4, 1, (2,), True)
-        L(act, slot(T.wt, 2), ps[2][:, 0:NB], F.Exp, "ps2 bwb", "wt2", scale=-LN2 / 32, bias=pc(39))
-        L(cp, sub("pni"), lp, "lp" + s, "pni")
-        L(ts, sub("t2"), sub("pli"), 31, None, AND, None, "pli", "t2")
-        L(ts, sub("bo"), sub("pli"), 496, None, AND, None, "pli", "bo")
-        L(qz, "wt", 0, 128, T.wt[:], "wt0 wt1 wt2", "wtq")
-        L(mm, 7, 128, ct(WG + 2), ("wt", 0), True, True, "qWG wtq")
-        L(cp, sub("o32"), sub("t2"), "t2", "o32")
-        L(ts, sub("t1"), sub("pni"), 31, None, AND, None, "pni", "t1")
-        L(thr, 2)
-        n_early = len(bgq)
-        L(ts, sub("bn"), sub("pni"), 496, None, AND, None, "pni", "bn")
-        L(cp, sub("n32"), sub("t1"), "t1", "n32")
+            zero(T.xs, 2, 4 * NB, "xs2", 4)
+        for h in range(2):
+            for u in range(4):
+                for t in range(len(DL[u])):
+                    compare(h, u, t)
+                    bg(1)
+                n = ((0, 2, 0, 2), (0, 2, 1, 1))[h][u]
+                if n:
+                    quant_co(h, u + 1 - n, n)
+                for w in range(u + 1 - n, u + 1):
+                    rank_mm(h, w, 3 + h)
+                if h == 1 and u == 0:
+                    weigh(slot(T.wt, 0, 0, 80), 3, "bw", "wt00")
+                    weigh(T.wp[:, 0:80], 3, "bx", "wp0")
+                if u == 2 * (1 - h):
+                    for b in (2 * h, 2 * h + 1):
+                        decode("n" + s, "n" + s, b, (0, 1, 2, 7)[b], plane(T.vp, b), "vp%d" % b)
+        bg(99)
+        weigh(slot(T.wt, 0, 80, NB), 4, "bw", "wt01")
+        weigh(T.wp[:, 80:NB], 4, "bx", "wp1")
+        tt(T.d0[:, 256:384], T.sa[:].indirect(sub("bl", 16, 24)), T.aex[:, 256:384], A.subtract, "sa bl1 aex", "d02")
+        qz("wt", 0, NB, T.wt[:], "wt00 wt01 wt1 wt2 wt3", "wtq")
+        act(T.dd[:, 256:384], T.d0[:, 256:384], F.Abs, "d02", "dd2")
+        preload(0)
+
+        def upper_weights():
+            for h in range(2):
+                weigh(slot(T.wt, 2, 80 * h, 80 * h + 80), 2, "u%d" % h, "wt2")
+            for h in range(2):
+                weigh(T.wp[:, NB + 80 * h:NB + 80 * h + 80], 2, "u%d" % (h + 2), "wp2")
+
+        def order_row(a, b):
+            cp(T.orow[:].indirect(sub("pl" + s, a, b)), T.iot[:, 16 * a:16 * b], "iot pl" + s, "orow")
+
+        def order_list():
+            ts(olist, T.ls[:, 15:C:16], pc("o0"), None, ADD, None, "ls _o0", "ol" + s)
+            send(prv, ln, olist, "ao" + s, "ol" + s)
+            send(nxt, lv, olist, "av" + s, "ol" + s)
+
+        def sent(b):
+            decode("p" + s, "p" + s, b, (1, 3, 4, 1)[b], plane(T.gp, b), "gp%d" % b)
+
+        gaps = [[(compare, 2, 0, 0), (compare, 2, 0, 1), (compare, 2, 0, 2), (order_row, 0, 6)],
+                [(compare, 2, 0, 3), (order_row, 6, 12), (quant_co, 2, 0, 1)],
+                [(compare, 2, 1, 0), (order_row, 12, 16)],
+                [(compare, 2, 1, 1), (order_row, 16, 20)],
+                [(compare, 2, 1, 2), (scan, T.ls[:], T.pen[:], T.orow[:], 0.0, ADD, A.max, "pen orow", "ls"), (quant_co, 2, 1, 1)],
+                [(order_list,), (qz, "w2", 0, NB, T.wt[:], "wt00 wt01 wt1 wt2 wt3", "w2q")]]
+        behind = {1: [(sent, 0)], 2: [(rank_mm, 2, 0, 2)], 3: [(sent, 1)], 4: [(sent, 2)], 5: [(rank_mm, 2, 1, 2), (upper_weights,)],
+                  6: [(sent, 3)]}
         if first:
             consts_tail()
-        per = [1, 1, 1, 4, 4, 3, 5]
-        rest = len(bgq) - n_early
         arrive(prv, "ap" + s, 2, "p" + s)
         arrive(nxt, "ao" + s, 1, "ln" + s)
         arrive(prv, "av" + s, 1, "lv" + s)
         for k in range(SW - 1):
-            nt = 2 if k < 7 else 3
-            if k == 7:
-                bg(len(bgq) - rest)
-            for t in range(nt):
-                mm(5 + t, 128, ct(W1 + t), ("xs", 0), True, False, "qW1 xsq")
-                mm(5 + t, 128, ct(WG + t), ("xs", 0), False, True, "qWG xsq")
-            if k == 0:
-                if first:
-                    dma("Y", T.lwc[:].bitcast(dt.uint8), T.wc[:], "thr1", "wq")
-                    dma("Y", T.lws[:], T.ws[:], "", "wsc")
-                    dma("Y", T.vt[:], T.v[:], "", "vt")
-                act(T.mkn[:], T.bm[:].indirect(lp), F.Copy, "bm lp" + s, "mkn")
-                act(T.mko[:], T.bm[:].indirect(pl), F.Copy, "bm pl" + s, "mko")
-                if first:
-                    consts_tail_scalar()
-            if k == 6 and first:
-                for a in ("st", "gt"):
-                    zero(T[a], 0, 512, a + "0 " + a + "1 " + a + "2")
-                for a in ("h1", "h2"):
-                    zero(T[a], C, 544, a)
-            if 2 <= k <= 5:
-                decode("p" + s, k - 2, banks[k - 2], plane(T.gp, k - 2), "gp%d" % (k - 2))
-            if k <= 3:
-                a, b = ((0, 6), (6, 12), (12, 16), (16, 20))[k]
-                cp(T.orow[:].indirect(sub("pl" + s, a, b)), T.iot[:, 16 * a:16 * b], "iot pl" + s, "orow")
-            if k == 4:
-                scan(T.ls[:], T.pen[:], T.orow[:], 0.0, A.add, A.max, "pen orow", "ls")
-            if k == 5:
-                ts(olist, T.ls[:, 15:C:16], pc(0), None, A.add, None, "ls pf0", "ol" + s)
-                send(prv, ln, olist, "ao" + s, "ol" + s)
-                send(nxt, lv, olist, "av" + s, "ol" + s)
+            if k:
+                mm(LB[k % 2], NB, ct(MX), ("xs", 0), False, True, "qMX xsq")
             if k >= 7:
-                b = k - 7
-                act(plane(T.vo, b), plane(T.vp, b).indirect(ln), F.Copy, "vp%d ln%s" % (b, s), "vo%d" % b)
-                act(plane(T.go, b), plane(T.gp, b).indirect(lv), F.Copy, "gp%d lv%s" % (b, s), "go%d" % b)
-            bg(per[k] if k < 7 else 6 if first else 1)
-            for t in range(nt):
-                tt(slot(T.rt, t), ps[5 + t][:, 0:NB], T.thr[:, 128 * t:128 * t + NB], A.is_gt, "ps%d thr%d" % (5 + t, t), "rt%d" % t)
-                if t:
-                    tt(slot(T.xs, t - 1), slot(T.rt, t - 1), slot(T.wt, t - 1), A.mult, "rt%d wt%d" % (t - 1, t - 1), "xs%d" % (t - 1))
-            t = nt - 1
-            tt(slot(T.xs, t), slot(T.rt, t), slot(T.wt, t), A.mult, "rt%d wt%d" % (t, t), "xs%d" % t)
-            qz("xs", 0, 128, T.xs[:], "xs0 xs1 xs2", "xsq")
+                mm(UB[k % 2], NB, ct(MX + 1), ("xs", 0), False, True, "qMX xsq")
+            if k < SW - 2:
+                preload(k + 1)
+            if k == 0 and first:
+                dma("Y", T.lwc[:].bitcast(dt.uint8), T.wc[:], "wtq", "wq")
+                dma("Y", T.lws[:], T.ws[:], "", "wsc")
+                dma("Y", T.vt[:], T.v[:], "", "vt")
+            for call in behind.get(k, ()):
+                call[0](*call[1:])
+            if k == 0 and first:
+                consts_tail_numbers()
+            if k == 5 and first:
+                consts_tail_scalar()
+            if k == 10 and final:
+                sc(T.onr[:], T.iot[:].indirect(ln), "iot ln" + s, "onr")
+            if k >= 7:
+                sc(plane(T.vo, k - 7), plane(T.vp, k - 7).indirect(ln), "vp%d ln%s" % (k - 7, s), "vo%d" % (k - 7))
+            tt(slot(T.xs, 0), ps[LB[k % 2]][:, 0:NB], T.wp[:, 0:NB], A.min, "ps%d wp0 wp1" % LB[k % 2], "xs0")
+            if k >= 7:
+                tt(slot(T.xs, 2), ps[UB[k % 2]][:, 0:NB], T.wp[:, NB:C], A.min, "ps%d wp2" % UB[k % 2], "xs2")
+            live = T.xs[:, 0:4 * NB:2] if k >= 7 else slot(T.xs, 0)
+            ts(live, live, 0.0, SIG, A.max, MUL, "xs0 xs2", "xs0 xs2" if k >= 7 else "xs0")
+            qz("xs", 0, NB, T.xs[:], "xs0 xs1 xs2 xs3", "xsq")
+            for call in gaps[k] if k < len(gaps) else ():
+                call[0](*call[1:])
+            if k >= len(gaps):
+                bg(3)
+        bg(99)
         for t in range(2):
-            mm(5 + t, 128, ct(SS + t), ("xs", 0), True, True, "qSS xsq")
-        bg(5)
-        for t in range(3):
-            tt(slot(T.st, t), ps[5 + t // 2][:, 0:NB], slot(T.xs, t), A.is_lt, "ps%d xs%d" % (5 + t // 2, t), "st%d" % t)
-        qz("st", 0, 128, T.st[:], "st0 st1 st2", "stq")
-        pick("s2", 0, "st", 0, 128, sub("so"), 128, "stq so", "s2")
-        for u in range(2):
-            mm(3 + u, 128, ct(FA), ("s2", 0), True, False, "qSS s2c s2s")
-            mm(3 + u, 128, ct(FB + u), ("s2", 0), False, True, "qFB s2c s2s")
-        bg(len(bgq) - 3)
-        for u in range(2):
-            ts(slot(T.gt, u, 128), ps[3 + u][:, 0:128], pc(59 + u), None, A.is_ge, None, "ps%d th0 th1" % (3 + u), "gt%d" % u)
-        bg(1)
-        qz("gt", 0, 128, T.gt[:], "gt0 gt1 gt2", "gtq")
-        mm(2, 128, ("s2", 0), ct(KS), True, False, "qK s2c s2s")
-        mm(2, 128, ("gt", 0), ct(KG), False, True, "qK gtq")
-        bg(2)
-        if final:
-            act(T.onr[:], T.iot[:].indirect(ln), F.Copy, "iot ln" + s, "onr")
-        cp(T.tw[:], ps[2][:, 0:64], "ps2", "tw")
-        list_pick("h1", 32, "n32", "mkn")
-        list_sum("h1", 0, 5)
-        list_pick("h2", 0, "o32", "mko")
-        list_end(5, "bn", "t1", hl, "hl" + s)
-        send(nxt, lh, hl, "ah" + s, "hl" + s)
-        list_sum("h2", 264, 6)
-        H = C // 2
-        hb = (banks, (2, 5, 7, 6))
-        for hf in range(2):
-            for b in range(4):
-                if hb[hf][b] == 6:
-                    list_end(6, "bo", "t2", sub("ix1"), "ix1")
-                mm(hb[hf][b], H, ct(E0 + b), (xq, H * hf), True, False, "qE " + xq)
-        for b in (2, 3):
-            act(plane(T.vg, b), plane(T.vo, b).indirect(sub("ix1")), F.Copy, "vo%d ix1" % b, "vg%d" % b)
-        for b in (0, 1):
-            cp(plane(T.vg, b), plane(T.vo, b).indirect(sub("ix1")), "vo%d ix1" % b, "vg%d" % b)
+            mm(3 + t, NB, ct(SS + t), ("xs", 0), True, True, "qSS xsq")
+        for b in (3, 0, 1, 2):
+            sc(plane(T.go, b), plane(T.gp, b).indirect(lv), "gp%d lv%s" % (b, s), "go%d" % b)
+        for t in range(2):
+            tt(slot(T.st, 2 * t), ps[3 + t][:, 0:NB], slot(T.xs, 2 * t), A.is_lt, "ps%d xs%d" % (3 + t, 2 * t), "st%d" % (2 * t))
+        qz("st", 0, NB, T.st[:], "st0 st1 st2 st3", "stq")
+        mm(1, NB, ct(FA), ("st", 0), True, True, "qMU stq")
         if final:
             qz("v", 0, 128, T.vt[:], "vt", "vq")
-            act(T.wrow[:], T.onr[:].indirect(sub("ix1")), F.Copy, "onr ix1", "wrow")
-            for k in range(8):
-                dma("Y", T.ol[k:k + 1, :], T.wrow[16 * k:16 * k + 1, :], "wrow", "")
-        arrive(prv, "ah" + s, 1, "lh" + s)
-        for hf in range(2):
-            act(T.g2[:, H * hf:H * hf + H], plane(T.go, 3).indirect(sub("lh" + s, 10 * hf, 10 * hf + 10)), F.Copy, "go3 lh" + s, "g2%d" % hf)
+        ts(slot(T.st, 1), ps[1][:, 0:NB], pc("th"), None, EQ, None, "ps1 _th", "st1")
+        qz("s2", 0, NB, T.st[:], "st0 st1 st2 st3", "s2q")
+        places(MI, 2, "mt", sub("hl" + s, 0, 32), "hl" + s)
+        send(nxt, lh, hl, "ah" + s, "hl" + s)
+        places(MU, 3, "mt2", sub("mu", 0, 32), "mu")
         for hf in range(2):
             for b in range(4):
-                a = plane(T.go, b).indirect(sub("lh" + s, 10 * hf, 10 * hf + 10)) if b < 3 else T.g2[:, H * hf:H * hf + H]
-                tt(T.zt[:, 4 * H * hf + b:4 * H * (hf + 1):4], a, T.vg[:, C * b + H * hf:C * b + H * hf + H], A.max,
-                   "vg3 g2%d" % hf if b == 3 else "go%d vg%d lh%s" % (b, b, s), "zt%d%d" % (hf, b))
+                mm(HB[hf][b], H, et(b), (xq, H * hf), True, False, "qE " + xk)
+        cp(plane(T.vq, 3), plane(T.vo, 3).indirect(sub("mu")), "vo3 mu", "vq3")
+        for b in (0, 1):
+            cp(plane(T.vq, b), plane(T.vo, b).indirect(sub("mu")), "vo%d mu" % b, "vq%d" % b)
+        sc(plane(T.vq, 2), plane(T.vo, 2).indirect(sub("mu")), "vo2 mu", "vq2")
+        sc(T.vg[:], plane(T.vq, 3).indirect(pl), "vq3 pl" + s, "vg")
+        if final:
+            sc(T.wrow[:], T.onr[:].indirect(sub("mu")), "onr mu", "wrow")
+        arrive(prv, "ah" + s, 1, "lh" + s)
+        sc(T.gq[:], plane(T.go, 3).indirect(lh), "go3 lh" + s, "gq")
+        for b in range(3):
+            tt(plane(T.zp, b), plane(T.go, b).indirect(lh), plane(T.vq, b), A.max, "go%d vq%d lh%s" % (b, b, s), "zp%d" % b)
+            if b < 2:
+                sc(slot(T.zt, b, 0, C), plane(T.zp, b).indirect(pl), "zp%d pl%s" % (b, s), "zt0%d zt1%d" % (b, b))
+        for hf in range(2):
+            half = sub("pl" + s, 10 * hf, 10 * hf + 10)
+            sc(slot(T.zt, 2, H * hf, H * hf + H), plane(T.zp, 2).indirect(half), "zp2 pl" + s, "zt%d2" % hf)
+            tt(slot(T.zt, 3, H * hf, H * hf + H), T.gq[:].indirect(half), T.vg[:, H * hf:H * hf + H], A.max, "gq vg pl" + s, "zt%d3" % hf)
+        if final:
+            sc(T.wro2[:], T.wrow[:].indirect(pl), "wrow pl" + s, "wro2")
+            for k in range(8):
+                dma("Y", T.ol[k:k + 1, :], T.wro2[16 * k:16 * k + 1, :], "wro2", "")
+        for hf in range(2):
             qz("z", H * hf, H * hf + H, T.zt[:, 4 * H * hf:4 * H * (hf + 1)], " ".join("zt%d%d" % (hf, b) for b in range(4)), "zq%d" % hf)
             for b in range(4):
-                mm(hb[hf][b], H, ("lw", 128 * b), ("z", H * hf), False, True, "wq wsc zq%d" % hf)
+                mm(HB[hf][b], H, ("lw", 128 * b), ("z", H * hf), False, True, "wq wsc zq%d" % hf)
         xq = "x%d" % (r + 1)
         for hf in range(2):
             for b in range(4):
-                o, bank = T.xn[:, 4 * H * hf + b:4 * H * (hf + 1):4], hb[hf][b]
-                if (hf == 1 and b % 2) or (hf == 0 and b == 3):
-                    ts(o, ps[bank][:, 0:H], 1.0 / 32, None, A.mult, None, "ps%d" % bank, "xn%d%d" % (hf, b))
+                o, bank = slot(T.xn, b, H * hf, H * hf + H), HB[hf][b]
+                if b % 2:
+                    ts(o, ps[bank][:, 0:H], 1.0 / 32, None, MUL, None, "ps%d" % bank, "xn%d%d" % (hf, b))
                 else:
                     act(o, ps[bank][:, 0:H], F.Copy, "ps%d" % bank, "xn%d%d" % (hf, b), scale=1.0 / 32)
-            qz(xq, H * hf, H * hf + H, T.xn[:, 4 * H * hf:4 * H * (hf + 1)], " ".join("xn%d%d" % (hf, b) for b in range(4)), xq)
+            qz(xq, H * hf, H * hf + H, T.xn[:, 4 * H * hf:4 * H * (hf + 1)], " ".join("xn%d%d" % (hf, b) for b in range(4)), xq + "ab"[hf])
+            if final:
+                mm(hf, H, ("v", 0), (xq, H * hf), True, True, "vq " + xq + "ab"[hf])
+                dma("Y", T.oc[:, 4 * H * hf:4 * H * (hf + 1)], T[xq + "c"][:, H * hf:H * hf + H].bitcast(dt.uint8), xq + "ab"[hf], "")
         if not final:
-            send_q(prv, xq, "n%d" % (r + 1), "an%d" % (r + 1), xq)
-    mm(2, C, ("v", 0), (xq, 0), True, True, "vq " + xq)
-    dma("Y", T.oc[:], T[xq + "c"][:].bitcast(dt.uint8), xq, "")
+            send_q(prv, xq, "n%d" % (r + 1), "an%d" % (r + 1), "%sa %sb" % (xq, xq))
+    sc(T.yb[:, 0:H], ps[0][:, 0:H], "ps0", "yb0")
+    cp(T.yb[:, H:C], ps[1][:, 0:H], "ps1", "yb1")
+    for hf in range(2):
+        dma("Y", T.y[:, H * hf:H * hf + H], T.yb[:, H * hf:H * hf + H], "yb%d" % hf, "")
     for k in range(4):
-        dma("S", T.osc[4 * k:4 * k + 4, :], T[xq + "s"][32 * k:32 * k + 4, :], xq, "")
-    cp(T.orow[:], ps[2][:, 0:C], "ps2", "orow")
-    dma("Y", T.y[:], T.orow[:], "orow", "")
+        dma("S", T.osc[4 * k:4 * k + 4, :], T[xq + "s"][32 * k:32 * k + 4, :], "%sa %sb" % (xq, xq), "")
     emit(g, T, ops)

@@ -5,17 +5,28 @@ A = AluOpType
 F = ActivationFunctionType
 C, NR, SW, NB = 320, 2, 12, 160
 BIG = 1.0e29
-CW, GW, SIG = 2.0 ** 13, 2.0 ** 16, 16.0
+CW, GW, GU, SIG = 2.0 ** 13, 2.0 ** 16, 2.0 ** 8, 16.0
 LN2 = math.log(2.0)
 X4, U8, BF, F32, I32, U16 = "float8_e4m3fn_x4", "uint8", "bfloat16", "float32", "int32", "uint16"
-WB, E0, K0, KN, MX, PG, PO, SS, MU, FA, MI, NT = 0, 1, 5, 9, 10, 12, 14, 16, 18, 19, 20, 21
+WB, E0, K0, KN, MX, SS, MU, FA, MI, NT = 0, 1, 5, 9, 10, 13, 15, 16, 17, 18
 SLOT = (0, 2, 1, 3)
 SOFF, SWID = [0, 320, 576, 768, 896], [320, 256, 192, 128, 128]
 DL, DU = ((15, 14, 13, 12), (11, 10, 9, 8), (7, 6, 5, 4), (3, 2, 1)), ((7, 6, 5, 4), (3, 2, 1))
-LOW, FEW = [18, 19], [4, 4]
-LB, UB, HB = (5, 6), (7, 0), ((0, 1, 4, 5), (6, 7, 2, 3))
+QUANT = [[0, 2, 0, 2], [0, 2, 1, 1], [1, 1]]
+POOL = ["cz1", "co1", "w20", "st0", "st1"]
+PICK = ["VVSS", "VVVV", "SSSV"]
+LOW, FEW = [18, 18], [4, 4]
+DIAG = [0, 1]
+PIECES, AEX, WHOLE, OLE = [(0, 10), (10, 20)], [1], [1, 1, 0, 0], ["S", "S"]
+LISTS = set("uoff ky al bl tl mu pl px xy ol ln lv lh".split())
+START, WAKE, PASSES = {"V": 5, "S": 110, "P": 30, "G": 10, "Y": 0, "A": 0}, [140, 180], 4
+BULK = [3000, 3000, 3000, 7000]
+PE = [0.5, 2.2, 2.2, 1500]
+SPLIT = [0]
+BEFORE = {}
+LB, UB, HB = 5, (6, 7), ((0, 1, 4, 5), (6, 7, 2, 3))
 
-SCRATCH, SUB = {}, {}
+SCRATCH, SUB, ORDER = {}, {}, []
 
 
 def _b(names, n, d):
@@ -31,38 +42,43 @@ def _q(names, n):
 
 def _s(buf, names, d):
     for i, s in enumerate(names.split()):
-        SUB[s] = (buf, 32 * i, {"uoff": 16, "al": 24, "bl": 24, "ky": 16, "tl": 2}.get(s, 20))
+        SUB[s] = (buf, 32 * i, {"uoff": 16, "al": 24, "bl": 24, "ky": 16, "tl": 2, "ends": 2}.get(s, 20))
     _b(buf, 32 * len(names.split()), d)
 
 
 _b("xt at zt xn vp vo vq gp go zp", 4 * C, BF)
 _b("ut vt wb", 512, BF)
-_b("kn", 520, BF)
-_b("zb", 1024, BF)
-_b("wt xs st", 4 * NB, BF)
+_b("kn zb", 520, BF)
+_b("w2", 832, BF)
+_b("xs st", 1024, BF)
+_b("vg", 4 * C, BF)
 _b("sg", 2064, BF)
+_b("ys dg", C, BF)
 _b("sot", 4096, BF)
 _b("cot", 5120, BF)
 _b("jk", 3400, BF)
-_b("m16 k16 k01 pen m10 k10 e10 ru e16 r16 r10 wp gq vg", C, BF)
-_b("iot mk mn ms tmp sb ls sa sq orow onr wrow wro2 yb", C, F32)
+_b("m16 k16 k01 pen k10 e10 ru e16 r16 r10 wp", C, BF)
+_b("iot mk mn sb ls sa sn sq orow onr wrow wro2", C, F32)
 _b("aex d0 dd", 384, F32)
 _b("wr r8 lr", 128, BF)
 _b("psr pir a1 a2 b1t b2t", 256, BF)
-_b("fa", 640, BF)
-_b("bs mt mt2", NB, F32)
+_b("fa", 512, BF)
+_b("fb", 768, BF)
+_b("mt mt2 bs", NB, F32)
+_b("ms mst m2 m2t", C, F32)
 _b("pi", 8, I32)
 _b("pf", 64, F32)
 _b("li", 96, I32)
 _b("kf", 128, F32)
 _s("sf", "rs pre cbs fx", F32)
 _s("si", "pli j32 j10", I32)
-_s("of", "uoff xy al bl ky tl mu", U16)
+_s("of", "uoff al bl ky tl mu xy", U16)
 _s("snd", "pl0 pl1 ol0 ol1 hl0 hl1", U16)
 _s("lnd", "lp0 lp1 ln0 ln1 lv0 lv1 lh0 lh1", U16)
 _q("lw", 512)
 _q("u v", 128)
-_q("wt w2 xs st s2", NB)
+_q("xs st s2", 256)
+_q("w2", 208)
 _q("up", 256)
 _q("x0 x1 x2 g0 g1 n0 n1 p0 p1 z", C)
 _q("c", 128 * NT)
@@ -72,6 +88,55 @@ for _i in range(8):
     SCRATCH["b%d" % _i] = ("psum", [128, 512], F32)
 SEMAPHORES = ["V", "S", "P", "G", "loc"] + ["d%d" % i for i in range(40)] + \
              [a + str(r) for r in range(NR) for a in ("an", "ap", "al", "ao", "av", "ah")]
+
+
+def arrange(ops, deps):
+    n = len(ops)
+    t = [o["t"] + START[o["e"]] for o in ops]
+
+    def after(j, i):
+        if ops[j]["e"] == ops[i]["e"] and (ops[j]["e"] == "P" or ops[j]["k"] == "r"):
+            return t[j]
+        return t[j] + ops[j].get("late", 0) + (0 if ops[j]["k"] == "r" else WAKE[ops[j]["e"] == ops[i]["e"]])
+
+    chain = [t[i] + ops[i].get("late", 0) for i in range(n)]
+    for i in range(n - 1, -1, -1):
+        for j in deps[i]:
+            chain[j] = max(chain[j], after(j, i) + ops[j].get("spare", 0) + chain[i])
+    users = [[] for _ in range(n)]
+    for i in range(n):
+        for j in deps[i]:
+            users[j].append(i)
+
+    def place(order, earliest):
+        start, held = [0.0] * n, {e: [] for e in START}
+        for i in order:
+            s, h = earliest(i, start), held[ops[i]["e"]]
+            k = len(h)
+            while k and h[k - 1][1] > s:
+                k -= 1
+            while k < len(h) and s + t[i] > h[k][0]:
+                s = max(s, h[k][1])
+                k += 1
+            start[i] = s
+            h.insert(k, (s, s + t[i]))
+        return start
+
+    def early(i, start):
+        return max([start[j] + after(j, i) for j in deps[i]], default=0.0)
+
+    def late(j, back):
+        return max([back[i] + t[i] - t[j] + after(j, i) + ops[j].get("spare", 0) for i in users[j]], default=ops[j].get("late", 0))
+
+    best, key = None, [-c for c in chain]
+    for _ in range(PASSES):
+        start = place(sorted(range(n), key=lambda i: (key[i], i)), early)
+        end = max(start[i] + t[i] + ops[i].get("late", 0) for i in range(n))
+        if best is None or end < best[0]:
+            best = (end, start)
+        back = place(sorted(range(n), key=lambda i: (-start[i], -i)), late)
+        key = [-back[i] - t[i] for i in range(n)]
+    return sorted(range(n), key=lambda i: (best[1][i], i))
 
 
 def emit(g, T, ops):
@@ -94,7 +159,13 @@ def emit(g, T, ops):
             lastw[k] = i
             readers[k] = []
         d.discard(i)
-        deps.append([j for j in d if ops[j]["k"] != "r" and not (o["e"] == "P" and ops[j]["e"] == "P")])
+        deps.append(d)
+    if not ORDER:
+        ORDER.extend(arrange(ops, deps))
+    order = ORDER
+    at = {j: i for i, j in enumerate(order)}
+    ops, deps = [ops[j] for j in order], [[at[k] for k in deps[j]] for j in order]
+    deps = [[j for j in d if ops[j]["k"] != "r" and not (o["e"] == "P" and ops[j]["e"] == "P")] for o, d in zip(ops, deps)]
     ev, cnt, nd, tot = [], {}, [0], {}
     for o in ops:
         if o["k"] == "c":
@@ -168,32 +239,41 @@ def rank_program(g, core, T, topo):
     nxt, prv = T.cores[(rank + 1) % n_ranks], T.cores[(rank - 1) % n_ranks]
     ops, bgq = [], []
 
-    def op(e, f, R, W, k="c", **kw):
-        ops.append(dict(e=e, f=f, R=R.split(), W=W.split(), k=k, **kw))
+    def op(e, f, R, W, t, k="c", **kw):
+        ops.append(dict(e=e, f=f, R=R.split(), W=W.split(), t=t, k=k, **kw))
+
+    def span(R, *aps, rate=1.0):
+        n = aps[0].shape[1]
+        if LISTS.intersection(a.rstrip("01") for a in R.split()):
+            return 60 + n * (PE[2] if "px" in R else PE[1])
+        if rate == 1.0 and all("bfloat16" in str(a.dtype) for a in aps):
+            rate = 0.5
+        return max(64, n * rate)
 
     def ts(out, in0, s1, s2, o0, o1, R, W):
         if s2 is None:
-            op("V", lambda q: q.tensor_scalar(out, in0, s1, None, o0), R, W)
+            op("V", lambda q: q.tensor_scalar(out, in0, s1, None, o0), R, W, span(R, out, in0))
         else:
-            op("V", lambda q: q.tensor_scalar(out, in0, s1, s2, o0, o1), R, W)
+            op("V", lambda q: q.tensor_scalar(out, in0, s1, s2, o0, o1), R, W, span(R, out, in0))
 
     def tt(out, a, b, o, R, W):
-        op("V", lambda q: q.tensor_tensor(out, a, b, o), R, W)
+        op("V", lambda q: q.tensor_tensor(out, a, b, o), R, W, span(R, out, rate=1.01 if "ps" in R else 2.0))
 
     def cp(out, a, R, W):
-        op("V", lambda q: q.tensor_copy(out, a), R, W)
+        op("V", lambda q: q.tensor_copy(out, a), R, W, span(R, a if "px" in R else out, rate=1.01))
 
     def ms(out, c, W):
-        op("V", lambda q: q.memset(out, c), "", W)
+        op("V", lambda q: q.memset(out, c), "", W, span("", out))
 
     def scan(out, d0, d1, init, o0, o1, R, W):
-        op("V", lambda q: q.tensor_tensor_scan(out, d0, d1, init, o0, o1), R, W)
+        op("V", lambda q: q.tensor_tensor_scan(out, d0, d1, init, o0, o1), R, W, span(R, out, d0, d1))
 
     def qz(name, a, b, src, R, W):
-        op("V", lambda q: q.quantize_mx(T[name + "c"][:, a:b], T[name + "s"][:, a:b], src), R, W)
+        op("V", lambda q: q.quantize_mx(T[name + "c"][:, a:b], T[name + "s"][:, a:b], src), R, W, 15 + 1.06 * (b - a))
 
     def act(out, a, func, R, W, **kw):
-        op("S", lambda q: q.activation(out, a, func, **kw), R, W)
+        load = 1600 if W == "xw01" and not any("wp0" in o["W"] for o in ops) else 0
+        op("S", lambda q: q.activation(out, a, func, **kw), R, W, span(R, out, rate=1.01) + load)
 
     def af(out, a, scale, bias, R, W):
         act(out, a, F.Identity, R, W, scale=scale, bias=bias)
@@ -211,38 +291,41 @@ def rank_program(g, core, T, topo):
     def mm(bank, n, lhs, rhs, start, stop, R):
         (ln, la), (rn, ra) = lhs, rhs
         op("P", lambda q: q.matmul_mx(T["b%d" % bank][:, 0:n], T[ln + "c"][:, la:la + 128], T[ln + "s"][:, la:la + 128],
-                                      T[rn + "c"][:, ra:ra + n], T[rn + "s"][:, ra:ra + n], start, stop), R, "ps%d" % bank)
+                                      T[rn + "c"][:, ra:ra + n], T[rn + "s"][:, ra:ra + n], start, stop), R, "ps%d" % bank,
+           PE[0] * (n + 16))
 
-    def dma(e, out, a, R, W):
-        op(e, lambda q: q.dma_start(out, a), R, W, k="d")
+    def dma(e, out, a, R, W, late=2400):
+        op(e, lambda q: q.dma_start(out, a), R, W, 70, k="d", late=late)
 
     def iota(out, pat, base, cm, W, small=True):
         if small:
-            op("G", lambda q: q.iota(out, pat, base, cm, allow_small_or_imprecise_dtypes=True), "", W)
+            op("G", lambda q: q.iota(out, pat, base, cm, allow_small_or_imprecise_dtypes=True), "", W, 160 + 2 * out.shape[1])
         else:
-            op("G", lambda q: q.iota(out, pat, base, cm), "", W)
+            op("G", lambda q: q.iota(out, pat, base, cm), "", W, 160 + 2 * out.shape[1])
 
     def sel(out, a, pat, o, fill, base, cm, R, W):
-        op("G", lambda q: q.affine_select(out, a, pat, o, fill, base, cm), R, W)
+        op("G", lambda q: q.affine_select(out, a, pat, o, fill, base, cm), R, W, 200 + 2 * out.shape[1])
 
-    def send(dst, out, a, sem, R):
+    def send(dst, out, a, sem, R, late=0, t=300, spare=0):
+        late = late or PE[3]
         rid, pid, _ = topo.addr(dst)
         m = topo.mask(core, dst)
-        op("G", lambda q: q.remote_dma(out, a, T.sem[sem], T.sem.loc, pid, rid, m), R, "", k="r", n=len(topo.engines(core, dst)))
+        op("G", lambda q: q.remote_dma(out, a, T.sem[sem], T.sem.loc, pid, rid, m), R, "#" + sem, t, k="r", late=late, spare=spare,
+           n=len(topo.engines(core, dst)))
 
-    def send_q(dst, src, land, sem, R):
-        send(dst, T[land + "c"][:].bitcast(dt.uint8), T[src + "c"][:].bitcast(dt.uint8), sem, R)
-        send(dst, T[land + "s"][:], T[src + "s"][:], sem, R)
+    def send_q(dst, src, land, sem, R, t=300):
+        send(dst, T[land + "c"][:].bitcast(dt.uint8), T[src + "c"][:].bitcast(dt.uint8), sem, R, 4400, t)
+        send(dst, T[land + "s"][:], T[src + "s"][:], sem, R, BULK[3], 300, BULK[src[0] == "g"])
 
     def arrive(src, sem, calls, W):
-        op("G", None, "", W, k="a", sem=sem, n=calls * len(topo.engines(src, core)))
+        op("A", None, "#" + sem, W, 0, k="a", sem=sem, n=calls * len(topo.engines(src, core)))
 
     def bg(n=1):
         for _ in range(min(n, len(bgq))):
             bgq.pop(0)()
 
     def L(f, *a, **kw):
-        bgq.append(lambda: f(*a, **kw))
+        f(*a, **kw)
 
     def sub(name, a=0, b=None):
         buf, o, n = SUB[name]
@@ -253,6 +336,9 @@ def rank_program(g, core, T, topo):
 
     def sg(i, t, n=128):
         return T.sg[:, 512 * i + t:512 * i + 4 * n:4]
+
+    def staged(i, slots):
+        return " ".join("sg%d%d" % (i, t) for t in slots)
 
     def qc(i, j, n, R, W):
         qz("c", 128 * i, 128 * (i + n), T.sg[:, 512 * j:512 * (j + n)], R, W)
@@ -267,9 +353,10 @@ def rank_program(g, core, T, topo):
     pi, pf, li, kf = T.pi, T.pf, T.li, T.kf
     SH, AND, EQ, MUL, ADD = A.logical_shift_right, A.bitwise_and, A.is_equal, A.mult, A.add
     H = C // 2
+    chains, nq, nv = ((0, 1), 128, 80) if SPLIT[0] else ((0,), NB, NB)
 
     names = ("p g l8 p3 p1 q s hb s4 s2 c1 c2 c3 lB sB iA iB z nz nnz co s16 vl vu alo blo alu blu tl t0 t1 t2 cb o0 fx "
-             "bw bx u0 u1 u2 u3 th fl fu fs").split()
+             "t3 t4 t5 t6 t7 bw bx l15 u0 u1 u2 u3 th fl fu fs").split()
 
     def pc(name, n=1):
         i = names.index(name)
@@ -282,7 +369,7 @@ def rank_program(g, core, T, topo):
         else:
             ts(pc(name), pc(src), float(k), a, MUL, ADD, R, "_" + name)
 
-    dma("Y", T.xt[:], T.x[:], "", "xt")
+    dma("Y", T.xt[:], T.x[:], "", "xt", 4500)
     dma("S", T.ut[:], T.u[:], "", "ut")
     iota(pi[:, 0:1], [[0, 1]], 0, 1, "pi0", False)
     iota(T.r16[:], [[0, 20], [1, 16]], 0, 0, "r16")
@@ -292,7 +379,6 @@ def rank_program(g, core, T, topo):
     ms(T.zb[:], 0.0, "zb")
     for c, s, m in ((1, 4, 7), (2, 3, 15), (3, 0, 3), (4, 0, 1), (5, 0, 15)):
         ts(pi[:, c:c + 1], pi[:, 0:1], s, m, SH, AND, "pi0", "pi%d" % c)
-    qz("co", 0, 128, T.zb[:, 0:512], "zb", "coz")
     cp(pc("p", 6), pi[:, 0:6], "pi0 pi1 pi2 pi3 pi4 pi5", "_p _g _l8 _p3 _p1 _q")
     for u in range(4):
         zero(T.sot, 4 * (SOFF[u] + SWID[u] - 48), 4 * (SOFF[u] + SWID[u]), "sz%d" % u)
@@ -307,7 +393,7 @@ def rank_program(g, core, T, topo):
     af(T.pen[:], T.e16[:], -1049600.0, 1024.0, "e16", "pen")
     qz("c", 128 * WB, 128 * E0, T.wb[:], "wb0 wb1 wb2 wb3", "qWB")
     for n, s, k, a in (("s", "l8", -8, "p"), ("hb", "g", -2, "l8"), ("s2", "p1", -1, "p3"), ("cb", "q", 1023, 15 - 15360),
-                       ("fx", "q", 1, -4.5), ("o0", "q", 1024, -15360), ("s4", "p3", -1, "s"), ("alo", "hb", 10, 9),
+                       ("o0", "q", 1024, -15360), ("s4", "p3", -1, "s"), ("alo", "hb", 10, 9),
                        ("blo", "s", 10, 9), ("t0", "hb", 160, 9), ("c1", "s2", -2, 2), ("t1", "s", -30, 249)):
         lin(n, s, k, a, "V")
     qz("u", 0, 128, T.ut[:], "ut", "uq")
@@ -315,8 +401,9 @@ def rank_program(g, core, T, topo):
         lin(n, s, k, a, "V")
     pick("up", 0, "u", 0, 128, sub("uoff", 0, 8), 128, "uq uoff", "up0")
     pick("up", 128, "u", 0, 128, sub("uoff", 8, 16), 128, "uq uoff", "up1")
-    for n, s, k, a in (("alu", "s4", 20, "t0"), ("blu", "s", 10, "t0"), ("c2", "s4", -2, 4), ("lB", "s4", 2, "g"),
-                       ("c3", "hb", -16, "t1"), ("vl", "hb", 16, "t2"), ("vu", "s4", 32, "t2"), ("iB", "lB", 16, "sB")):
+    for n, s, k, a in (("c2", "s4", -2, 4), ("c3", "hb", -16, "t1"), ("vl", "hb", 16, "t2"), ("vu", "s4", 32, "t2")):
+        lin(n, s, k, a, "V")
+    for n, s, k, a in (("alu", "s4", 20, "t0"), ("blu", "s", 10, "t0"), ("lB", "s4", 2, "g"), ("iB", "lB", 16, "sB")):
         lin(n, s, k, a, "S")
     iota(li[:, 52:60], [[0, 4], [1, 2]], 0, 0, "li3", False)
     iota(li[:, 60:68], [[0, 2], [1, 2], [0, 2]], 0, 0, "li4", False)
@@ -324,112 +411,101 @@ def rank_program(g, core, T, topo):
     iota(li[:, 76:84], [[1, 4], [0, 2]], 0, 0, "li6", False)
     iota(li[:, 36:52], [[160, 2], [0, 8]], 0, 0, "li2", False)
     iota(T.r10[:], [[0, 32], [1, 10]], 0, 0, "r10")
+    ts(kf[:, 0:16], li[:, 52:68], pc("p1"), pc("c1"), EQ, MUL, "li3 li4 _p1 _c1", "k0")
+    ts(kf[:, 40:48], li[:, 76:84], pc("p3"), 8.0, A.not_equal, MUL, "li6 _p3", "k3")
+    ts(pc("z"), pc("g"), pc("s"), None, EQ, None, "_g _s", "_z")
+    ts(kf[:, 16:32], li[:, 68:84], pc("p3"), pc("c2"), EQ, MUL, "li5 li6 _p3 _c2", "k1")
+    ts(kf[:, 32:40], li[:, 16:24], pc("s16"), pc("c3"), EQ, MUL, "li1 _s16 _c3", "k2")
+    ts(kf[:, 48:56], li[:, 16:24], 2.0, pc("vl"), MUL, ADD, "li1 _vl", "k4")
+    ts(kf[:, 56:64], li[:, 16:24], pc("vu"), None, ADD, None, "li1 _vu", "k5")
     for b in range(4):
         if b == 1:
             qz("x0", 0, C, T.xt[:], "xt", "x0a x0b")
-            send_q(prv, "x0", "n0", "an0", "x0a x0b")
-        sel(T.sg[:, 512 * b:512 * b + 512], T.zb[:, 0:512], [[4, 128], [1, 4]], A.not_equal, 32.0, -SLOT[b], -4, "zb", "sg%d" % b)
+            send_q(prv, "x0", "n0", "an0", "x0a x0b", 2700)
+        sel(T.sg[:, 512 * b:512 * b + 512], T.zb[:, 0:512], [[4, 128], [1, 4]], A.not_equal, 32.0, -SLOT[b], -4, "zb", staged(b, range(4)))
+    iota(T.iot[:], [[1, C]], 0, 0, "iot")
+    qz("co", 0, 128, T.zb[:, 0:512], "zb", "coz")
     for a in (640, 1280):
         dma("Y", T.coc[:, a:a + 128].bitcast(dt.uint8), T.coc[:, 0:128].bitcast(dt.uint8), "coz xt", "cy%dc" % a)
-        dma("Y", T.cos[:, a:a + 128], T.cos[:, 0:128], "coz", "cy%ds" % a)
-    for i in range(5):
-        tiles = ["%d%d" % (i // 2, 2 * (i % 2) + j) for j in range(2)]
-        dma("Y", T.cot[:, 1024 * i:1024 * i + 1024], T.zb[:], "zb", " ".join("cz%s co%s3" % (a, a) for a in tiles))
-    for a in ("wt", "xs", "st"):
-        dma("Y", T[a][:], T.zb[:, 0:4 * NB], "zb", " ".join(a + t for t in ("0", "00", "01", "1", "2", "3")))
-    iota(T.iot[:], [[1, C]], 0, 0, "iot")
+        dma("Y", T.cos[:, a:a + 128], T.cos[:, 0:128], "coz xt", "cy%ds" % a)
+    ms(sub("rs", 0, 1), 0.0, "rs0")
+    lin("fx", "q", 1, -4.5, "V")
+    ts(sub("fx"), li[:, 16:36], pc("fx"), 0.1, ADD, MUL, "li1 _fx", "fx")
+    ts(sub("j32"), li[:, 16:36], pc("q"), 32.0, ADD, MUL, "li1 _q", "j32")
+    cp(sub("j10"), sub("fx"), "fx", "j10")
+    ts(sub("j10"), sub("j10"), -319.0, None, MUL, None, "j10", "j10")
+    tt(sub("j32"), sub("j32"), sub("j10"), ADD, "j32 j10", "j32")
+    cp(sub("xy"), sub("j32"), "j32", "xy")
 
     L(ts, sub("cbs"), li[:, 16:36], pc("cb"), None, ADD, None, "li1 _cb", "cbs")
-    L(ms, sub("rs", 0, 1), 0.0, "rs0")
-    L(ts, sub("fx"), li[:, 16:36], pc("fx"), 0.1, ADD, MUL, "li1 _fx", "fx")
-    L(ts, sub("j32"), li[:, 16:36], pc("q"), 32.0, ADD, MUL, "li1 _q", "j32")
-    L(cp, sub("j10"), sub("fx"), "fx", "j10")
     L(ts, sub("al", 0, 16), li[:, 16:32], 1.25, pc("alo"), MUL, ADD, "li1 _alo", "al0")
-    L(ts, sub("j10"), sub("j10"), -319.0, None, MUL, None, "j10", "j10")
     L(ts, sub("al", 16, 24), li[:, 16:24], 0.625, pc("alu"), MUL, ADD, "li1 _alu", "al1")
-    L(tt, sub("j32"), sub("j32"), sub("j10"), ADD, "j32 j10", "j32")
     L(ts, T.e10[:], T.r10[:], pc("q"), None, EQ, None, "r10 _q", "e10")
-    L(cp, sub("xy"), sub("j32"), "j32", "xy")
     L(ts, T.k10[:], T.r10[:], 0.5, None, A.is_gt, None, "r10", "k10")
     L(ts, sub("bl", 0, 16), li[:, 36:52], pc("blo"), None, ADD, None, "li2 _blo", "bl0")
     L(ts, sub("bl", 16, 24), li[:, 36:44], pc("blu"), 80.0, ADD, ADD, "li2 _blu", "bl1")
 
-    def consts_keys():
-        ts(kf[:, 0:16], li[:, 52:68], pc("p1"), pc("c1"), EQ, MUL, "li3 li4 _p1 _c1", "k0")
-        ts(kf[:, 16:32], li[:, 68:84], pc("p3"), pc("c2"), EQ, MUL, "li5 li6 _p3 _c2", "k1")
-        ts(kf[:, 32:40], li[:, 16:24], pc("s16"), pc("c3"), EQ, MUL, "li1 _s16 _c3", "k2")
-        ts(kf[:, 40:48], li[:, 76:84], pc("p3"), 8.0, A.not_equal, MUL, "li6 _p3", "k3")
-        ts(kf[:, 48:56], li[:, 16:24], 2.0, pc("vl"), MUL, ADD, "li1 _vl", "k4")
-        ts(kf[:, 56:64], li[:, 16:24], pc("vu"), None, ADD, None, "li1 _vu", "k5")
-        tt(kf[:, 64:96], kf[:, 0:32], kf[:, 32:64], ADD, "k0 k1 k2 k3 k4 k5", "k6")
-        ts(pc("z"), pc("g"), pc("s"), None, EQ, None, "_g _s", "_z")
-        tt(kf[:, 96:112], kf[:, 64:80], kf[:, 80:96], ADD, "k6", "k7")
+    L(tt, kf[:, 64:96], kf[:, 0:32], kf[:, 32:64], ADD, "k0 k1 k2 k3 k4 k5", "k6")
+    L(lin, "nz", "z", -1, 1, "V")
+    L(tt, kf[:, 96:112], kf[:, 64:80], kf[:, 80:96], ADD, "k6", "k7")
+    L(lin, "nnz", "z", 1, -1, "V")
+    L(ts, sub("ky"), kf[:, 96:112], 1.0, None, ADD, None, "k7", "ky")
+    L(lin, "co", "z", -1 / GW, -1 / GW, "V")
 
     def consts_rows():
-        ts(sub("ky"), kf[:, 96:112], 1.0, None, ADD, None, "k7", "ky")
-        lin("nz", "z", -1, 1)
-        lin("nnz", "z", 1, -1)
-        lin("co", "z", -1 / GW, -1.5 / GW)
         sc(T.psr[:], T.r16[:].indirect(sub("ky")), "r16 ky", "psr")
         sc(T.pir[:], T.iot[:].indirect(sub("ky")), "iot ky", "pir")
 
     def consts_court():
-        L(qc, K0, 0, 4, "sg0 sg1 sg2 sg3", "qK")
-        L(qz, "c", 128 * KN, 128 * MX, T.kn[:, 0:512], "kn", "qKN")
-        L(ts, T.a1[:], T.psr[:], pc("s"), CW, EQ, MUL, "psr _s", "a1")
-        L(ts, T.a2[:], T.pir[:], pc("iA"), CW * GW, EQ, MUL, "pir _iA", "a2")
-        L(ms, sg(2, 1), 0.0, "sg2")
-        L(ms, sg(3, 3), 0.0, "sg3")
-        L(af, T.b1t[:], T.a1[:], pc("z"), 0.0, "a1 _z", "b1t")
-        L(af, T.b2t[:], T.a2[:], pc("co"), 0.0, "a2 _co", "b2t")
-        L(af, sg(2, 0, 256), T.a2[:], pc("nnz"), 0.0, "a2 _nnz", "sg2 sg3")
-        L(tt, T.fa[:, 0:256], T.a1[:], T.a2[:], ADD, "a1 a2", "fa0")
-        L(af, sg(0, 0, 256), T.fa[:, 0:256], pc("nz"), 0.0, "fa0 _nz", "sg0 sg1")
-        L(ts, T.fa[:, 256:384], T.psr[:, 128:256], pc("sB"), CW, EQ, MUL, "psr _sB", "fa1")
-        L(ts, T.fa[:, 384:512], T.pir[:, 128:256], pc("iB"), CW * GW, EQ, MUL, "pir _iB", "fa2")
-        L(af, sg(3, 2), T.fa[:, 384:512], -1.0, 0.0, "fa2", "sg3")
-        L(tt, sg(1, 2), T.fa[:, 256:384], T.fa[:, 384:512], ADD, "fa1 fa2", "sg1")
-        L(qc, PG, 2, 2, "sg2 sg3", "qPG")
-        L(qc, MX, 0, 2, "sg0 sg1", "qMX")
-        L(af, sg(3, 2), T.fa[:, 384:512], -1.5 / GW, 0.0, "fa2", "sg3")
-        L(tt, sg(2, 0, 256), T.b1t[:], T.b2t[:], ADD, "b1t b2t", "sg2 sg3")
-        L(qc, PO, 2, 2, "sg2 sg3", "qPO")
+        ts(T.a1[:], T.psr[:], pc("s"), CW, EQ, MUL, "psr _s", "a1")
+        ts(T.a2[:], T.pir[:], pc("iA"), CW * GW, EQ, MUL, "pir _iA", "a2")
+        tt(T.fa[:, 0:256], T.a1[:], T.a2[:], ADD, "a1 a2", "fa0")
+        af(T.b1t[:], T.a1[:], pc("z"), 0.0, "a1 _z", "b1t")
+        af(T.b2t[:], T.a2[:], pc("co"), 0.0, "a2 _co", "b2t")
+        af(sg(0, 1, 256), T.a2[:], pc("nnz"), 0.0, "a2 _nnz qE", "sg01 sg11")
+        af(sg(0, 0, 256), T.fa[:, 0:256], pc("nz"), 0.0, "fa0 _nz qE", "sg00 sg10")
+        tt(sg(0, 3, 256), T.b1t[:], T.b2t[:], ADD, "b1t b2t qE", "sg03 sg13")
+        ts(T.fa[:, 256:384], T.psr[:, 128:256], pc("sB"), CW, EQ, MUL, "psr _sB", "fa1")
+        ts(T.fa[:, 384:512], T.pir[:, 128:256], pc("iB"), CW * GU, EQ, MUL, "pir _iB", "fa2")
+        tt(sg(1, 2), T.fa[:, 256:384], T.fa[:, 384:512], A.max, "fa1 fa2 qE", "sg12")
+        ts(sg(2, 0), T.pir[:, 128:256], pc("iB"), -CW * GU, EQ, MUL, "pir _iB qE", "sg20")
+        ts(sg(2, 1), T.pir[:, 128:256], pc("iB"), -CW, EQ, MUL, "pir _iB qE", "sg21")
+        qc(MX, 0, 1, staged(0, range(4)), "qMX")
+        qc(MX + 1, 1, 2, staged(1, range(4)) + " " + staged(2, range(4)), "qMU_")
 
     def consts_weights():
-        for n, s, k, a in (("bw", "l8", LN2, 0), ("bx", "l8", LN2, -math.log(SIG)), ("t0", "g", LN2, 8 * LN2),
-                           ("t1", "g", LN2, 8 * LN2 - 200), ("u0", "hb", -200, "t0"), ("u1", "hb", 200, "t1"),
+        for n, s, k, a in (("bw", "l8", LN2, 0), ("bx", "l8", LN2, -math.log(SIG)), ("t6", "g", LN2, 8 * LN2),
+                           ("t7", "g", LN2, 8 * LN2 - 200), ("u0", "hb", -200, "t6"), ("u1", "hb", 200, "t7"),
                            ("u2", "u0", 1, -math.log(SIG)), ("u3", "u1", 1, -math.log(SIG))):
-            lin(n, s, k, a)
-
-    def consts_tail_numbers():
-        for n, s, k, a in (("fl", "l8", -3, 1), ("fu", "lB", -3, 1), ("fs", "s", -2, 2), ("t0", "s", 4, 0), ("t1", "q", 0.5, 0),
-                           ("th", "l8", -4, "t0"), ("t2", "g", 10, "t1"), ("tl", "p1", 79.5, "t2")):
-            lin(n, s, k, a)
-
-    def consts_tail_scalar():
-        for j, (row, k, b) in enumerate(((T.lr, 3.0, "fl"), (T.lr, 3.0, "fu"), (T.r8, 2.0, "fs"))):
-            act(T.fa[:, 512:640], row[:], F.Relu, "lr r8 _" + b, "fa3", scale=k, bias=pc(b))
-            act(T.fa[:, 128 * j:128 * j + 128], T.fa[:, 512:640], F.Relu, "fa3", "fa0 fa1", scale=-1.0, bias=4.0)
-        af(sg(1, 0), T.fa[:, 0:128], 1.0, -4.0, "fa0", "sg1")
+            lin(n, s, k, a, "V")
 
     def consts_tail():
-        L(ms, sg(3, 0), 0.0, "sg3")
-        L(ts, sg(2, 0), T.r8[:], pc("s"), 0.5, EQ, MUL, "r8 _s", "sg2")
-        L(ts, sg(3, 2), T.r8[:], pc("s"), 0.5, EQ, MUL, "r8 _s", "sg3")
+        for n, s, k, a in (("fl", "l8", -3, 1), ("fu", "lB", -3, 1), ("fs", "s", -2, 2), ("t3", "s", 4, 0), ("t4", "q", 0.5, 0),
+                           ("th", "l8", -4, "t3"), ("t5", "g", 10, "t4"), ("tl", "p1", 79.5, "t5")):
+            lin(n, s, k, a, "V")
+        for j, (row, k, b) in enumerate(((T.lr, 3.0, "fl"), (T.lr, 3.0, "fu"), (T.r8, 2.0, "fs"))):
+            act(T.fb[:, 128 * j:128 * j + 128], row[:], F.Relu, "lr r8 _" + b, "fb%d" % j, scale=k, bias=pc(b))
+            act(T.fb[:, 384 + 128 * j:512 + 128 * j], T.fb[:, 128 * j:128 * j + 128], F.Relu, "fb%d" % j, "fc%d" % j, scale=-1.0, bias=4.0)
+        for i, t in ((3, 3), (2, 0), (2, 1), (0, 3), (1, 1), (1, 3)):
+            ms(sg(i, t), 0.0, "sg%d%d" % (i, t))
+        ts(sg(3, 0), T.r8[:], pc("s"), 0.5 / SIG, EQ, MUL, "r8 _s qE", "sg30")
+        ts(sg(2, 2), T.r8[:], pc("s"), 0.5 / SIG, EQ, MUL, "r8 _s", "sg22")
+        qc(SS, 2, 2, staged(2, range(4)) + " " + staged(3, range(4)), "qSS")
+        af(sg(1, 0), T.fb[:, 384:512], 1.0, -4.0, "fc0", "sg10")
+        tt(sg(1, 2), T.fb[:, 512:640], T.fb[:, 640:768], A.subtract, "fc1 fc2", "sg12")
         for t, (a, b) in enumerate((("l8", "s"), ("l8", "sB"), ("lB", "sB"))):
-            L(ts, sg(0, t), T.r16[:, 0:128], pc(a), pc(b), EQ, MUL, "r16 _%s _%s" % (a, b), "sg0")
-        L(qc, SS, 2, 2, "sg2 sg3", "qSS")
-        L(tt, sg(1, 2), T.fa[:, 128:256], T.fa[:, 256:384], A.subtract, "fa0 fa1", "sg1")
+            ts(sg(0, t), T.r16[:, 0:128], pc(a), pc(b), EQ, MUL, "r16 _%s _%s" % (a, b), "sg0%d" % t)
+        qc(MU, 0, 2, staged(0, range(4)) + " " + staged(1, range(4)), "qMU")
         for t, (a, b) in enumerate((("s", "l8"), ("sB", "l8"), ("sB", "lB"))):
-            L(ts, sg(2, t), T.r16[:, 0:128], pc(a), pc(b), EQ, MUL, "r16 _%s _%s" % (a, b), "sg2")
-        L(qc, MU, 0, 2, "sg0 sg1", "qMU")
-        L(ts, kf[:, 112:114], li[:, 16:18], 0.5, pc("tl"), MUL, ADD, "li1 _tl", "k8")
-        L(qc, MI, 2, 1, "sg2", "qMI")
-        L(ts, sub("tl"), kf[:, 112:114], NB - 1.0, None, A.min, None, "k8", "tl")
+            ts(sg(2, t), T.r16[:, 0:128], pc(a), pc(b), EQ, MUL, "r16 _%s _%s" % (a, b), "sg2%d" % t)
+        qc(MI, 2, 1, staged(2, range(4)), "qMI")
+        ts(kf[:, 112:114], li[:, 16:18], 0.5, pc("tl"), MUL, ADD, "li1 _tl", "k8")
+        ts(sub("tl"), kf[:, 112:114], NB - 1.0, None, A.min, None, "k8", "tl")
 
-    def pick32(src, skey, dst, dkey):
-        tt(T.tmp[:], src[:].indirect(sub("xy")), T.e10[:], MUL, skey + " xy e10", "tmp")
-        scan(dst[:], T.k10[:], T.tmp[:], 0.0, MUL, ADD, "k10 tmp", dkey)
+    def pick32(src, place, skey, mid, dst, dkey):
+        cp(T[mid][:].indirect(place), src[:], skey + " px", mid)
+        tt(T[mid + "t"][:], T[mid][:].indirect(sub("xy")), T.e10[:], MUL, mid + " xy e10", mid + "t")
+        scan(dst[:], T.k10[:], T[mid + "t"][:], 0.0, MUL, ADD, "k10 %st" % mid, dkey)
 
     def et(b):
         return ct(E0 + SLOT.index(b))
@@ -445,41 +521,49 @@ def rank_program(g, core, T, topo):
     def shifts(h):
         return (DL, 8) if h < 2 else (DU, 16)
 
-    def compare(h, u, t):
+    def wins(h, bank):
         D, w = shifts(h)
-        d, a = D[u][t], 2048 * h + 512 * u
-        n = 128 - w * d
-        tt(T.cot[:, a + t:a + 4 * n:4], T.dd[:, 128 * h:128 * h + n], T.dd[:, 128 * h + w * d:128 * h + 128], A.is_le,
-           "dd%d cz%d%d" % (h, h, u), "co%d%d%d" % (h, u, t))
+        for u, ds in enumerate(D):
+            a, c = 2048 * h + 512 * u, 128 + 640 * h
+            for t, d in enumerate(ds):
+                n = 128 - w * d
+                tt(T.cot[:, a + t:a + 4 * n:4], T.dd[:, 128 * h:128 * h + n], T.dd[:, 128 * h + w * d:128 * h + 128], A.is_le,
+                   "dd%d cz%d%d" % (h, h, u) + (" cq%d%d" % BEFORE[h, u] if (h, u) in BEFORE else ""), "co%d%d%d" % (h, u, t))
+            n = QUANT[h][u]
+            if n:
+                qz("co", c + 128 * (u + 1 - n), c + 128 * (u + 1), T.cot[:, a + 512 - 512 * n:a + 512],
+                   " ".join("co%d%d%d" % (h, v, t) for v in range(u + 1 - n, u + 1) for t in range(4)),
+                   " ".join("cq%d%d" % (h, v) for v in range(u + 1 - n, u + 1)))
+            for v in range(u + 1 - n, u + 1):
+                before = "cq%d%d" % (h, v - 1) if v else ("coz", "cy640c cy640s", "cy1280c cy1280s")[h]
+                mm(bank, 128, ("co", c + 128 * v), ct(KN), v == 0, False, "cq%d%d qKN" % (h, v))
+                for t, d in enumerate(D[v]):
+                    mm(bank, 128, ("co", c + 128 * v - w * d), ct(K0 + SLOT.index(t)), False,
+                       v == len(D) - 1 and t == len(D[v]) - 1, "cq%d%d qK %s" % (h, v, before))
 
-    def quant_co(h, u, n):
-        a, b = 128 + 640 * h + 128 * u, 2048 * h + 512 * u
-        qz("co", a, a + 128 * n, T.cot[:, b:b + 512 * n], " ".join("co%d%d%d" % (h, v, t) for v in range(u, u + n) for t in range(4)),
-           " ".join("cq%d%d" % (h, v) for v in range(u, u + n)))
+    def clear(buf, a, b, W, step=1):
+        if W[:3] in POOL:
+            iota(buf[:, a:b:step], [[0, (b - a + step - 1) // step]], 0, 0, W)
+        else:
+            ms(buf[:, a:b:step], 0.0, W)
 
-    def rank_mm(h, u, bank):
+    def clear_co(h):
         D, w = shifts(h)
-        a = 128 + 640 * h + 128 * u
-        before = "cq%d%d" % (h, u - 1) if u else ("coz", "cy640c cy640s", "cy1280c cy1280s")[h]
-        mm(bank, 128, ("co", a), ct(KN), u == 0, False, "cq%d%d qKN" % (h, u))
-        for t, d in enumerate(D[u]):
-            mm(bank, 128, ("co", a - w * d), ct(K0 + SLOT.index(t)), False, u == len(D) - 1 and t == len(D[u]) - 1,
-               "cq%d%d qK %s" % (h, u, before))
+        for u, ds in enumerate(D):
+            a = 2048 * h + 512 * u
+            clear(T.cot, a + 4 * (128 - w * ds[0]), a + 512, "cz%d%d" % (h, u))
+            if len(ds) < 4:
+                clear(T.cot, a + 3, a + 4 * (128 - w * ds[0]), "co%d%d3" % (h, u), 4)
 
     def weigh(out, bank, bias, W):
-        act(out, ps[bank][:, 0:NB // 2], F.Exp, "ps%d _%s" % (bank, bias), W, scale=-LN2 / 32, bias=pc(bias))
+        act(out, ps[bank][:, 0:NB // 2], F.Exp, "ps%d _%s" % (bank, bias), W, scale=-LN2, bias=pc(bias))
 
-    def preload(k):
-        mm(LB[k % 2], NB, ct(PG), ("wt", 0), True, False, "qPG wtq")
-        mm(LB[k % 2], NB, ct(PO), ("wt", 0), False, k == 0, "qPO wtq")
-        if k >= 7:
-            mm(UB[k % 2], NB, ct(PG + 1), ("w2", 0), True, False, "qPG w2q")
-            mm(UB[k % 2], NB, ct(PO + 1), ("w2", 0), False, False, "qPO w2q")
-
-    def places(tile, bank, mid, out, okey):
-        mm(bank, NB, ct(tile), ("s2", 0), True, True, "qMU qMI s2q")
-        tt(T[mid][:], ps[bank][:, 0:NB], T.bs[:], ADD, "ps%d bs" % bank, mid)
-        cp(out, T[mid][:].indirect(sub("tl")), mid + " tl", okey)
+    def places(tile, banks, mid, out, okey):
+        for h in chains:
+            bank = banks[h]
+            mm(bank, nq, ct(tile), ("s2", 128 * h), True, True, "qMU qMI s2q%d" % h)
+            tt(T[mid][:, 80 * h:80 * h + nv], ps[bank][:, 0:nv], T.bs[:, 80 * h:80 * h + nv], ADD, "ps%d bs" % bank, mid + "xy"[h])
+        cp(out, T[mid][:].indirect(sub("tl")), "%sx %sy tl" % (mid, mid), okey)
 
     for r in range(NR):
         s = str(r)
@@ -505,190 +589,176 @@ def rank_program(g, core, T, topo):
                 i = 20 - 4 * u - t
                 view, key, jk = so_view(i)
                 if i == 20:
-                    tt(view, T.sb[:], ps[0][:, 0:C], A.is_ge, "sb ps0 sz0", key)
-                elif i < low:
+                    tt(T.dg[:], T.sb[:], ps[0][:, 0:C], A.is_ge, "sb ps0", "dg")
+                    (cp if DIAG[0] else sc)(view, T.dg[:], "dg sz0", key)
+                elif i < low and DIAG[1]:
                     ts(view, ps[0][:, 0:16 * i], T.sb[:, 16 * i + 15:16 * i + 16], None, A.is_lt, None, "sb ps0 sz%d" % u, key)
                     if i > few:
                         act(jk, view, F.Copy, key, "rs%d jk%d" % (i, i), accum_out=sub("rs", i, i + 1))
-                    bg(1)
-            for i in range(min(few, 20 - 4 * u), max(0, 16 - 4 * u), -1):
-                view, key, jk = so_view(i)
-                op("V", lambda q, i=i, view=view: q.tensor_reduce(sub("rs", i, i + 1), view, AxisListType.X, ADD), key, "rs%d" % i)
+                    else:
+                        op("V", lambda q, i=i, view=view: q.tensor_reduce(sub("rs", i, i + 1), view, AxisListType.X, ADD), key,
+                           "rs%d" % i, max(64, 16 * i))
+                elif i < low:
+                    ts(jk, ps[0][:, 0:16 * i], T.sb[:, 16 * i + 15:16 * i + 16], None, A.is_lt, None, "sb ps0", "jk%d" % i)
+                    if i > few:
+                        act(view, jk, F.Copy, "jk%d sz%d" % (i, u), key + " rs%d" % i, accum_out=sub("rs", i, i + 1))
+                    else:
+                        ts(view, ps[0][:, 0:16 * i], T.sb[:, 16 * i + 15:16 * i + 16], None, A.is_lt, None, "sb ps0 sz%d" % u, key)
+                        op("V", lambda q, i=i, jk=jk: q.tensor_reduce(sub("rs", i, i + 1), jk, AxisListType.X, ADD), "jk%d" % i,
+                           "rs%d" % i, max(64, 16 * i))
             if u == 0:
-                scan(T.ru[:], T.k01[:], T.sot[:, 0:4 * C:4], 0.0, MUL, ADD, "k01 so00", "ru")
+                scan(T.ru[:], T.k01[:], T.dg[:], 0.0, MUL, ADD, "k01 dg", "ru")
             if u == 1:
-                tt(sub("pre"), sub("cbs"), T.ru[:, 15:C:16], A.subtract, "cbs ru", "pre")
+                tt(sub("pre"), T.ru[:, 15:C:16], sub("cbs"), A.subtract, "cbs ru", "pre")
             for v in after.get(u, []):
                 qz("so", SOFF[v], SOFF[v] + SWID[v], T.sot[:, 4 * SOFF[v]:4 * (SOFF[v] + SWID[v])],
                    " ".join("so%d%d" % (v, t) for t in range(4)), "soq%d" % v)
                 mm(2, SWID[v], ct(WB), ("so", SOFF[v]), v == 0, v == 4, "qWB soq%d" % v)
-        tt(sub("pre"), sub("pre"), sub("rs"), A.subtract, "pre " + " ".join("rs%d" % i for i in range(20)), "pre")
-        sc(T.mk[:], ps[1][:, 0:C], "ps1", "mk")
-        scan(T.ls[:], T.pen[:], ps[2][:, 0:C], 0.0, ADD, A.max, "pen ps2", "ls")
-        tt(sub("pli"), T.ls[:, 15:C:16], sub("pre"), ADD, "ls pre", "pli")
-        cp(pl, sub("pli"), "pli", "pl" + s)
-        send(prv, lp, pl, "al" + s, "pl" + s)
-        bg(99)
         if first:
-            qc(E0, 0, 4, "sg0 sg1 sg2 sg3", "qE")
-            for i in range(4):
-                sel(T.sg[:, 512 * i + SLOT[i]:512 * i + 520:4], T.zb[:, 0:130], [[-16, 13], [-1, 10]], A.not_equal, 32.0, 0, 1,
-                    "zb", "sg%d sg%d" % (i, i + 1))
-            sel(T.kn[:], T.zb[:, 0:520], [[-16, 13], [-1, 10], [0, 4]], A.not_equal, -32.0, 0, 1, "zb", "kn")
-        cp(T.ms[:].indirect(pl), T.mk[:], "mk pl" + s, "ms")
+            qc(E0, 0, 4, " ".join(staged(i, range(4)) for i in range(4)), "qE")
+        sc(T.mk[:], ps[1][:, 0:C], "ps1", "mk")
         arrive(nxt, "an" + s, 2, "n" + s)
         mm(1, C, ("up", 128), ("n" + s, 0), True, True, "up1c up1s n" + s)
-        sc(T.mn[:], ps[1][:, 0:C], "ps1", "mn")
-        pick32(T.ms, "ms", T.sa, "sa")
-        for b in range(2):
-            decode(xq, xk, b, 4 + b, slot(T.at, b, 0, C), "at%d" % b)
-        sc(T.aex[:], T.sa[:].indirect(sub("al")), "sa al0 al1", "aex")
-        for b in range(2, 4):
-            decode(xq, xk, b, 4 + b, slot(T.at, b, 0, C), "at%d" % b)
-        if first:
-            consts_keys()
-        arrive(nxt, "al" + s, 1, "lp" + s)
-        cp(T.ms[:].indirect(lp), T.mn[:], "mn lp" + s, "ms")
         if first:
             consts_rows()
-        pick32(T.ms, "ms", T.sa, "sa")
-        tt(T.d0[:, 0:256], T.sa[:].indirect(sub("bl", 0, 16)), T.aex[:, 0:256], A.subtract, "sa bl0 aex", "d01")
-        for h in range(2):
-            act(T.dd[:, 128 * h:128 * h + 128], T.d0[:, 128 * h:128 * h + 128], F.Abs, "d01", "dd%d" % h)
-        qz("g" + s, 0, C, T.at[:], "at0 at1 at2 at3", "g" + s)
-        send_q(nxt, "g" + s, "p" + s, "ap" + s, "g" + s)
+        for b in range(4):
+            decode(xq, xk, b, 4 + b, slot(T.at, b, 0, C), "at%d" % b)
+        scan(T.ls[:], T.pen[:], ps[2][:, 0:C], 0.0, ADD, A.max, "pen ps2", "ls")
+        tt(sub("pre"), sub("pre"), sub("rs"), ADD, "pre " + " ".join("rs%d" % i for i in range(20)), "pre")
+        tt(sub("pli"), T.ls[:, 15:C:16], sub("pre"), A.subtract, "ls pre", "pli")
+        cp(pl, sub("pli"), "pli", "pl" + s)
+        send(prv, lp, pl, "al" + s, "pl" + s)
+        for a, b in PIECES:
+            cp(T.orow[:].indirect(sub("pl" + s, a, b)), T.iot[:, 16 * a:16 * b], "iot px pl" + s, "orow")
+        scan(T.ls[:], T.pen[:], T.orow[:], 0.0, ADD, A.max, "pen orow", "ls")
+        ts(olist, T.ls[:, 15:C:16], pc("o0"), None, ADD, None, "ls _o0", "ol" + s)
+        send(prv, ln, olist, "ao" + s, "ol" + s, spare=BULK[2])
+        send(nxt, lv, olist, "av" + s, "ol" + s, spare=BULK[2])
         if first:
+            sel(T.kn[:], T.zb[:, 0:520], [[-16, 13], [-1, 10], [0, 4]], A.not_equal, -1.0, 0, 1, "zb", "kn")
+            for i in range(4):
+                sel(sg(i, SLOT[i], 130), T.zb[:, 0:130], [[-16, 13], [-1, 10]], A.not_equal, 1.0, 0, 1, "zb",
+                    "sg%d%d sg%d%d" % (i, SLOT[i], i + 1, SLOT[i]))
+            qc(K0, 0, 4, " ".join(staged(i, range(4)) for i in range(4)), "qK")
+            consts_court()
+        pick32(T.mk, pl, "mk pl" + s, "ms", T.sa, "sa")
+        sc(T.mn[:], ps[1][:, 0:C], "ps1", "mn")
+        for a, b in ((0, 8), (8, 16), (16, 24)) if AEX[0] else ((0, 24),):
+            sc(T.aex[:, 16 * a:16 * b], T.sa[:].indirect(sub("al", a, b)), "sa al0 al1", "aex%d" % (a // 8) if AEX[0] else "aex0 aex1 aex2")
+        arrive(nxt, "al" + s, 1, "lp" + s)
+        arrive(nxt, "ao" + s, 1, "ln" + s)
+        arrive(prv, "av" + s, 1, "lv" + s)
+        pick32(T.mn, lp, "mn lp" + s, "m2", T.sn, "sn")
+        for h in range(2):
+            a = slice(128 * h, 128 * h + 128)
+            tt(T.d0[:, a], T.sn[:].indirect(sub("bl", 8 * h, 8 * h + 8)), T.aex[:, a], A.subtract, "sn bl0 aex%d" % h, "d0%d" % h)
+            act(T.dd[:, a], T.d0[:, a], F.Abs, "d0%d" % h, "dd%d" % h)
+        qz("g" + s, 0, C, T.at[:], "at0 at1 at2 at3", "g" + s)
+        send_q(nxt, "g" + s, "p" + s, "ap" + s, "g%s pl%s #al%s" % (s, s, s))
+        if first:
+            for h in range(3):
+                clear_co(h)
+            clear(T.w2, 0, 832, "w20 w21")
+            for h in chains:
+                clear(T.st, 512 * h, 512 * h + 4 * nq, "st%d0 st%d1 st%d2" % (h, h, h))
+                if SPLIT[0]:
+                    clear(T.xs, 512 * h + 320, 512 * h + 512, "xs%d0" % h)
             iota(T.r8[:], [[0, 16], [1, 8]], 0, 0, "r8")
             iota(T.lr[:], [[1, 16], [0, 8]], 0, 0, "lr")
             iota(T.bs[:], [[16, 2], [0, 8], [32, 10]], 0, 0, "bs")
             consts_weights()
-            consts_court()
-            bg(2)
-        else:
-            zero(T.xs, 2, 4 * NB, "xs2", 4)
+            qz("c", 128 * KN, 128 * MX, T.kn[:, 0:512], "kn", "qKN")
+        for h in chains:
+            ms(T.xs[:, 512 * h:512 * h + 4 * nv:2], 0.0, "xs%d0 xs%d2" % (h, h))
+        for b in range(4):
+            decode("n" + s, "n" + s, b, (0, 1, 2, 7)[b], plane(T.vp, b), "vp%d" % b)
+            sc(plane(T.vo, b), plane(T.vp, b).indirect(ln), "vp%d ln%s" % (b, s), "vo%d" % b)
         for h in range(2):
-            for u in range(4):
-                for t in range(len(DL[u])):
-                    compare(h, u, t)
-                    bg(1)
-                n = ((0, 2, 0, 2), (0, 2, 1, 1))[h][u]
-                if n:
-                    quant_co(h, u + 1 - n, n)
-                for w in range(u + 1 - n, u + 1):
-                    rank_mm(h, w, 3 + h)
-                if h == 1 and u == 0:
-                    weigh(slot(T.wt, 0, 0, 80), 3, "bw", "wt00")
-                    weigh(T.wp[:, 0:80], 3, "bx", "wp0")
-                if u == 2 * (1 - h):
-                    for b in (2 * h, 2 * h + 1):
-                        decode("n" + s, "n" + s, b, (0, 1, 2, 7)[b], plane(T.vp, b), "vp%d" % b)
-        bg(99)
-        weigh(slot(T.wt, 0, 80, NB), 4, "bw", "wt01")
-        weigh(T.wp[:, 80:NB], 4, "bx", "wp1")
-        tt(T.d0[:, 256:384], T.sa[:].indirect(sub("bl", 16, 24)), T.aex[:, 256:384], A.subtract, "sa bl1 aex", "d02")
-        qz("wt", 0, NB, T.wt[:], "wt00 wt01 wt1 wt2 wt3", "wtq")
+            wins(h, 3 + h)
+            for t in (1, 3):
+                a = (512 if SPLIT[0] else 320) * h
+                weigh(T.xs[:, a + t:a + 320:4], 3 + h, "bw", "xw%d%d" % (h, t))
+            weigh(T.wp[:, 80 * h:80 * h + 80], 3 + h, "bx", "wp%d" % h)
+        tt(T.d0[:, 256:384], T.sn[:].indirect(sub("bl", 16, 24)), T.aex[:, 256:384], A.subtract, "sn bl1 aex2", "d02")
         act(T.dd[:, 256:384], T.d0[:, 256:384], F.Abs, "d02", "dd2")
-        preload(0)
-
-        def upper_weights():
-            for h in range(2):
-                weigh(slot(T.wt, 2, 80 * h, 80 * h + 80), 2, "u%d" % h, "wt2")
-            for h in range(2):
-                weigh(T.wp[:, NB + 80 * h:NB + 80 * h + 80], 2, "u%d" % (h + 2), "wp2")
-
-        def order_row(a, b):
-            cp(T.orow[:].indirect(sub("pl" + s, a, b)), T.iot[:, 16 * a:16 * b], "iot pl" + s, "orow")
-
-        def order_list():
-            ts(olist, T.ls[:, 15:C:16], pc("o0"), None, ADD, None, "ls _o0", "ol" + s)
-            send(prv, ln, olist, "ao" + s, "ol" + s)
-            send(nxt, lv, olist, "av" + s, "ol" + s)
-
-        def sent(b):
-            decode("p" + s, "p" + s, b, (1, 3, 4, 1)[b], plane(T.gp, b), "gp%d" % b)
-
-        gaps = [[(compare, 2, 0, 0), (compare, 2, 0, 1), (compare, 2, 0, 2), (order_row, 0, 6)],
-                [(compare, 2, 0, 3), (order_row, 6, 12), (quant_co, 2, 0, 1)],
-                [(compare, 2, 1, 0), (order_row, 12, 16)],
-                [(compare, 2, 1, 1), (order_row, 16, 20)],
-                [(compare, 2, 1, 2), (scan, T.ls[:], T.pen[:], T.orow[:], 0.0, ADD, A.max, "pen orow", "ls"), (quant_co, 2, 1, 1)],
-                [(order_list,), (qz, "w2", 0, NB, T.wt[:], "wt00 wt01 wt1 wt2 wt3", "w2q")]]
-        behind = {1: [(sent, 0)], 2: [(rank_mm, 2, 0, 2)], 3: [(sent, 1)], 4: [(sent, 2)], 5: [(rank_mm, 2, 1, 2), (upper_weights,)],
-                  6: [(sent, 3)]}
+        wins(2, 2)
+        for h in range(2):
+            for t in range(2):
+                weigh(slot(T.w2, t, 80 * h, 80 * h + 80), 2, "u%d" % h, "w2%d" % t)
+            weigh(T.wp[:, NB + 80 * h:NB + 80 * h + 80], 2, "u%d" % (h + 2), "wp2")
+        qz("w2", 0, 208, T.w2[:], "w20 w21", "w2q")
         if first:
+            dma("Y", T.lwc[:].bitcast(dt.uint8), T.wc[:], "wp1", "wq")
+            dma("Y", T.lws[:], T.ws[:], "wp1", "wsc")
+            dma("Y", T.vt[:], T.v[:], "wp1", "vt")
             consts_tail()
         arrive(prv, "ap" + s, 2, "p" + s)
-        arrive(nxt, "ao" + s, 1, "ln" + s)
-        arrive(prv, "av" + s, 1, "lv" + s)
-        for k in range(SW - 1):
-            if k:
-                mm(LB[k % 2], NB, ct(MX), ("xs", 0), False, True, "qMX xsq")
-            if k >= 7:
-                mm(UB[k % 2], NB, ct(MX + 1), ("xs", 0), False, True, "qMX xsq")
-            if k < SW - 2:
-                preload(k + 1)
-            if k == 0 and first:
-                dma("Y", T.lwc[:].bitcast(dt.uint8), T.wc[:], "wtq", "wq")
-                dma("Y", T.lws[:], T.ws[:], "", "wsc")
-                dma("Y", T.vt[:], T.v[:], "", "vt")
-            for call in behind.get(k, ()):
-                call[0](*call[1:])
-            if k == 0 and first:
-                consts_tail_numbers()
-            if k == 5 and first:
-                consts_tail_scalar()
-            if k == 10 and final:
-                sc(T.onr[:], T.iot[:].indirect(ln), "iot ln" + s, "onr")
-            if k >= 7:
-                sc(plane(T.vo, k - 7), plane(T.vp, k - 7).indirect(ln), "vp%d ln%s" % (k - 7, s), "vo%d" % (k - 7))
-            tt(slot(T.xs, 0), ps[LB[k % 2]][:, 0:NB], T.wp[:, 0:NB], A.min, "ps%d wp0 wp1" % LB[k % 2], "xs0")
-            if k >= 7:
-                tt(slot(T.xs, 2), ps[UB[k % 2]][:, 0:NB], T.wp[:, NB:C], A.min, "ps%d wp2" % UB[k % 2], "xs2")
-            live = T.xs[:, 0:4 * NB:2] if k >= 7 else slot(T.xs, 0)
-            ts(live, live, 0.0, SIG, A.max, MUL, "xs0 xs2", "xs0 xs2" if k >= 7 else "xs0")
-            qz("xs", 0, NB, T.xs[:], "xs0 xs1 xs2 xs3", "xsq")
-            for call in gaps[k] if k < len(gaps) else ():
-                call[0](*call[1:])
-            if k >= len(gaps):
-                bg(3)
-        bg(99)
-        for t in range(2):
-            mm(3 + t, NB, ct(SS + t), ("xs", 0), True, True, "qSS xsq")
         for b in (3, 0, 1, 2):
+            decode("p" + s, "p" + s, b, (1, 3, 4, 1)[b], plane(T.gp, b), "gp%d" % b)
             sc(plane(T.go, b), plane(T.gp, b).indirect(lv), "gp%d lv%s" % (b, s), "go%d" % b)
-        for t in range(2):
-            tt(slot(T.st, 2 * t), ps[3 + t][:, 0:NB], slot(T.xs, 2 * t), A.is_lt, "ps%d xs%d" % (3 + t, 2 * t), "st%d" % (2 * t))
-        qz("st", 0, NB, T.st[:], "st0 st1 st2 st3", "stq")
-        mm(1, NB, ct(FA), ("st", 0), True, True, "qMU stq")
+        if final:
+            sc(T.onr[:], T.iot[:].indirect(ln), "iot ln" + s, "onr")
+        def tile(name, src, h, R, W):
+            qz(name, 128 * h, 128 * h + nq, src[:, 512 * h:512 * h + 4 * nq], R, W)
+
+        def part(buf, h, t):
+            return buf[:, 512 * h + t:512 * h + 4 * nv:4]
+
+        def ys(h, t):
+            return slice(NB * t + 80 * h, NB * t + 80 * h + nv)
+
+        for k in range(SW):
+            for h in chains:
+                x, lb, ub = ("xs", 128 * h), 5 + h, (7, 0)[h] if SPLIT[0] else (7, 0)[k % 2]
+                tile("xs", T.xs, h, "xs%d0 xs%d2 xw%d1 xw%d3" % (h, h, h, h) + ("" if SPLIT[0] else " xw11 xw13"), "xq%d" % h)
+                if k == SW - 1:
+                    continue
+                mm(lb, nq, ct(MX), x, True, True, "qMX xq%d" % h)
+                tt(T.ys[:, ys(h, 0)], ps[lb][:, 0:nv], T.wp[:, ys(h, 0)], A.min, "ps%d wp%d" % (lb, h) + ("" if SPLIT[0] else " wp1"), "ys%d0" % h)
+                ts(part(T.xs, h, 0), T.ys[:, ys(h, 0)], 0.0, SIG, A.max, MUL, "ys%d0" % h, "xs%d0" % h)
+                if k >= 7:
+                    mm(ub, nq, ct(MX + 2), ("w2", 80 * h), True, False, "qMU_ w2q")
+                    mm(ub, nq, ct(MX + 1), x, False, True, "qMU_ xq%d" % h)
+                    tt(T.ys[:, ys(h, 1)], ps[ub][:, 0:nv], T.wp[:, ys(h, 1)], A.min, "ps%d wp2" % ub, "ys%d1" % h)
+                    ts(part(T.xs, h, 2), T.ys[:, ys(h, 1)], 0.0, SIG, A.max, MUL, "ys%d1" % h, "xs%d2" % h)
+        for h in chains:
+            for t in range(2):
+                bank = ((3, 4), (1, 2))[h][t]
+                mm(bank, nq, ct(SS + 1 - t), ("xs", 128 * h), True, True, "qSS xq%d" % h)
+                tt(part(T.st, h, 2 * t), ps[bank][:, 0:nv], T.ys[:, ys(h, t)], A.is_lt, "ps%d ys%d%d" % (bank, h, t), "st%d%d" % (h, 2 * t))
+            tile("st", T.st, h, "st%d0 st%d1 st%d2" % (h, h, h), "sq%d" % h)
+            mm(5 + h, nq, ct(FA), ("st", 128 * h), True, True, "qMU sq%d" % h)
+            ts(part(T.st, h, 1), ps[5 + h][:, 0:nv], pc("th"), None, EQ, None, "ps%d _th" % (5 + h), "st%d1" % h)
+            tile("s2", T.st, h, "st%d0 st%d1 st%d2" % (h, h, h), "s2q%d" % h)
         if final:
             qz("v", 0, 128, T.vt[:], "vt", "vq")
-        ts(slot(T.st, 1), ps[1][:, 0:NB], pc("th"), None, EQ, None, "ps1 _th", "st1")
-        qz("s2", 0, NB, T.st[:], "st0 st1 st2 st3", "s2q")
-        places(MI, 2, "mt", sub("hl" + s, 0, 32), "hl" + s)
+        places(MI, (3, 1), "mt", sub("hl" + s, 0, 32), "hl" + s)
         send(nxt, lh, hl, "ah" + s, "hl" + s)
-        places(MU, 3, "mt2", sub("mu", 0, 32), "mu")
+        places(MU, (4, 2), "mt2", sub("mu", 0, 32), "mu")
         for hf in range(2):
             for b in range(4):
                 mm(HB[hf][b], H, et(b), (xq, H * hf), True, False, "qE " + xk)
-        cp(plane(T.vq, 3), plane(T.vo, 3).indirect(sub("mu")), "vo3 mu", "vq3")
-        for b in (0, 1):
-            cp(plane(T.vq, b), plane(T.vo, b).indirect(sub("mu")), "vo%d mu" % b, "vq%d" % b)
-        sc(plane(T.vq, 2), plane(T.vo, 2).indirect(sub("mu")), "vo2 mu", "vq2")
-        sc(T.vg[:], plane(T.vq, 3).indirect(pl), "vq3 pl" + s, "vg")
+        for b in range(4):
+            (cp if PICK[0][b] == "V" else sc)(plane(T.vq, b), plane(T.vo, b).indirect(sub("mu")), "vo%d mu" % b, "vq%d" % b)
+            if PICK[2][b] == "F":
+                (cp if PICK[1][b] == "V" else sc)(plane(T.vg, b), plane(T.vq, b).indirect(pl), "vq%d pl%s" % (b, s), "vg%d" % b)
         if final:
-            sc(T.wrow[:], T.onr[:].indirect(sub("mu")), "onr mu", "wrow")
+            (cp if OLE[0] == "V" else sc)(T.wrow[:], T.onr[:].indirect(sub("mu")), "onr mu", "wrow")
         arrive(prv, "ah" + s, 1, "lh" + s)
-        sc(T.gq[:], plane(T.go, 3).indirect(lh), "go3 lh" + s, "gq")
-        for b in range(3):
-            tt(plane(T.zp, b), plane(T.go, b).indirect(lh), plane(T.vq, b), A.max, "go%d vq%d lh%s" % (b, b, s), "zp%d" % b)
-            if b < 2:
-                sc(slot(T.zt, b, 0, C), plane(T.zp, b).indirect(pl), "zp%d pl%s" % (b, s), "zt0%d zt1%d" % (b, b))
-        for hf in range(2):
-            half = sub("pl" + s, 10 * hf, 10 * hf + 10)
-            sc(slot(T.zt, 2, H * hf, H * hf + H), plane(T.zp, 2).indirect(half), "zp2 pl" + s, "zt%d2" % hf)
-            tt(slot(T.zt, 3, H * hf, H * hf + H), T.gq[:].indirect(half), T.vg[:, H * hf:H * hf + H], A.max, "gq vg pl" + s, "zt%d3" % hf)
+        for b in range(4):
+            if PICK[2][b] == "F":
+                sc(plane(T.zp, b), plane(T.go, b).indirect(lh), "go%d lh%s" % (b, s), "zp%d" % b)
+            else:
+                tt(plane(T.zp, b), plane(T.go, b).indirect(lh), plane(T.vq, b), A.max, "go%d vq%d lh%s" % (b, b, s), "zp%d" % b)
+            for lo, hi in ((0, 2),) if WHOLE[b] else ((0, 1), (1, 2)):
+                out, src = slot(T.zt, b, H * lo, H * hi), plane(T.zp, b).indirect(sub("pl" + s, 10 * lo, 10 * hi))
+                W = " ".join("zt%d%d" % (hf, b) for hf in range(lo, hi))
+                if PICK[2][b] == "F":
+                    tt(out, src, plane(T.vg, b, H * lo, H * hi), A.max, "zp%d vg%d pl%s" % (b, b, s), W)
+                else:
+                    (cp if PICK[2][b] == "V" else sc)(out, src, "zp%d pl%s" % (b, s), W)
         if final:
-            sc(T.wro2[:], T.wrow[:].indirect(pl), "wrow pl" + s, "wro2")
+            (cp if OLE[1] == "V" else sc)(T.wro2[:], T.wrow[:].indirect(pl), "wrow pl" + s, "wro2")
             for k in range(8):
                 dma("Y", T.ol[k:k + 1, :], T.wro2[16 * k:16 * k + 1, :], "wro2", "")
         for hf in range(2):
@@ -709,10 +779,10 @@ def rank_program(g, core, T, topo):
                 dma("Y", T.oc[:, 4 * H * hf:4 * H * (hf + 1)], T[xq + "c"][:, H * hf:H * hf + H].bitcast(dt.uint8), xq + "ab"[hf], "")
         if not final:
             send_q(prv, xq, "n%d" % (r + 1), "an%d" % (r + 1), "%sa %sb" % (xq, xq))
-    sc(T.yb[:, 0:H], ps[0][:, 0:H], "ps0", "yb0")
-    cp(T.yb[:, H:C], ps[1][:, 0:H], "ps1", "yb1")
+    sc(T.sq[:, 0:H], ps[0][:, 0:H], "ps0 sq", "yb0")
+    cp(T.sq[:, H:C], ps[1][:, 0:H], "ps1 sq", "yb1")
     for hf in range(2):
-        dma("Y", T.y[:, H * hf:H * hf + H], T.yb[:, H * hf:H * hf + H], "yb%d" % hf, "")
+        dma("Y", T.y[:, H * hf:H * hf + H], T.sq[:, H * hf:H * hf + H], "yb%d" % hf, "")
     for k in range(4):
         dma("S", T.osc[4 * k:4 * k + 4, :], T[xq + "s"][32 * k:32 * k + 4, :], "%sa %sb" % (xq, xq), "")
     emit(g, T, ops)

@@ -11,18 +11,24 @@ X4, U8, BF, F32, I32, U16 = "float8_e4m3fn_x4", "uint8", "bfloat16", "float32", 
 WB, E0, K0, KN, MX, SS, MU, FA, MI, NT = 0, 1, 5, 9, 10, 13, 15, 16, 17, 18
 SLOT = (0, 2, 1, 3)
 SOFF, SWID = [0, 320, 576, 768, 896], [320, 256, 192, 128, 128]
-DL, DU = ((15, 14, 13, 12), (11, 10, 9, 8), (7, 6, 5, 4), (3, 2, 1)), ((7, 6, 5, 4), (3, 2, 1))
-QUANT = [[0, 2, 0, 2], [0, 2, 1, 1], [1, 1]]
-POOL = ["cz1", "co1", "w20", "st0", "st1"]
-PICK = ["VVSS", "VVVV", "SSSV"]
-LOW, FEW = [18, 18], [4, 4]
-DIAG = [0, 1]
-PIECES, AEX, WHOLE, OLE = [(0, 10), (10, 20)], [1], [1, 1, 0, 0], ["S", "S"]
-LISTS = set("uoff ky al bl tl mu pl px xy ol ln lv lh".split())
-START, WAKE, PASSES = {"V": 5, "S": 110, "P": 30, "G": 10, "Y": 0, "A": 0}, [140, 180], 4
-BULK = [3000, 3000, 3000, 7000]
-PE = [0.5, 2.2, 2.2, 1500]
-SPLIT = [0]
+DL, DU = ((1, 2, 3, 4), (5, 6, 7, 8)), ((1, 2, 3, 4),)
+POOL = ["ct1", "ct3", "ct4", "w20", "st0"]
+PICK = ["VVSV", "VVVS", "SSSF"]
+LOW, FEW = [18, 18], [6, 6]
+DIAG = [1, 1]
+PIECES, AEX, WHOLE, OLE = [(0, 20)], [0], [1, 1, 0, 0], ["S", "S"]
+FIRST, OUT, SPARE = [1], ["V", "S"], [0, 0]
+LIGHT = [0, 0, 0]
+LISTS = set("uoff ky al bl tl mu pl px xy ol ln lv lh zl ey".split())
+START, WAKE, PASSES = {"V": 5, "S": 110, "P": 30, "G": 10, "Y": 0, "A": 0}, [190, 230], 4
+BULK = [3000, 3000, 5000, 7000]
+PE = [0.5, 1.8, 2.4, 1800, 4500]
+BOTH = [4]
+SPLIT = [1]
+XN, LAST, MB = ["SVSV", "SVSV"], [0], ["SSVV"]
+RUNS = [2, 2]
+JIT = [0]
+AHEAD = [1500, 500, 1000, 0, 0]
 BEFORE = {}
 LB, UB, HB = 5, (6, 7), ((0, 1, 4, 5), (6, 7, 2, 3))
 
@@ -42,12 +48,12 @@ def _q(names, n):
 
 def _s(buf, names, d):
     for i, s in enumerate(names.split()):
-        SUB[s] = (buf, 32 * i, {"uoff": 16, "al": 24, "bl": 24, "ky": 16, "tl": 2, "ends": 2}.get(s, 20))
+        SUB[s] = (buf, 32 * i, {"uoff": 16, "al": 24, "bl": 24, "ky": 16, "tl": 2, "zl": 8}.get(s, 20))
     _b(buf, 32 * len(names.split()), d)
 
 
 _b("xt at zt xn vp vo vq gp go zp", 4 * C, BF)
-_b("ut vt wb", 512, BF)
+_b("ut vt", 512, BF)
 _b("kn zb", 520, BF)
 _b("w2", 832, BF)
 _b("xs st", 1024, BF)
@@ -55,16 +61,20 @@ _b("vg", 4 * C, BF)
 _b("sg", 2064, BF)
 _b("ys dg", C, BF)
 _b("sot", 4096, BF)
-_b("cot", 5120, BF)
+_b("cot", 2560, BF)
+_b("dd", 384, F32)
 _b("jk", 3400, BF)
 _b("m16 k16 k01 pen k10 e10 ru e16 r16 r10 wp", C, BF)
 _b("iot mk mn sb ls sa sn sq orow onr wrow wro2", C, F32)
-_b("aex d0 dd", 384, F32)
+_b("aex d0", 384, F32)
 _b("wr r8 lr", 128, BF)
-_b("psr pir a1 a2 b1t b2t", 256, BF)
+_b("psr pir a1 a2", 256, BF)
+_b("bt", 512, BF)
 _b("fa", 512, BF)
 _b("fb", 768, BF)
 _b("mt mt2 bs", NB, F32)
+_b("er", 128, BF)
+_b("kr", 130, BF)
 _b("ms mst m2 m2t", C, F32)
 _b("pi", 8, I32)
 _b("pf", 64, F32)
@@ -72,7 +82,7 @@ _b("li", 96, I32)
 _b("kf", 128, F32)
 _s("sf", "rs pre cbs fx", F32)
 _s("si", "pli j32 j10", I32)
-_s("of", "uoff al bl ky tl mu xy", U16)
+_s("of", "uoff al bl ky tl mu xy zl ey", U16)
 _s("snd", "pl0 pl1 ol0 ol1 hl0 hl1", U16)
 _s("lnd", "lp0 lp1 ln0 ln1 lv0 lv1 lh0 lh1", U16)
 _q("lw", 512)
@@ -83,10 +93,10 @@ _q("up", 256)
 _q("x0 x1 x2 g0 g1 n0 n1 p0 p1 z", C)
 _q("c", 128 * NT)
 _q("so", 1024)
-_q("co", 1664)
+_q("co", 1408)
 for _i in range(8):
     SCRATCH["b%d" % _i] = ("psum", [128, 512], F32)
-SEMAPHORES = ["V", "S", "P", "G", "loc"] + ["d%d" % i for i in range(40)] + \
+SEMAPHORES = ["V", "S", "P", "G", "loc"] + ["d%d" % i for i in range(32)] + \
              [a + str(r) for r in range(NR) for a in ("an", "ap", "al", "ao", "av", "ah")]
 
 
@@ -136,6 +146,9 @@ def arrange(ops, deps):
             best = (end, start)
         back = place(sorted(range(n), key=lambda i: (-start[i], -i)), late)
         key = [-back[i] - t[i] for i in range(n)]
+        if JIT[0] and _ % 2:
+            for i in range(n):
+                key[i] = max([key[i] + JIT[0] * ((i * 7919 + _ * 104729) % 1000 / 500 - 1)] + [key[j] + 1 for j in deps[i]])
     return sorted(range(n), key=lambda i: (best[1][i], i))
 
 
@@ -243,7 +256,7 @@ def rank_program(g, core, T, topo):
         ops.append(dict(e=e, f=f, R=R.split(), W=W.split(), t=t, k=k, **kw))
 
     def span(R, *aps, rate=1.0):
-        n = aps[0].shape[1]
+        n = math.prod(aps[0].shape[1:])
         if LISTS.intersection(a.rstrip("01") for a in R.split()):
             return 60 + n * (PE[2] if "px" in R else PE[1])
         if rate == 1.0 and all("bfloat16" in str(a.dtype) for a in aps):
@@ -272,7 +285,7 @@ def rank_program(g, core, T, topo):
         op("V", lambda q: q.quantize_mx(T[name + "c"][:, a:b], T[name + "s"][:, a:b], src), R, W, 15 + 1.06 * (b - a))
 
     def act(out, a, func, R, W, **kw):
-        load = 1600 if W == "xw01" and not any("wp0" in o["W"] for o in ops) else 0
+        load = 1600 if W == "_nz" else 0
         op("S", lambda q: q.activation(out, a, func, **kw), R, W, span(R, out, rate=1.01) + load)
 
     def af(out, a, scale, bias, R, W):
@@ -353,9 +366,9 @@ def rank_program(g, core, T, topo):
     pi, pf, li, kf = T.pi, T.pf, T.li, T.kf
     SH, AND, EQ, MUL, ADD = A.logical_shift_right, A.bitwise_and, A.is_equal, A.mult, A.add
     H = C // 2
-    chains, nq, nv = ((0, 1), 128, 80) if SPLIT[0] else ((0,), NB, NB)
+    chains, nq, nv, wide = ((0, 1), 128, 80, 512) if SPLIT[0] else ((0,), NB, NB, 320)
 
-    names = ("p g l8 p3 p1 q s hb s4 s2 c1 c2 c3 lB sB iA iB z nz nnz co s16 vl vu alo blo alu blu tl t0 t1 t2 cb o0 fx "
+    names = ("p g l8 p3 p1 q l7 aw ax s hb s4 s2 c1 c2 c3 lB sB iA iB z nz cn gn cz co s16 vl vu alo blo alu blu tl t0 t1 t2 cb o0 fx "
              "t3 t4 t5 t6 t7 bw bx l15 u0 u1 u2 u3 th fl fu fs").split()
 
     def pc(name, n=1):
@@ -369,7 +382,7 @@ def rank_program(g, core, T, topo):
         else:
             ts(pc(name), pc(src), float(k), a, MUL, ADD, R, "_" + name)
 
-    dma("Y", T.xt[:], T.x[:], "", "xt", 4500)
+    dma("Y", T.xt[:], T.x[:], "", "xt", PE[4])
     dma("S", T.ut[:], T.u[:], "", "ut")
     iota(pi[:, 0:1], [[0, 1]], 0, 1, "pi0", False)
     iota(T.r16[:], [[0, 20], [1, 16]], 0, 0, "r16")
@@ -377,21 +390,21 @@ def rank_program(g, core, T, topo):
     iota(li[:, 0:16], [[1, 2], [16, 8]], 0, 0, "li0", False)
     iota(li[:, 16:36], [[16, 20]], 0, 0, "li1", False)
     ms(T.zb[:], 0.0, "zb")
-    for c, s, m in ((1, 4, 7), (2, 3, 15), (3, 0, 3), (4, 0, 1), (5, 0, 15)):
+    for c, s, m in ((1, 4, 7), (2, 3, 15), (3, 0, 3), (4, 0, 1), (5, 0, 15), (6, 6, 1)):
         ts(pi[:, c:c + 1], pi[:, 0:1], s, m, SH, AND, "pi0", "pi%d" % c)
-    cp(pc("p", 6), pi[:, 0:6], "pi0 pi1 pi2 pi3 pi4 pi5", "_p _g _l8 _p3 _p1 _q")
+    cp(pc("p", 7), pi[:, 0:7], "pi0 pi1 pi2 pi3 pi4 pi5 pi6", "_p _g _l8 _p3 _p1 _q _l7")
     for u in range(4):
         zero(T.sot, 4 * (SOFF[u] + SWID[u] - 48), 4 * (SOFF[u] + SWID[u]), "sz%d" % u)
     zero(T.sot, 4 * SOFF[4], 4096, "sz4")
     ts(T.e16[:], T.r16[:], pc("q"), None, EQ, None, "r16 _q", "e16")
     ts(T.k01[:], T.r16[:], 0.0, None, A.is_gt, None, "r16", "k01")
     for t in range(4):
-        ts(T.wb[:, t:512:4], T.wr[:], pc("g"), None, EQ, None, "wr _g", "wb%d" % t)
+        ts(T.fa[:, t:512:4], T.wr[:], pc("g"), None, EQ, None, "wr _g", "wb%d" % t)
     cp(sub("uoff"), li[:, 0:16], "li0", "uoff")
     af(T.m16[:], T.e16[:], 2 * BIG, -BIG, "e16", "m16")
     af(T.k16[:], T.k01[:], 2 * BIG, -BIG, "k01", "k16")
     af(T.pen[:], T.e16[:], -1049600.0, 1024.0, "e16", "pen")
-    qz("c", 128 * WB, 128 * E0, T.wb[:], "wb0 wb1 wb2 wb3", "qWB")
+    qz("c", 128 * WB, 128 * E0, T.fa[:], "wb0 wb1 wb2 wb3 fa0 fa1 fa2", "qWB")
     for n, s, k, a in (("s", "l8", -8, "p"), ("hb", "g", -2, "l8"), ("s2", "p1", -1, "p3"), ("cb", "q", 1023, 15 - 15360),
                        ("o0", "q", 1024, -15360), ("s4", "p3", -1, "s"), ("alo", "hb", 10, 9),
                        ("blo", "s", 10, 9), ("t0", "hb", 160, 9), ("c1", "s2", -2, 2), ("t1", "s", -30, 249)):
@@ -422,12 +435,15 @@ def rank_program(g, core, T, topo):
         if b == 1:
             qz("x0", 0, C, T.xt[:], "xt", "x0a x0b")
             send_q(prv, "x0", "n0", "an0", "x0a x0b", 2700)
-        sel(T.sg[:, 512 * b:512 * b + 512], T.zb[:, 0:512], [[4, 128], [1, 4]], A.not_equal, 32.0, -SLOT[b], -4, "zb", staged(b, range(4)))
+        if b < LIGHT[0]:
+            ms(T.sg[:, 512 * b:512 * b + 512], 0.0, staged(b, range(4)))
+            sel(sg(b, SLOT[b]), T.zb[:, 0:128], [[1, 128]], A.not_equal, 32.0, 0, -1, "zb", staged(b, [SLOT[b]]))
+        else:
+            sel(T.sg[:, 512 * b:512 * b + 512], T.zb[:, 0:512], [[4, 128], [1, 4]], A.not_equal, 32.0, -SLOT[b], -4, "zb",
+                staged(b, range(4)))
     iota(T.iot[:], [[1, C]], 0, 0, "iot")
-    qz("co", 0, 128, T.zb[:, 0:512], "zb", "coz")
-    for a in (640, 1280):
-        dma("Y", T.coc[:, a:a + 128].bitcast(dt.uint8), T.coc[:, 0:128].bitcast(dt.uint8), "coz xt", "cy%dc" % a)
-        dma("Y", T.cos[:, a:a + 128], T.cos[:, 0:128], "coz xt", "cy%ds" % a)
+    for i in range(6):
+        qz("co", 256 * i, 256 * i + 128, T.zb[:, 0:512], "zb", "cz%d" % i)
     ms(sub("rs", 0, 1), 0.0, "rs0")
     lin("fx", "q", 1, -4.5, "V")
     ts(sub("fx"), li[:, 16:36], pc("fx"), 0.1, ADD, MUL, "li1 _fx", "fx")
@@ -446,36 +462,47 @@ def rank_program(g, core, T, topo):
     L(ts, sub("bl", 16, 24), li[:, 36:44], pc("blu"), 80.0, ADD, ADD, "li2 _blu", "bl1")
 
     L(tt, kf[:, 64:96], kf[:, 0:32], kf[:, 32:64], ADD, "k0 k1 k2 k3 k4 k5", "k6")
-    L(lin, "nz", "z", -1, 1, "V")
+    act(pc("nz"), pc("z"), F.Exp, "_z", "_nz", scale=-200.0)
     L(tt, kf[:, 96:112], kf[:, 64:80], kf[:, 80:96], ADD, "k6", "k7")
-    L(lin, "nnz", "z", 1, -1, "V")
+    lin("cn", "nz", CW, 0)
+    lin("gn", "nz", CW * GW, 0)
+    lin("cz", "z", CW, 0, "V")
     L(ts, sub("ky"), kf[:, 96:112], 1.0, None, ADD, None, "k7", "ky")
-    L(lin, "co", "z", -1 / GW, -1 / GW, "V")
+    lin("co", "z", -CW, -CW, "V")
 
     def consts_rows():
         sc(T.psr[:], T.r16[:].indirect(sub("ky")), "r16 ky", "psr")
         sc(T.pir[:], T.iot[:].indirect(sub("ky")), "iot ky", "pir")
+        if FIRST[0]:
+            lin("t6", "t2", 16, 16, "V")
+            lin("t7", "hb", 1, -2, "V")
+            ts(kf[:, 116:124], li[:, 16:24], pc("t6"), pc("t7"), EQ, MUL, "li1 _t6 _t7", "k9")
+            ts(sub("ey", 0, 8), kf[:, 116:124], 2.0, None, ADD, None, "k9", "ey")
+            sc(T.er[:], T.iot[:].indirect(sub("ey", 0, 8)), "iot ey", "er")
+            ts(sub("zl"), li[:, 16:24], 4.25, None, MUL, None, "li1", "zl")
 
     def consts_court():
-        ts(T.a1[:], T.psr[:], pc("s"), CW, EQ, MUL, "psr _s", "a1")
-        ts(T.a2[:], T.pir[:], pc("iA"), CW * GW, EQ, MUL, "pir _iA", "a2")
-        tt(T.fa[:, 0:256], T.a1[:], T.a2[:], ADD, "a1 a2", "fa0")
-        af(T.b1t[:], T.a1[:], pc("z"), 0.0, "a1 _z", "b1t")
-        af(T.b2t[:], T.a2[:], pc("co"), 0.0, "a2 _co", "b2t")
-        af(sg(0, 1, 256), T.a2[:], pc("nnz"), 0.0, "a2 _nnz qE", "sg01 sg11")
-        af(sg(0, 0, 256), T.fa[:, 0:256], pc("nz"), 0.0, "fa0 _nz qE", "sg00 sg10")
-        tt(sg(0, 3, 256), T.b1t[:], T.b2t[:], ADD, "b1t b2t qE", "sg03 sg13")
+        for i in range(2):
+            a, b = slice(128 * i, 128 * i + 128), slice(256 + 128 * i, 384 + 128 * i)
+            ts(T.a1[:, a], T.psr[:, a], pc("s"), pc("cn"), EQ, MUL, "psr _s _cn", "a1%d" % i)
+            ts(T.a2[:, a], T.pir[:, a], pc("iA"), pc("gn"), EQ, MUL, "pir _iA _gn", "a2%d" % i)
+            ts(T.bt[:, a], T.psr[:, a], pc("s"), pc("cz"), EQ, MUL, "psr _s _cz", "b1%d" % i)
+            ts(T.bt[:, b], T.pir[:, a], pc("iA"), pc("co"), EQ, MUL, "pir _iA _co", "b2%d" % i)
+            tt(sg(i, 0), T.a1[:, a], T.a2[:, a], A.max, "a1%d a2%d" % (i, i), "sg%d0" % i)
+            af(sg(i, 1), T.a2[:, a], -1.0, 0.0, "a2%d" % i, "sg%d1" % i)
+            tt(sg(i, 3), T.bt[:, a], T.bt[:, b], ADD, "b1%d b2%d" % (i, i), "sg%d3" % i)
         ts(T.fa[:, 256:384], T.psr[:, 128:256], pc("sB"), CW, EQ, MUL, "psr _sB", "fa1")
         ts(T.fa[:, 384:512], T.pir[:, 128:256], pc("iB"), CW * GU, EQ, MUL, "pir _iB", "fa2")
         tt(sg(1, 2), T.fa[:, 256:384], T.fa[:, 384:512], A.max, "fa1 fa2 qE", "sg12")
         ts(sg(2, 0), T.pir[:, 128:256], pc("iB"), -CW * GU, EQ, MUL, "pir _iB qE", "sg20")
         ts(sg(2, 1), T.pir[:, 128:256], pc("iB"), -CW, EQ, MUL, "pir _iB qE", "sg21")
         qc(MX, 0, 1, staged(0, range(4)), "qMX")
+        ops[-1]["spare"] = SPARE[0]
         qc(MX + 1, 1, 2, staged(1, range(4)) + " " + staged(2, range(4)), "qMU_")
 
     def consts_weights():
-        for n, s, k, a in (("bw", "l8", LN2, 0), ("bx", "l8", LN2, -math.log(SIG)), ("t6", "g", LN2, 8 * LN2),
-                           ("t7", "g", LN2, 8 * LN2 - 200), ("u0", "hb", -200, "t6"), ("u1", "hb", 200, "t7"),
+        for n, s, k, a in (("bw", "l7", LN2, 7 * LN2), ("bx", "l7", LN2, 7 * LN2 - math.log(SIG)), ("aw", "l7", LN2, 11 * LN2),
+                           ("ax", "l7", LN2, 11 * LN2 - 200), ("u0", "hb", -200, "aw"), ("u1", "hb", 200, "ax"),
                            ("u2", "u0", 1, -math.log(SIG)), ("u3", "u1", 1, -math.log(SIG))):
             lin(n, s, k, a, "V")
 
@@ -524,36 +551,31 @@ def rank_program(g, core, T, topo):
     def wins(h, bank):
         D, w = shifts(h)
         for u, ds in enumerate(D):
-            a, c = 2048 * h + 512 * u, 128 + 640 * h
+            i = 2 * h + u
+            a, c, o, R = 512 * i, 128 + 256 * i, 128 * h, "dd%d" % h + BEFORE.get((h, u), "")
             for t, d in enumerate(ds):
                 n = 128 - w * d
-                tt(T.cot[:, a + t:a + 4 * n:4], T.dd[:, 128 * h:128 * h + n], T.dd[:, 128 * h + w * d:128 * h + 128], A.is_le,
-                   "dd%d cz%d%d" % (h, h, u) + (" cq%d%d" % BEFORE[h, u] if (h, u) in BEFORE else ""), "co%d%d%d" % (h, u, t))
-            n = QUANT[h][u]
-            if n:
-                qz("co", c + 128 * (u + 1 - n), c + 128 * (u + 1), T.cot[:, a + 512 - 512 * n:a + 512],
-                   " ".join("co%d%d%d" % (h, v, t) for v in range(u + 1 - n, u + 1) for t in range(4)),
-                   " ".join("cq%d%d" % (h, v) for v in range(u + 1 - n, u + 1)))
-            for v in range(u + 1 - n, u + 1):
-                before = "cq%d%d" % (h, v - 1) if v else ("coz", "cy640c cy640s", "cy1280c cy1280s")[h]
-                mm(bank, 128, ("co", c + 128 * v), ct(KN), v == 0, False, "cq%d%d qKN" % (h, v))
-                for t, d in enumerate(D[v]):
-                    mm(bank, 128, ("co", c + 128 * v - w * d), ct(K0 + SLOT.index(t)), False,
-                       v == len(D) - 1 and t == len(D[v]) - 1, "cq%d%d qK %s" % (h, v, before))
+                tt(T.cot[:, a + t:a + 4 * n:4], T.dd[:, o:o + n], T.dd[:, o + w * d:o + 128], A.is_le, R, "co%d%d" % (i, t))
+                if w * d < 64:
+                    tt(T.cot[:, a + 4 * n + t:a + 512:4], T.dd[:, o + n:o + 128], T.dd[:, o:o + w * d], A.is_lt, R, "ct%d%d" % (i, t))
+            qz("co", c, c + 128, T.cot[:, a:a + 512], " ".join("co%d%d ct%d%d" % (i, t, i, t) for t in range(4)), "cq%d" % i)
+            ops[-1]["spare"] = AHEAD[i]
+            mm(bank, 128, ("co", c), ct(KN), u == 0, False, "cq%d qKN" % i)
+            for t, d in enumerate(ds):
+                R = "cq%d qK cz%d cz%d" % (i, i, i + 1)
+                if w * d < 64:
+                    mm(bank, 128, ("co", c + 128 - w * d), ct(K0 + SLOT.index(t)), False, False, R)
+                mm(bank, 128, ("co", c - w * d), ct(K0 + SLOT.index(t)), False, w * d == 64, R)
 
-    def clear(buf, a, b, W, step=1):
+    def clear(out, W):
         if W[:3] in POOL:
-            iota(buf[:, a:b:step], [[0, (b - a + step - 1) // step]], 0, 0, W)
+            iota(out, [[0, out.shape[1]]], 0, 0, W)
         else:
-            ms(buf[:, a:b:step], 0.0, W)
+            ms(out, 0.0, W)
 
     def clear_co(h):
-        D, w = shifts(h)
-        for u, ds in enumerate(D):
-            a = 2048 * h + 512 * u
-            clear(T.cot, a + 4 * (128 - w * ds[0]), a + 512, "cz%d%d" % (h, u))
-            if len(ds) < 4:
-                clear(T.cot, a + 3, a + 4 * (128 - w * ds[0]), "co%d%d3" % (h, u), 4)
+        i = (1, 3, 4)[h]
+        clear(T.cot[:, 512 * i + 259:512 * i + 512:4], "ct%d3" % i)
 
     def weigh(out, bank, bias, W):
         act(out, ps[bank][:, 0:NB // 2], F.Exp, "ps%d _%s" % (bank, bias), W, scale=-LN2, bias=pc(bias))
@@ -624,8 +646,13 @@ def rank_program(g, core, T, topo):
         for b in range(4):
             decode(xq, xk, b, 4 + b, slot(T.at, b, 0, C), "at%d" % b)
         scan(T.ls[:], T.pen[:], ps[2][:, 0:C], 0.0, ADD, A.max, "pen ps2", "ls")
-        tt(sub("pre"), sub("pre"), sub("rs"), ADD, "pre " + " ".join("rs%d" % i for i in range(20)), "pre")
-        tt(sub("pli"), T.ls[:, 15:C:16], sub("pre"), A.subtract, "ls pre", "pli")
+        rows = " ".join("rs%d" % i for i in range(20))
+        if LAST[0]:
+            tt(sub("pre"), T.ls[:, 15:C:16], sub("pre"), A.subtract, "ls pre", "pre")
+            tt(sub("pli"), sub("pre"), sub("rs"), A.subtract, "pre " + rows, "pli")
+        else:
+            tt(sub("pre"), sub("pre"), sub("rs"), ADD, "pre " + rows, "pre")
+            tt(sub("pli"), T.ls[:, 15:C:16], sub("pre"), A.subtract, "ls pre", "pli")
         cp(pl, sub("pli"), "pli", "pl" + s)
         send(prv, lp, pl, "al" + s, "pl" + s)
         for a, b in PIECES:
@@ -635,11 +662,15 @@ def rank_program(g, core, T, topo):
         send(prv, ln, olist, "ao" + s, "ol" + s, spare=BULK[2])
         send(nxt, lv, olist, "av" + s, "ol" + s, spare=BULK[2])
         if first:
-            sel(T.kn[:], T.zb[:, 0:520], [[-16, 13], [-1, 10], [0, 4]], A.not_equal, -1.0, 0, 1, "zb", "kn")
+            sel(T.kr[:], T.zb[:, 0:130], [[-16, 13], [-1, 10]], A.not_equal, 1.0, 0, 1, "zb", "kr")
             for i in range(4):
-                sel(sg(i, SLOT[i], 130), T.zb[:, 0:130], [[-16, 13], [-1, 10]], A.not_equal, 1.0, 0, 1, "zb",
-                    "sg%d%d sg%d%d" % (i, SLOT[i], i + 1, SLOT[i]))
+                (cp if LIGHT[1] else sc)(sg(i, SLOT[i]), T.kr[:, 0:128], "kr", "sg%d%d" % (i, SLOT[i]))
+                if LIGHT[2]:
+                    ts(T.kn[:, i:512:4], T.kr[:, 0:128], -1.0, None, MUL, None, "kr", "kn%d" % i)
+                else:
+                    af(T.kn[:, i:512:4], T.kr[:, 0:128], -1.0, 0.0, "kr", "kn%d" % i)
             qc(K0, 0, 4, " ".join(staged(i, range(4)) for i in range(4)), "qK")
+            ops[-1]["spare"] = SPARE[1]
             consts_court()
         pick32(T.mk, pl, "mk pl" + s, "ms", T.sa, "sa")
         sc(T.mn[:], ps[1][:, 0:C], "ps1", "mn")
@@ -658,35 +689,36 @@ def rank_program(g, core, T, topo):
         if first:
             for h in range(3):
                 clear_co(h)
-            clear(T.w2, 0, 832, "w20 w21")
-            for h in chains:
-                clear(T.st, 512 * h, 512 * h + 4 * nq, "st%d0 st%d1 st%d2" % (h, h, h))
-                if SPLIT[0]:
-                    clear(T.xs, 512 * h + 320, 512 * h + 512, "xs%d0" % h)
+            clear(T.w2[:], "w20 w21 w22 w23")
+            clear(T.st[:], "st00 st01 st02 st10 st11 st12")
+            for h in chains if SPLIT[0] else ():
+                clear(T.xs[:, 512 * h + 320:512 * h + 512], "xs%d0" % h)
             iota(T.r8[:], [[0, 16], [1, 8]], 0, 0, "r8")
             iota(T.lr[:], [[1, 16], [0, 8]], 0, 0, "lr")
             iota(T.bs[:], [[16, 2], [0, 8], [32, 10]], 0, 0, "bs")
             consts_weights()
-            qz("c", 128 * KN, 128 * MX, T.kn[:, 0:512], "kn", "qKN")
+            qz("c", 128 * KN, 128 * MX, T.kn[:, 0:512], "kn0 kn1 kn2 kn3", "qKN")
         for h in chains:
             ms(T.xs[:, 512 * h:512 * h + 4 * nv:2], 0.0, "xs%d0 xs%d2" % (h, h))
         for b in range(4):
             decode("n" + s, "n" + s, b, (0, 1, 2, 7)[b], plane(T.vp, b), "vp%d" % b)
             sc(plane(T.vo, b), plane(T.vp, b).indirect(ln), "vp%d ln%s" % (b, s), "vo%d" % b)
+        def held(h, bank, bias):
+            for t in (1, 3):
+                weigh(T.xs[:, wide * h + t:wide * h + 320:4], bank, bias, "xw%d%d" % (h, t))
+
         for h in range(2):
             wins(h, 3 + h)
-            for t in (1, 3):
-                a = (512 if SPLIT[0] else 320) * h
-                weigh(T.xs[:, a + t:a + 320:4], 3 + h, "bw", "xw%d%d" % (h, t))
+            held(h, 3 + h, "bw")
             weigh(T.wp[:, 80 * h:80 * h + 80], 3 + h, "bx", "wp%d" % h)
         tt(T.d0[:, 256:384], T.sn[:].indirect(sub("bl", 16, 24)), T.aex[:, 256:384], A.subtract, "sn bl1 aex2", "d02")
         act(T.dd[:, 256:384], T.d0[:, 256:384], F.Abs, "d02", "dd2")
         wins(2, 2)
         for h in range(2):
             for t in range(2):
-                weigh(slot(T.w2, t, 80 * h, 80 * h + 80), 2, "u%d" % h, "w2%d" % t)
-            weigh(T.wp[:, NB + 80 * h:NB + 80 * h + 80], 2, "u%d" % (h + 2), "wp2")
-        qz("w2", 0, 208, T.w2[:], "w20 w21", "w2q")
+                weigh(slot(T.w2, t, 80 * h, 80 * h + 80), 2, "u%d" % h, "w2%d" % (2 * h + t))
+            weigh(T.wp[:, NB + 80 * h:NB + 80 * h + 80], 2, "u%d" % (h + 2), "wp%d" % (2 + h))
+        qz("w2", 0, 208, T.w2[:], "w20 w21 w22 w23", "w2q")
         if first:
             dma("Y", T.lwc[:].bitcast(dt.uint8), T.wc[:], "wp1", "wq")
             dma("Y", T.lws[:], T.ws[:], "wp1", "wsc")
@@ -710,16 +742,30 @@ def rank_program(g, core, T, topo):
         for k in range(SW):
             for h in chains:
                 x, lb, ub = ("xs", 128 * h), 5 + h, (7, 0)[h] if SPLIT[0] else (7, 0)[k % 2]
-                tile("xs", T.xs, h, "xs%d0 xs%d2 xw%d1 xw%d3" % (h, h, h, h) + ("" if SPLIT[0] else " xw11 xw13"), "xq%d" % h)
+                if k == 0 and FIRST[0]:
+                    js = (h,) if SPLIT[0] else (0, 1)
+                    for j in js:
+                        tt(T.st[:, 512 * j:512 * j + 512:4], T.cot[:, 1024 * j:1024 * j + 512].indirect(sub("zl")), T.er[:], EQ,
+                           " ".join("co%d%d ct%d%d" % (2 * j, t, 2 * j, t) for t in range(4)) + " zl er", "st%d0 zz%d" % (h, j))
+                    qz("s2", 128 * h, 128 * (js[-1] + 1), T.st[:, 512 * h:512 * (js[-1] + 1)],
+                       "st%d0 st%d1 st%d2 " % (h, h, h) + " ".join("zz%d" % j for j in js), "s2q%d" % h)
+                    for j in js:
+                        a = wide * j
+                        mm(5 + j, 128, ("s2", 128 * j), ct(K0), True, True, "qK s2q%d" % h)
+                        tt(T.xs[:, a:a + 320:4], ps[5 + j][:, 0:80], T.xs[:, a + 1:a + 320:4], MUL, "ps%d xw%d1 xs%d0" % (5 + j, j, h),
+                           "xf%d" % j)
+                    continue
+                tile("xs", T.xs, h, "xs%d0 xs%d2 xw%d1 xw%d3 xf%d" % (h, h, h, h, h) + ("" if SPLIT[0] else " xw11 xw13 xf1"), "xq%d" % h)
                 if k == SW - 1:
                     continue
                 mm(lb, nq, ct(MX), x, True, True, "qMX xq%d" % h)
-                tt(T.ys[:, ys(h, 0)], ps[lb][:, 0:nv], T.wp[:, ys(h, 0)], A.min, "ps%d wp%d" % (lb, h) + ("" if SPLIT[0] else " wp1"), "ys%d0" % h)
+                w = "wp"
+                tt(T.ys[:, ys(h, 0)], ps[lb][:, 0:nv], T[w][:, ys(h, 0)], A.min, "ps%d wp%d" % (lb, h) + ("" if SPLIT[0] else " wp1"), "ys%d0" % h)
                 ts(part(T.xs, h, 0), T.ys[:, ys(h, 0)], 0.0, SIG, A.max, MUL, "ys%d0" % h, "xs%d0" % h)
                 if k >= 7:
                     mm(ub, nq, ct(MX + 2), ("w2", 80 * h), True, False, "qMU_ w2q")
                     mm(ub, nq, ct(MX + 1), x, False, True, "qMU_ xq%d" % h)
-                    tt(T.ys[:, ys(h, 1)], ps[ub][:, 0:nv], T.wp[:, ys(h, 1)], A.min, "ps%d wp2" % ub, "ys%d1" % h)
+                    tt(T.ys[:, ys(h, 1)], ps[ub][:, 0:nv], T.wp[:, ys(h, 1)], A.min, "ps%d wp2 wp3" % ub, "ys%d1" % h)
                     ts(part(T.xs, h, 2), T.ys[:, ys(h, 1)], 0.0, SIG, A.max, MUL, "ys%d1" % h, "xs%d2" % h)
         for h in chains:
             for t in range(2):
@@ -735,9 +781,10 @@ def rank_program(g, core, T, topo):
         places(MI, (3, 1), "mt", sub("hl" + s, 0, 32), "hl" + s)
         send(nxt, lh, hl, "ah" + s, "hl" + s)
         places(MU, (4, 2), "mt2", sub("mu", 0, 32), "mu")
-        for hf in range(2):
+        runs = ((0, 1), (1, 2)) if RUNS[r] == 2 else ((0, 2),)
+        for hf, hi in runs:
             for b in range(4):
-                mm(HB[hf][b], H, et(b), (xq, H * hf), True, False, "qE " + xk)
+                mm(HB[hf][b], H * (hi - hf), et(b), (xq, H * hf), True, False, "qE " + xk)
         for b in range(4):
             (cp if PICK[0][b] == "V" else sc)(plane(T.vq, b), plane(T.vo, b).indirect(sub("mu")), "vo%d mu" % b, "vq%d" % b)
             if PICK[2][b] == "F":
@@ -759,30 +806,29 @@ def rank_program(g, core, T, topo):
                     (cp if PICK[2][b] == "V" else sc)(out, src, "zp%d pl%s" % (b, s), W)
         if final:
             (cp if OLE[1] == "V" else sc)(T.wro2[:], T.wrow[:].indirect(pl), "wrow pl" + s, "wro2")
-            for k in range(8):
-                dma("Y", T.ol[k:k + 1, :], T.wro2[16 * k:16 * k + 1, :], "wro2", "")
-        for hf in range(2):
-            qz("z", H * hf, H * hf + H, T.zt[:, 4 * H * hf:4 * H * (hf + 1)], " ".join("zt%d%d" % (hf, b) for b in range(4)), "zq%d" % hf)
+            dma("Y", T.ol[:], T.wro2[0:128:16, :], "wro2", "")
+        for hf, hi in runs:
+            lo, n = H * hf, H * (hi - hf)
+            qz("z", lo, lo + n, T.zt[:, 4 * lo:4 * (lo + n)], " ".join("zt%d%d" % (j, b) for j in range(hf, hi) for b in range(4)), "zq%d" % hf)
             for b in range(4):
-                mm(HB[hf][b], H, ("lw", 128 * b), ("z", H * hf), False, True, "wq wsc zq%d" % hf)
+                mm(HB[hf][b], n, ("lw", 128 * b), ("z", lo), False, True, "wq wsc zq%d" % hf)
         xq = "x%d" % (r + 1)
-        for hf in range(2):
+        for hf, hi in runs:
+            lo, n, key = H * hf, H * (hi - hf), " ".join(xq + "ab"[j] for j in range(hf, hi))
             for b in range(4):
-                o, bank = slot(T.xn, b, H * hf, H * hf + H), HB[hf][b]
-                if b % 2:
-                    ts(o, ps[bank][:, 0:H], 1.0 / 32, None, MUL, None, "ps%d" % bank, "xn%d%d" % (hf, b))
+                o, bank, W = slot(T.xn, b, lo, lo + n), HB[hf][b], " ".join("xn%d%d" % (j, b) for j in range(hf, hi))
+                if XN[hf][b] == "V":
+                    ts(o, ps[bank][:, 0:n], 1.0 / 32, None, MUL, None, "ps%d" % bank, W)
                 else:
-                    act(o, ps[bank][:, 0:H], F.Copy, "ps%d" % bank, "xn%d%d" % (hf, b), scale=1.0 / 32)
-            qz(xq, H * hf, H * hf + H, T.xn[:, 4 * H * hf:4 * H * (hf + 1)], " ".join("xn%d%d" % (hf, b) for b in range(4)), xq + "ab"[hf])
+                    act(o, ps[bank][:, 0:n], F.Copy, "ps%d" % bank, W, scale=1.0 / 32)
+            qz(xq, lo, lo + n, T.xn[:, 4 * lo:4 * (lo + n)], " ".join("xn%d%d" % (j, b) for j in range(hf, hi) for b in range(4)), key)
             if final:
-                mm(hf, H, ("v", 0), (xq, H * hf), True, True, "vq " + xq + "ab"[hf])
-                dma("Y", T.oc[:, 4 * H * hf:4 * H * (hf + 1)], T[xq + "c"][:, H * hf:H * hf + H].bitcast(dt.uint8), xq + "ab"[hf], "")
+                mm(hf, n, ("v", 0), (xq, lo), True, True, "vq " + key)
+                dma("Y", T.oc[:, 4 * lo:4 * (lo + n)], T[xq + "c"][:, lo:lo + n].bitcast(dt.uint8), key, "")
+                (cp if hi == 2 or OUT[0] == "V" else sc)(T.sq[:, lo:lo + n], ps[hf][:, 0:n], "ps%d sq" % hf, "yb%d" % hf)
+                dma("Y", T.y[:, lo:lo + n], T.sq[:, lo:lo + n], "yb%d" % hf, "")
         if not final:
             send_q(prv, xq, "n%d" % (r + 1), "an%d" % (r + 1), "%sa %sb" % (xq, xq))
-    sc(T.sq[:, 0:H], ps[0][:, 0:H], "ps0 sq", "yb0")
-    cp(T.sq[:, H:C], ps[1][:, 0:H], "ps1 sq", "yb1")
-    for hf in range(2):
-        dma("Y", T.y[:, H * hf:H * hf + H], T.sq[:, H * hf:H * hf + H], "yb%d" % hf, "")
     for k in range(4):
-        dma("S", T.osc[4 * k:4 * k + 4, :], T[xq + "s"][32 * k:32 * k + 4, :], "%sa %sb" % (xq, xq), "")
+        dma(OUT[1] if k % 2 else "S", T.osc[4 * k:4 * k + 4, :], T[xq + "s"][32 * k:32 * k + 4, :], "%sa %sb" % (xq, xq), "")
     emit(g, T, ops)

import math
from concourse.mybir import dt, AluOpType, AxisListType, ActivationFunctionType

A = AluOpType
F = ActivationFunctionType
C, NR, SW, NB = 320, 2, 12, 160
BIG = 1.0e29
CW, GW, GU, SIG = 2.0 ** 13, 2.0 ** 16, 2.0 ** 8, 16.0
LN2 = math.log(2.0)
X4, U8, BF, F32, I32, U16 = "float8_e4m3fn_x4", "uint8", "bfloat16", "float32", "int32", "uint16"
WB, E0, K0, KN, MX, SS, MU, FA, MI, NT = 0, 1, 5, 9, 10, 13, 15, 16, 17, 18
SLOT = (0, 2, 1, 3)
SOFF, SWID = [0, 320, 576, 768, 896], [320, 256, 192, 128, 128]
DL, DU = ((1, 2, 3, 4), (5, 6, 7, 8)), ((1, 2, 3, 4),)
POOL = ["ct1", "ct3", "ct4", "w20", "st0"]
PICK = ["VVSV", "VVVS", "SSSF"]
LOW, FEW = [18, 18], [6, 6]
DIAG = [1, 1]
PIECES, AEX, WHOLE, OLE = [(0, 20)], [0], [1, 1, 0, 0], ["S", "S"]
FIRST, OUT, SPARE = [1], ["V", "S"], [0, 0]
LIGHT = [0, 0, 0]
LISTS = set("uoff ky al bl tl mu pl px xy ol ln lv lh zl ey".split())
START, WAKE, PASSES = {"V": 5, "S": 110, "P": 30, "G": 10, "Y": 0, "A": 0}, [190, 230], 4
BULK = [3000, 3000, 5000, 7000]
PE = [0.5, 1.8, 2.4, 1800, 4500]
BOTH = [4]
SPLIT = [1]
XN, LAST, MB = ["SVSV", "SVSV"], [0], ["SSVV"]
RUNS = [2, 2]
JIT = [0]
AHEAD = [1500, 500, 1000, 0, 0]
BEFORE = {}
LB, UB, HB = 5, (6, 7), ((0, 1, 4, 5), (6, 7, 2, 3))

SCRATCH, SUB, ORDER = {}, {}, []


def _b(names, n, d):
    for s in names.split():
        SCRATCH[s] = ("sbuf", [128, n], d)


def _q(names, n):
    for s in names.split():
        SCRATCH[s + "c"] = ("sbuf", [128, n], X4)
        SCRATCH[s + "s"] = ("sbuf", [128, n], U8)


def _s(buf, names, d):
    for i, s in enumerate(names.split()):
        SUB[s] = (buf, 32 * i, {"uoff": 16, "al": 24, "bl": 24, "ky": 16, "tl": 2, "zl": 8}.get(s, 20))
    _b(buf, 32 * len(names.split()), d)


_b("xt at zt xn vp vo vq gp go zp", 4 * C, BF)
_b("ut vt", 512, BF)
_b("kn zb", 520, BF)
_b("w2", 832, BF)
_b("xs st", 1024, BF)
_b("vg", 4 * C, BF)
_b("sg", 2064, BF)
_b("ys dg", C, BF)
_b("sot", 4096, BF)
_b("cot", 2560, BF)
_b("dd", 384, F32)
_b("jk", 3400, BF)
_b("m16 k16 k01 pen k10 e10 ru e16 r16 r10 wp", C, BF)
_b("iot mk mn sb ls sa sn sq orow onr wrow wro2", C, F32)
_b("aex d0", 384, F32)
_b("wr r8 lr", 128, BF)
_b("psr pir a1 a2", 256, BF)
_b("bt", 512, BF)
_b("fa", 512, BF)
_b("fb", 768, BF)
_b("mt mt2 bs", NB, F32)
_b("er", 128, BF)
_b("kr", 130, BF)
_b("ms mst m2 m2t", C, F32)
_b("pi", 8, I32)
_b("pf", 64, F32)
_b("li", 96, I32)
_b("kf", 128, F32)
_s("sf", "rs pre cbs fx", F32)
_s("si", "pli j32 j10", I32)
_s("of", "uoff al bl ky tl mu xy zl ey", U16)
_s("snd", "pl0 pl1 ol0 ol1 hl0 hl1", U16)
_s("lnd", "lp0 lp1 ln0 ln1 lv0 lv1 lh0 lh1", U16)
_q("lw", 512)
_q("u v", 128)
_q("xs st s2", 256)
_q("w2", 208)
_q("up", 256)
_q("x0 x1 x2 g0 g1 n0 n1 p0 p1 z", C)
_q("c", 128 * NT)
_q("so", 1024)
_q("co", 1408)
for _i in range(8):
    SCRATCH["b%d" % _i] = ("psum", [128, 512], F32)
SEMAPHORES = ["V", "S", "P", "G", "loc"] + ["d%d" % i for i in range(32)] + \
             [a + str(r) for r in range(NR) for a in ("an", "ap", "al", "ao", "av", "ah")]


def arrange(ops, deps):
    n = len(ops)
    t = [o["t"] + START[o["e"]] for o in ops]

    def after(j, i):
        if ops[j]["e"] == ops[i]["e"] and (ops[j]["e"] == "P" or ops[j]["k"] == "r"):
            return t[j]
        return t[j] + ops[j].get("late", 0) + (0 if ops[j]["k"] == "r" else WAKE[ops[j]["e"] == ops[i]["e"]])

    chain = [t[i] + ops[i].get("late", 0) for i in range(n)]
    for i in range(n - 1, -1, -1):
        for j in deps[i]:
            chain[j] = max(chain[j], after(j, i) + ops[j].get("spare", 0) + chain[i])
    users = [[] for _ in range(n)]
    for i in range(n):
        for j in deps[i]:
            users[j].append(i)

    def place(order, earliest):
        start, held = [0.0] * n, {e: [] for e in START}
        for i in order:
            s, h = earliest(i, start), held[ops[i]["e"]]
            k = len(h)
            while k and h[k - 1][1] > s:
                k -= 1
            while k < len(h) and s + t[i] > h[k][0]:
                s = max(s, h[k][1])
                k += 1
            start[i] = s
            h.insert(k, (s, s + t[i]))
        return start

    def early(i, start):
        return max([start[j] + after(j, i) for j in deps[i]], default=0.0)

    def late(j, back):
        return max([back[i] + t[i] - t[j] + after(j, i) + ops[j].get("spare", 0) for i in users[j]], default=ops[j].get("late", 0))

    best, key = None, [-c for c in chain]
    for _ in range(PASSES):
        start = place(sorted(range(n), key=lambda i: (key[i], i)), early)
        end = max(start[i] + t[i] + ops[i].get("late", 0) for i in range(n))
        if best is None or end < best[0]:
            best = (end, start)
        back = place(sorted(range(n), key=lambda i: (-start[i], -i)), late)
        key = [-back[i] - t[i] for i in range(n)]
        if JIT[0] and _ % 2:
            for i in range(n):
                key[i] = max([key[i] + JIT[0] * ((i * 7919 + _ * 104729) % 1000 / 500 - 1)] + [key[j] + 1 for j in deps[i]])
    return sorted(range(n), key=lambda i: (best[1][i], i))


def emit(g, T, ops):
    Q = {"V": g.vector, "S": g.scalar, "P": g.tensor, "G": g, "Y": g.sync}
    lastw, readers, deps = {}, {}, []
    for i, o in enumerate(ops):
        d = set()
        for k in o["R"]:
            if k in lastw:
                d.add(lastw[k])
            if k.startswith("ps"):
                d.update(j for j in readers.get(k, []) if ops[j]["e"] != o["e"])
        for k in o["W"]:
            if k in lastw:
                d.add(lastw[k])
            d.update(readers.get(k, []))
        for k in o["R"]:
            readers.setdefault(k, []).append(i)
        for k in o["W"]:
            lastw[k] = i
            readers[k] = []
        d.discard(i)
        deps.append(d)
    if not ORDER:
        ORDER.extend(arrange(ops, deps))
    order = ORDER
    at = {j: i for i, j in enumerate(order)}
    ops, deps = [ops[j] for j in order], [[at[k] for k in deps[j]] for j in order]
    deps = [[j for j in d if ops[j]["k"] != "r" and not (o["e"] == "P" and ops[j]["e"] == "P")] for o, d in zip(ops, deps)]
    ev, cnt, nd, tot = [], {}, [0], {}
    for o in ops:
        if o["k"] == "c":
            cnt[o["e"]] = cnt.get(o["e"], 0) + 1
            ev.append((o["e"], cnt[o["e"]]))
        elif o["k"] == "d":
            ev.append(("d%d" % nd[0], 16))
            nd[0] += 1
        elif o["k"] == "a":
            ev.append((o["sem"], o["n"]))
        else:
            ev.append(None)
    known = {e: {} for e in Q}
    clock, waits, need = [], [], set()
    for i, o in enumerate(ops):
        if o["k"] == "a":
            clock.append({ev[i][0]: ev[i][1]})
            waits.append([])
            continue
        kn, w = known[o["e"]], []
        for j in sorted(deps[i], reverse=True):
            s, v = ev[j]
            if kn.get(s, 0) < v:
                w.append(j)
                need.add(j)
                for s2, v2 in clock[j].items():
                    kn[s2] = max(kn.get(s2, 0), v2)
        waits.append(w)
        c = dict(kn)
        if ev[i] is not None:
            c[ev[i][0]] = max(c.get(ev[i][0], 0), ev[i][1])
        clock.append(c)
    last = {}
    for i, o in enumerate(ops):
        if o["k"] == "c":
            last[o["e"]] = i
    need.update(last.values())
    val, n = {}, {}
    for i, o in enumerate(ops):
        if o["k"] == "c":
            if i in need:
                n[o["e"]] = n.get(o["e"], 0) + 1
                val[i] = n[o["e"]]
        elif ev[i] is not None:
            val[i] = ev[i][1]
    for i, o in enumerate(ops):
        if o["k"] == "a":
            tot[o["sem"]] = o["n"]
            continue
        q = Q[o["e"]]
        for j in waits[i]:
            q.wait_ge(T.sem[ev[j][0]], val[j])
        ins = o["f"](q)
        if o["k"] == "c" and i in need:
            ins.then_inc(T.sem[o["e"]], 1)
            tot[o["e"]] = val[i]
        elif o["k"] == "d":
            ins.then_inc(T.sem[ev[i][0]], 16)
            tot[ev[i][0]] = 16
        elif o["k"] == "r":
            tot["loc"] = tot.get("loc", 0) + o["n"]
    for s, v in tot.items():
        g.wait_ge(T.sem[s], v)


def rank_program(g, core, T, topo):
    rank = T.rank_of(core)
    if rank is None:
        return
    n_ranks = len(T.cores)
    nxt, prv = T.cores[(rank + 1) % n_ranks], T.cores[(rank - 1) % n_ranks]
    ops, bgq = [], []

    def op(e, f, R, W, t, k="c", **kw):
        ops.append(dict(e=e, f=f, R=R.split(), W=W.split(), t=t, k=k, **kw))

    def span(R, *aps, rate=1.0):
        n = math.prod(aps[0].shape[1:])
        if LISTS.intersection(a.rstrip("01") for a in R.split()):
            return 60 + n * (PE[2] if "px" in R else PE[1])
        if rate == 1.0 and all("bfloat16" in str(a.dtype) for a in aps):
            rate = 0.5
        return max(64, n * rate)

    def ts(out, in0, s1, s2, o0, o1, R, W):
        if s2 is None:
            op("V", lambda q: q.tensor_scalar(out, in0, s1, None, o0), R, W, span(R, out, in0))
        else:
            op("V", lambda q: q.tensor_scalar(out, in0, s1, s2, o0, o1), R, W, span(R, out, in0))

    def tt(out, a, b, o, R, W):
        op("V", lambda q: q.tensor_tensor(out, a, b, o), R, W, span(R, out, rate=1.01 if "ps" in R else 2.0))

    def cp(out, a, R, W):
        op("V", lambda q: q.tensor_copy(out, a), R, W, span(R, a if "px" in R else out, rate=1.01))

    def ms(out, c, W):
        op("V", lambda q: q.memset(out, c), "", W, span("", out))

    def scan(out, d0, d1, init, o0, o1, R, W):
        op("V", lambda q: q.tensor_tensor_scan(out, d0, d1, init, o0, o1), R, W, span(R, out, d0, d1))

    def qz(name, a, b, src, R, W):
        op("V", lambda q: q.quantize_mx(T[name + "c"][:, a:b], T[name + "s"][:, a:b], src), R, W, 15 + 1.06 * (b - a))

    def act(out, a, func, R, W, **kw):
        load = 1600 if W == "_nz" else 0
        op("S", lambda q: q.activation(out, a, func, **kw), R, W, span(R, out, rate=1.01) + load)

    def af(out, a, scale, bias, R, W):
        act(out, a, F.Identity, R, W, scale=scale, bias=bias)

    def sc(out, a, R, W):
        act(out, a, F.Copy, R, W)

    def zero(buf, a, b, W, step=1):
        sc(buf[:, a:b:step], T.zb[:, 0:(b - a + step - 1) // step], "zb", W)

    def pick(dst, a, src, b, w, off, n, R, W):
        cp(T[dst + "c"][:, a:a + n].bitcast(dt.uint32), T[src + "c"][:, b:b + w].bitcast(dt.uint32).indirect(off), R, W + "c")
        sc(T[dst + "s"][:, a:a + n], T[src + "s"][:, b:b + w].indirect(off), R, W + "s")

    def mm(bank, n, lhs, rhs, start, stop, R):
        (ln, la), (rn, ra) = lhs, rhs
        op("P", lambda q: q.matmul_mx(T["b%d" % bank][:, 0:n], T[ln + "c"][:, la:la + 128], T[ln + "s"][:, la:la + 128],
                                      T[rn + "c"][:, ra:ra + n], T[rn + "s"][:, ra:ra + n], start, stop), R, "ps%d" % bank,
           PE[0] * (n + 16))

    def dma(e, out, a, R, W, late=2400):
        op(e, lambda q: q.dma_start(out, a), R, W, 70, k="d", late=late)

    def iota(out, pat, base, cm, W, small=True):
        if small:
            op("G", lambda q: q.iota(out, pat, base, cm, allow_small_or_imprecise_dtypes=True), "", W, 160 + 2 * out.shape[1])
        else:
            op("G", lambda q: q.iota(out, pat, base, cm), "", W, 160 + 2 * out.shape[1])

    def sel(out, a, pat, o, fill, base, cm, R, W):
        op("G", lambda q: q.affine_select(out, a, pat, o, fill, base, cm), R, W, 200 + 2 * out.shape[1])

    def send(dst, out, a, sem, R, late=0, t=300, spare=0):
        late = late or PE[3]
        rid, pid, _ = topo.addr(dst)
        m = topo.mask(core, dst)
        op("G", lambda q: q.remote_dma(out, a, T.sem[sem], T.sem.loc, pid, rid, m), R, "#" + sem, t, k="r", late=late, spare=spare,
           n=len(topo.engines(core, dst)))

    def send_q(dst, src, land, sem, R, t=300):
        send(dst, T[land + "c"][:].bitcast(dt.uint8), T[src + "c"][:].bitcast(dt.uint8), sem, R, 4400, t)
        send(dst, T[land + "s"][:], T[src + "s"][:], sem, R, BULK[3], 300, BULK[src[0] == "g"])

    def arrive(src, sem, calls, W):
        op("A", None, "#" + sem, W, 0, k="a", sem=sem, n=calls * len(topo.engines(src, core)))

    def bg(n=1):
        for _ in range(min(n, len(bgq))):
            bgq.pop(0)()

    def L(f, *a, **kw):
        f(*a, **kw)

    def sub(name, a=0, b=None):
        buf, o, n = SUB[name]
        return T[buf][:, o + a:o + (n if b is None else b)]

    def ct(i):
        return ("c", 128 * i)

    def sg(i, t, n=128):
        return T.sg[:, 512 * i + t:512 * i + 4 * n:4]

    def staged(i, slots):
        return " ".join("sg%d%d" % (i, t) for t in slots)

    def qc(i, j, n, R, W):
        qz("c", 128 * i, 128 * (i + n), T.sg[:, 512 * j:512 * (j + n)], R, W)

    def slot(buf, t, a=0, b=NB):
        return buf[:, 4 * a + t:4 * b:4]

    def plane(buf, b, lo=0, hi=C):
        return buf[:, C * b + lo:C * b + hi]

    ps = [T["b%d" % i] for i in range(8)]
    pi, pf, li, kf = T.pi, T.pf, T.li, T.kf
    SH, AND, EQ, MUL, ADD = A.logical_shift_right, A.bitwise_and, A.is_equal, A.mult, A.add
    H = C // 2
    chains, nq, nv, wide = ((0, 1), 128, 80, 512) if SPLIT[0] else ((0,), NB, NB, 320)

    names = ("p g l8 p3 p1 q l7 aw ax s hb s4 s2 c1 c2 c3 lB sB iA iB z nz cn gn cz co s16 vl vu alo blo alu blu tl t0 t1 t2 cb o0 fx "
             "t3 t4 t5 t6 t7 bw bx l15 u0 u1 u2 u3 th fl fu fs").split()

    def pc(name, n=1):
        i = names.index(name)
        return pf[:, i:i + n]

    def lin(name, src, k, add, e="S"):
        a, R = (pc(add), "_%s _%s" % (src, add)) if isinstance(add, str) else (float(add), "_" + src)
        if e == "S":
            af(pc(name), pc(src), float(k), a, R, "_" + name)
        else:
            ts(pc(name), pc(src), float(k), a, MUL, ADD, R, "_" + name)

    dma("Y", T.xt[:], T.x[:], "", "xt", PE[4])
    dma("S", T.ut[:], T.u[:], "", "ut")
    iota(pi[:, 0:1], [[0, 1]], 0, 1, "pi0", False)
    iota(T.r16[:], [[0, 20], [1, 16]], 0, 0, "r16")
    iota(T.wr[:], [[1, 8], [0, 16]], 0, 0, "wr")
    iota(li[:, 0:16], [[1, 2], [16, 8]], 0, 0, "li0", False)
    iota(li[:, 16:36], [[16, 20]], 0, 0, "li1", False)
    ms(T.zb[:], 0.0, "zb")
    for c, s, m in ((1, 4, 7), (2, 3, 15), (3, 0, 3), (4, 0, 1), (5, 0, 15), (6, 6, 1)):
        ts(pi[:, c:c + 1], pi[:, 0:1], s, m, SH, AND, "pi0", "pi%d" % c)
    cp(pc("p", 7), pi[:, 0:7], "pi0 pi1 pi2 pi3 pi4 pi5 pi6", "_p _g _l8 _p3 _p1 _q _l7")
    for u in range(4):
        zero(T.sot, 4 * (SOFF[u] + SWID[u] - 48), 4 * (SOFF[u] + SWID[u]), "sz%d" % u)
    zero(T.sot, 4 * SOFF[4], 4096, "sz4")
    ts(T.e16[:], T.r16[:], pc("q"), None, EQ, None, "r16 _q", "e16")
    ts(T.k01[:], T.r16[:], 0.0, None, A.is_gt, None, "r16", "k01")
    for t in range(4):
        ts(T.fa[:, t:512:4], T.wr[:], pc("g"), None, EQ, None, "wr _g", "wb%d" % t)
    cp(sub("uoff"), li[:, 0:16], "li0", "uoff")
    af(T.m16[:], T.e16[:], 2 * BIG, -BIG, "e16", "m16")
    af(T.k16[:], T.k01[:], 2 * BIG, -BIG, "k01", "k16")
    af(T.pen[:], T.e16[:], -1049600.0, 1024.0, "e16", "pen")
    qz("c", 128 * WB, 128 * E0, T.fa[:], "wb0 wb1 wb2 wb3 fa0 fa1 fa2", "qWB")
    for n, s, k, a in (("s", "l8", -8, "p"), ("hb", "g", -2, "l8"), ("s2", "p1", -1, "p3"), ("cb", "q", 1023, 15 - 15360),
                       ("o0", "q", 1024, -15360), ("s4", "p3", -1, "s"), ("alo", "hb", 10, 9),
                       ("blo", "s", 10, 9), ("t0", "hb", 160, 9), ("c1", "s2", -2, 2), ("t1", "s", -30, 249)):
        lin(n, s, k, a, "V")
    qz("u", 0, 128, T.ut[:], "ut", "uq")
    for n, s, k, a in (("t2", "p1", -2, "s"), ("s16", "s", 16, 0), ("sB", "s", 1, 8), ("iA", "l8", 16, "s")):
        lin(n, s, k, a, "V")
    pick("up", 0, "u", 0, 128, sub("uoff", 0, 8), 128, "uq uoff", "up0")
    pick("up", 128, "u", 0, 128, sub("uoff", 8, 16), 128, "uq uoff", "up1")
    for n, s, k, a in (("c2", "s4", -2, 4), ("c3", "hb", -16, "t1"), ("vl", "hb", 16, "t2"), ("vu", "s4", 32, "t2")):
        lin(n, s, k, a, "V")
    for n, s, k, a in (("alu", "s4", 20, "t0"), ("blu", "s", 10, "t0"), ("lB", "s4", 2, "g"), ("iB", "lB", 16, "sB")):
        lin(n, s, k, a, "S")
    iota(li[:, 52:60], [[0, 4], [1, 2]], 0, 0, "li3", False)
    iota(li[:, 60:68], [[0, 2], [1, 2], [0, 2]], 0, 0, "li4", False)
    iota(li[:, 68:76], [[0, 2], [1, 4]], 0, 0, "li5", False)
    iota(li[:, 76:84], [[1, 4], [0, 2]], 0, 0, "li6", False)
    iota(li[:, 36:52], [[160, 2], [0, 8]], 0, 0, "li2", False)
    iota(T.r10[:], [[0, 32], [1, 10]], 0, 0, "r10")
    ts(kf[:, 0:16], li[:, 52:68], pc("p1"), pc("c1"), EQ, MUL, "li3 li4 _p1 _c1", "k0")
    ts(kf[:, 40:48], li[:, 76:84], pc("p3"), 8.0, A.not_equal, MUL, "li6 _p3", "k3")
    ts(pc("z"), pc("g"), pc("s"), None, EQ, None, "_g _s", "_z")
    ts(kf[:, 16:32], li[:, 68:84], pc("p3"), pc("c2"), EQ, MUL, "li5 li6 _p3 _c2", "k1")
    ts(kf[:, 32:40], li[:, 16:24], pc("s16"), pc("c3"), EQ, MUL, "li1 _s16 _c3", "k2")
    ts(kf[:, 48:56], li[:, 16:24], 2.0, pc("vl"), MUL, ADD, "li1 _vl", "k4")
    ts(kf[:, 56:64], li[:, 16:24], pc("vu"), None, ADD, None, "li1 _vu", "k5")
    for b in range(4):
        if b == 1:
            qz("x0", 0, C, T.xt[:], "xt", "x0a x0b")
            send_q(prv, "x0", "n0", "an0", "x0a x0b", 2700)
        if b < LIGHT[0]:
            ms(T.sg[:, 512 * b:512 * b + 512], 0.0, staged(b, range(4)))
            sel(sg(b, SLOT[b]), T.zb[:, 0:128], [[1, 128]], A.not_equal, 32.0, 0, -1, "zb", staged(b, [SLOT[b]]))
        else:
            sel(T.sg[:, 512 * b:512 * b + 512], T.zb[:, 0:512], [[4, 128], [1, 4]], A.not_equal, 32.0, -SLOT[b], -4, "zb",
                staged(b, range(4)))
    iota(T.iot[:], [[1, C]], 0, 0, "iot")
    for i in range(6):
        qz("co", 256 * i, 256 * i + 128, T.zb[:, 0:512], "zb", "cz%d" % i)
    ms(sub("rs", 0, 1), 0.0, "rs0")
    lin("fx", "q", 1, -4.5, "V")
    ts(sub("fx"), li[:, 16:36], pc("fx"), 0.1, ADD, MUL, "li1 _fx", "fx")
    ts(sub("j32"), li[:, 16:36], pc("q"), 32.0, ADD, MUL, "li1 _q", "j32")
    cp(sub("j10"), sub("fx"), "fx", "j10")
    ts(sub("j10"), sub("j10"), -319.0, None, MUL, None, "j10", "j10")
    tt(sub("j32"), sub("j32"), sub("j10"), ADD, "j32 j10", "j32")
    cp(sub("xy"), sub("j32"), "j32", "xy")

    L(ts, sub("cbs"), li[:, 16:36], pc("cb"), None, ADD, None, "li1 _cb", "cbs")
    L(ts, sub("al", 0, 16), li[:, 16:32], 1.25, pc("alo"), MUL, ADD, "li1 _alo", "al0")
    L(ts, sub("al", 16, 24), li[:, 16:24], 0.625, pc("alu"), MUL, ADD, "li1 _alu", "al1")
    L(ts, T.e10[:], T.r10[:], pc("q"), None, EQ, None, "r10 _q", "e10")
    L(ts, T.k10[:], T.r10[:], 0.5, None, A.is_gt, None, "r10", "k10")
    L(ts, sub("bl", 0, 16), li[:, 36:52], pc("blo"), None, ADD, None, "li2 _blo", "bl0")
    L(ts, sub("bl", 16, 24), li[:, 36:44], pc("blu"), 80.0, ADD, ADD, "li2 _blu", "bl1")

    L(tt, kf[:, 64:96], kf[:, 0:32], kf[:, 32:64], ADD, "k0 k1 k2 k3 k4 k5", "k6")
    act(pc("nz"), pc("z"), F.Exp, "_z", "_nz", scale=-200.0)
    L(tt, kf[:, 96:112], kf[:, 64:80], kf[:, 80:96], ADD, "k6", "k7")
    lin("cn", "nz", CW, 0)
    lin("gn", "nz", CW * GW, 0)
    lin("cz", "z", CW, 0, "V")
    L(ts, sub("ky"), kf[:, 96:112], 1.0, None, ADD, None, "k7", "ky")
    lin("co", "z", -CW, -CW, "V")

    def consts_rows():
        sc(T.psr[:], T.r16[:].indirect(sub("ky")), "r16 ky", "psr")
        sc(T.pir[:], T.iot[:].indirect(sub("ky")), "iot ky", "pir")
        if FIRST[0]:
            lin("t6", "t2", 16, 16, "V")
            lin("t7", "hb", 1, -2, "V")
            ts(kf[:, 116:124], li[:, 16:24], pc("t6"), pc("t7"), EQ, MUL, "li1 _t6 _t7", "k9")
            ts(sub("ey", 0, 8), kf[:, 116:124], 2.0, None, ADD, None, "k9", "ey")
            sc(T.er[:], T.iot[:].indirect(sub("ey", 0, 8)), "iot ey", "er")
            ts(sub("zl"), li[:, 16:24], 4.25, None, MUL, None, "li1", "zl")

    def consts_court():
        for i in range(2):
            a, b = slice(128 * i, 128 * i + 128), slice(256 + 128 * i, 384 + 128 * i)
            ts(T.a1[:, a], T.psr[:, a], pc("s"), pc("cn"), EQ, MUL, "psr _s _cn", "a1%d" % i)
            ts(T.a2[:, a], T.pir[:, a], pc("iA"), pc("gn"), EQ, MUL, "pir _iA _gn", "a2%d" % i)
            ts(T.bt[:, a], T.psr[:, a], pc("s"), pc("cz"), EQ, MUL, "psr _s _cz", "b1%d" % i)
            ts(T.bt[:, b], T.pir[:, a], pc("iA"), pc("co"), EQ, MUL, "pir _iA _co", "b2%d" % i)
            tt(sg(i, 0), T.a1[:, a], T.a2[:, a], A.max, "a1%d a2%d" % (i, i), "sg%d0" % i)
            af(sg(i, 1), T.a2[:, a], -1.0, 0.0, "a2%d" % i, "sg%d1" % i)
            tt(sg(i, 3), T.bt[:, a], T.bt[:, b], ADD, "b1%d b2%d" % (i, i), "sg%d3" % i)
        ts(T.fa[:, 256:384], T.psr[:, 128:256], pc("sB"), CW, EQ, MUL, "psr _sB", "fa1")
        ts(T.fa[:, 384:512], T.pir[:, 128:256], pc("iB"), CW * GU, EQ, MUL, "pir _iB", "fa2")
        tt(sg(1, 2), T.fa[:, 256:384], T.fa[:, 384:512], A.max, "fa1 fa2 qE", "sg12")
        ts(sg(2, 0), T.pir[:, 128:256], pc("iB"), -CW * GU, EQ, MUL, "pir _iB qE", "sg20")
        ts(sg(2, 1), T.pir[:, 128:256], pc("iB"), -CW, EQ, MUL, "pir _iB qE", "sg21")
        qc(MX, 0, 1, staged(0, range(4)), "qMX")
        ops[-1]["spare"] = SPARE[0]
        qc(MX + 1, 1, 2, staged(1, range(4)) + " " + staged(2, range(4)), "qMU_")

    def consts_weights():
        for n, s, k, a in (("bw", "l7", LN2, 7 * LN2), ("bx", "l7", LN2, 7 * LN2 - math.log(SIG)), ("aw", "l7", LN2, 11 * LN2),
                           ("ax", "l7", LN2, 11 * LN2 - 200), ("u0", "hb", -200, "aw"), ("u1", "hb", 200, "ax"),
                           ("u2", "u0", 1, -math.log(SIG)), ("u3", "u1", 1, -math.log(SIG))):
            lin(n, s, k, a, "V")

    def consts_tail():
        for n, s, k, a in (("fl", "l8", -3, 1), ("fu", "lB", -3, 1), ("fs", "s", -2, 2), ("t3", "s", 4, 0), ("t4", "q", 0.5, 0),
                           ("th", "l8", -4, "t3"), ("t5", "g", 10, "t4"), ("tl", "p1", 79.5, "t5")):
            lin(n, s, k, a, "V")
        for j, (row, k, b) in enumerate(((T.lr, 3.0, "fl"), (T.lr, 3.0, "fu"), (T.r8, 2.0, "fs"))):
            act(T.fb[:, 128 * j:128 * j + 128], row[:], F.Relu, "lr r8 _" + b, "fb%d" % j, scale=k, bias=pc(b))
            act(T.fb[:, 384 + 128 * j:512 + 128 * j], T.fb[:, 128 * j:128 * j + 128], F.Relu, "fb%d" % j, "fc%d" % j, scale=-1.0, bias=4.0)
        for i, t in ((3, 3), (2, 0), (2, 1), (0, 3), (1, 1), (1, 3)):
            ms(sg(i, t), 0.0, "sg%d%d" % (i, t))
        ts(sg(3, 0), T.r8[:], pc("s"), 0.5 / SIG, EQ, MUL, "r8 _s qE", "sg30")
        ts(sg(2, 2), T.r8[:], pc("s"), 0.5 / SIG, EQ, MUL, "r8 _s", "sg22")
        qc(SS, 2, 2, staged(2, range(4)) + " " + staged(3, range(4)), "qSS")
        af(sg(1, 0), T.fb[:, 384:512], 1.0, -4.0, "fc0", "sg10")
        tt(sg(1, 2), T.fb[:, 512:640], T.fb[:, 640:768], A.subtract, "fc1 fc2", "sg12")
        for t, (a, b) in enumerate((("l8", "s"), ("l8", "sB"), ("lB", "sB"))):
            ts(sg(0, t), T.r16[:, 0:128], pc(a), pc(b), EQ, MUL, "r16 _%s _%s" % (a, b), "sg0%d" % t)
        qc(MU, 0, 2, staged(0, range(4)) + " " + staged(1, range(4)), "qMU")
        for t, (a, b) in enumerate((("s", "l8"), ("sB", "l8"), ("sB", "lB"))):
            ts(sg(2, t), T.r16[:, 0:128], pc(a), pc(b), EQ, MUL, "r16 _%s _%s" % (a, b), "sg2%d" % t)
        qc(MI, 2, 1, staged(2, range(4)), "qMI")
        ts(kf[:, 112:114], li[:, 16:18], 0.5, pc("tl"), MUL, ADD, "li1 _tl", "k8")
        ts(sub("tl"), kf[:, 112:114], NB - 1.0, None, A.min, None, "k8", "tl")

    def pick32(src, place, skey, mid, dst, dkey):
        cp(T[mid][:].indirect(place), src[:], skey + " px", mid)
        tt(T[mid + "t"][:], T[mid][:].indirect(sub("xy")), T.e10[:], MUL, mid + " xy e10", mid + "t")
        scan(dst[:], T.k10[:], T[mid + "t"][:], 0.0, MUL, ADD, "k10 %st" % mid, dkey)

    def et(b):
        return ct(E0 + SLOT.index(b))

    def decode(name, key, b, bank, out, okey):
        mm(bank, C, et(b), (name, 0), True, True, "qE " + key)
        act(out, ps[bank][:, 0:C], F.Copy, "ps%d" % bank, okey, scale=1.0 / 32)

    def so_view(i):
        u, t = (20 - i) // 4, (20 - i) % 4
        return T.sot[:, 4 * SOFF[u] + t:4 * (SOFF[u] + 16 * i):4], "so%d%d" % (u, t), T.jk[:, 8 * i * (i - 1):8 * i * (i + 1)]

    def shifts(h):
        return (DL, 8) if h < 2 else (DU, 16)

    def wins(h, bank):
        D, w = shifts(h)
        for u, ds in enumerate(D):
            i = 2 * h + u
            a, c, o, R = 512 * i, 128 + 256 * i, 128 * h, "dd%d" % h + BEFORE.get((h, u), "")
            for t, d in enumerate(ds):
                n = 128 - w * d
                tt(T.cot[:, a + t:a + 4 * n:4], T.dd[:, o:o + n], T.dd[:, o + w * d:o + 128], A.is_le, R, "co%d%d" % (i, t))
                if w * d < 64:
                    tt(T.cot[:, a + 4 * n + t:a + 512:4], T.dd[:, o + n:o + 128], T.dd[:, o:o + w * d], A.is_lt, R, "ct%d%d" % (i, t))
            qz("co", c, c + 128, T.cot[:, a:a + 512], " ".join("co%d%d ct%d%d" % (i, t, i, t) for t in range(4)), "cq%d" % i)
            ops[-1]["spare"] = AHEAD[i]
            mm(bank, 128, ("co", c), ct(KN), u == 0, False, "cq%d qKN" % i)
            for t, d in enumerate(ds):
                R = "cq%d qK cz%d cz%d" % (i, i, i + 1)
                if w * d < 64:
                    mm(bank, 128, ("co", c + 128 - w * d), ct(K0 + SLOT.index(t)), False, False, R)
                mm(bank, 128, ("co", c - w * d), ct(K0 + SLOT.index(t)), False, w * d == 64, R)

    def clear(out, W):
        if W[:3] in POOL:
            iota(out, [[0, out.shape[1]]], 0, 0, W)
        else:
            ms(out, 0.0, W)

    def clear_co(h):
        i = (1, 3, 4)[h]
        clear(T.cot[:, 512 * i + 259:512 * i + 512:4], "ct%d3" % i)

    def weigh(out, bank, bias, W):
        act(out, ps[bank][:, 0:NB // 2], F.Exp, "ps%d _%s" % (bank, bias), W, scale=-LN2, bias=pc(bias))

    def places(tile, banks, mid, out, okey):
        for h in chains:
            bank = banks[h]
            mm(bank, nq, ct(tile), ("s2", 128 * h), True, True, "qMU qMI s2q%d" % h)
            tt(T[mid][:, 80 * h:80 * h + nv], ps[bank][:, 0:nv], T.bs[:, 80 * h:80 * h + nv], ADD, "ps%d bs" % bank, mid + "xy"[h])
        cp(out, T[mid][:].indirect(sub("tl")), "%sx %sy tl" % (mid, mid), okey)

    for r in range(NR):
        s = str(r)
        xq, first, final = "x" + s, r == 0, r == NR - 1
        xk = "%sa %sb" % (xq, xq)
        pl, olist, hl, lp, ln, lv, lh = (sub(a + s) for a in ("pl", "ol", "hl", "lp", "ln", "lv", "lh"))
        mm(0, C, ("up", 0), (xq, 0), True, True, "up0c up0s " + xk)
        mm(3, C, ("up", 0), (xq, 0), True, True, "up0c up0s " + xk)
        bg(1)
        tt(T.sq[:], ps[0][:, 0:C], T.m16[:], A.min, "ps0 m16", "sq")
        bg(1)
        scan(T.sb[:], T.k16[:], T.sq[:], -BIG, A.min, A.max, "k16 sq", "sb")
        bg(1)
        mm(1, C, ("up", 128), (xq, 0), True, True, "up1c up1s " + xk)
        low, few = LOW[r], FEW[r]
        for i in range(19, low - 1, -1):
            view, key, jk = so_view(i)
            act(jk, ps[3][:, 0:16 * i], F.Sign, "sb ps3", "jk%d" % i, scale=-1.0, bias=T.sb[:, 16 * i + 15:16 * i + 16])
            act(view, jk, F.Relu, "jk%d sz0 sz1" % i, key + " rs%d" % i, accum_out=sub("rs", i, i + 1))
        after = {1: [0, 1], 2: [2], 3: [3], 4: [4]}
        for u in range(5):
            for t in range(4):
                i = 20 - 4 * u - t
                view, key, jk = so_view(i)
                if i == 20:
                    tt(T.dg[:], T.sb[:], ps[0][:, 0:C], A.is_ge, "sb ps0", "dg")
                    (cp if DIAG[0] else sc)(view, T.dg[:], "dg sz0", key)
                elif i < low and DIAG[1]:
                    ts(view, ps[0][:, 0:16 * i], T.sb[:, 16 * i + 15:16 * i + 16], None, A.is_lt, None, "sb ps0 sz%d" % u, key)
                    if i > few:
                        act(jk, view, F.Copy, key, "rs%d jk%d" % (i, i), accum_out=sub("rs", i, i + 1))
                    else:
                        op("V", lambda q, i=i, view=view: q.tensor_reduce(sub("rs", i, i + 1), view, AxisListType.X, ADD), key,
                           "rs%d" % i, max(64, 16 * i))
                elif i < low:
                    ts(jk, ps[0][:, 0:16 * i], T.sb[:, 16 * i + 15:16 * i + 16], None, A.is_lt, None, "sb ps0", "jk%d" % i)
                    if i > few:
                        act(view, jk, F.Copy, "jk%d sz%d" % (i, u), key + " rs%d" % i, accum_out=sub("rs", i, i + 1))
                    else:
                        ts(view, ps[0][:, 0:16 * i], T.sb[:, 16 * i + 15:16 * i + 16], None, A.is_lt, None, "sb ps0 sz%d" % u, key)
                        op("V", lambda q, i=i, jk=jk: q.tensor_reduce(sub("rs", i, i + 1), jk, AxisListType.X, ADD), "jk%d" % i,
                           "rs%d" % i, max(64, 16 * i))
            if u == 0:
                scan(T.ru[:], T.k01[:], T.dg[:], 0.0, MUL, ADD, "k01 dg", "ru")
            if u == 1:
                tt(sub("pre"), T.ru[:, 15:C:16], sub("cbs"), A.subtract, "cbs ru", "pre")
            for v in after.get(u, []):
                qz("so", SOFF[v], SOFF[v] + SWID[v], T.sot[:, 4 * SOFF[v]:4 * (SOFF[v] + SWID[v])],
                   " ".join("so%d%d" % (v, t) for t in range(4)), "soq%d" % v)
                mm(2, SWID[v], ct(WB), ("so", SOFF[v]), v == 0, v == 4, "qWB soq%d" % v)
        if first:
            qc(E0, 0, 4, " ".join(staged(i, range(4)) for i in range(4)), "qE")
        sc(T.mk[:], ps[1][:, 0:C], "ps1", "mk")
        arrive(nxt, "an" + s, 2, "n" + s)
        mm(1, C, ("up", 128), ("n" + s, 0), True, True, "up1c up1s n" + s)
        if first:
            consts_rows()
        for b in range(4):
            decode(xq, xk, b, 4 + b, slot(T.at, b, 0, C), "at%d" % b)
        scan(T.ls[:], T.pen[:], ps[2][:, 0:C], 0.0, ADD, A.max, "pen ps2", "ls")
        rows = " ".join("rs%d" % i for i in range(20))
        if LAST[0]:
            tt(sub("pre"), T.ls[:, 15:C:16], sub("pre"), A.subtract, "ls pre", "pre")
            tt(sub("pli"), sub("pre"), sub("rs"), A.subtract, "pre " + rows, "pli")
        else:
            tt(sub("pre"), sub("pre"), sub("rs"), ADD, "pre " + rows, "pre")
            tt(sub("pli"), T.ls[:, 15:C:16], sub("pre"), A.subtract, "ls pre", "pli")
        cp(pl, sub("pli"), "pli", "pl" + s)
        send(prv, lp, pl, "al" + s, "pl" + s)
        for a, b in PIECES:
            cp(T.orow[:].indirect(sub("pl" + s, a, b)), T.iot[:, 16 * a:16 * b], "iot px pl" + s, "orow")
        scan(T.ls[:], T.pen[:], T.orow[:], 0.0, ADD, A.max, "pen orow", "ls")
        ts(olist, T.ls[:, 15:C:16], pc("o0"), None, ADD, None, "ls _o0", "ol" + s)
        send(prv, ln, olist, "ao" + s, "ol" + s, spare=BULK[2])
        send(nxt, lv, olist, "av" + s, "ol" + s, spare=BULK[2])
        if first:
            sel(T.kr[:], T.zb[:, 0:130], [[-16, 13], [-1, 10]], A.not_equal, 1.0, 0, 1, "zb", "kr")
            for i in range(4):
                (cp if LIGHT[1] else sc)(sg(i, SLOT[i]), T.kr[:, 0:128], "kr", "sg%d%d" % (i, SLOT[i]))
                if LIGHT[2]:
                    ts(T.kn[:, i:512:4], T.kr[:, 0:128], -1.0, None, MUL, None, "kr", "kn%d" % i)
                else:
                    af(T.kn[:, i:512:4], T.kr[:, 0:128], -1.0, 0.0, "kr", "kn%d" % i)
            qc(K0, 0, 4, " ".join(staged(i, range(4)) for i in range(4)), "qK")
            ops[-1]["spare"] = SPARE[1]
            consts_court()
        pick32(T.mk, pl, "mk pl" + s, "ms", T.sa, "sa")
        sc(T.mn[:], ps[1][:, 0:C], "ps1", "mn")
        for a, b in ((0, 8), (8, 16), (16, 24)) if AEX[0] else ((0, 24),):
            sc(T.aex[:, 16 * a:16 * b], T.sa[:].indirect(sub("al", a, b)), "sa al0 al1", "aex%d" % (a // 8) if AEX[0] else "aex0 aex1 aex2")
        arrive(nxt, "al" + s, 1, "lp" + s)
        arrive(nxt, "ao" + s, 1, "ln" + s)
        arrive(prv, "av" + s, 1, "lv" + s)
        pick32(T.mn, lp, "mn lp" + s, "m2", T.sn, "sn")
        for h in range(2):
            a = slice(128 * h, 128 * h + 128)
            tt(T.d0[:, a], T.sn[:].indirect(sub("bl", 8 * h, 8 * h + 8)), T.aex[:, a], A.subtract, "sn bl0 aex%d" % h, "d0%d" % h)
            act(T.dd[:, a], T.d0[:, a], F.Abs, "d0%d" % h, "dd%d" % h)
        qz("g" + s, 0, C, T.at[:], "at0 at1 at2 at3", "g" + s)
        send_q(nxt, "g" + s, "p" + s, "ap" + s, "g%s pl%s #al%s" % (s, s, s))
        if first:
            for h in range(3):
                clear_co(h)
            clear(T.w2[:], "w20 w21 w22 w23")
            clear(T.st[:], "st00 st01 st02 st10 st11 st12")
            for h in chains if SPLIT[0] else ():
                clear(T.xs[:, 512 * h + 320:512 * h + 512], "xs%d0" % h)
            iota(T.r8[:], [[0, 16], [1, 8]], 0, 0, "r8")
            iota(T.lr[:], [[1, 16], [0, 8]], 0, 0, "lr")
            iota(T.bs[:], [[16, 2], [0, 8], [32, 10]], 0, 0, "bs")
            consts_weights()
            qz("c", 128 * KN, 128 * MX, T.kn[:, 0:512], "kn0 kn1 kn2 kn3", "qKN")
        for h in chains:
            ms(T.xs[:, 512 * h:512 * h + 4 * nv:2], 0.0, "xs%d0 xs%d2" % (h, h))
        for b in range(4):
            decode("n" + s, "n" + s, b, (0, 1, 2, 7)[b], plane(T.vp, b), "vp%d" % b)
            sc(plane(T.vo, b), plane(T.vp, b).indirect(ln), "vp%d ln%s" % (b, s), "vo%d" % b)
        def held(h, bank, bias):
            for t in (1, 3):
                weigh(T.xs[:, wide * h + t:wide * h + 320:4], bank, bias, "xw%d%d" % (h, t))

        for h in range(2):
            wins(h, 3 + h)
            held(h, 3 + h, "bw")
            weigh(T.wp[:, 80 * h:80 * h + 80], 3 + h, "bx", "wp%d" % h)
        tt(T.d0[:, 256:384], T.sn[:].indirect(sub("bl", 16, 24)), T.aex[:, 256:384], A.subtract, "sn bl1 aex2", "d02")
        act(T.dd[:, 256:384], T.d0[:, 256:384], F.Abs, "d02", "dd2")
        wins(2, 2)
        for h in range(2):
            for t in range(2):
                weigh(slot(T.w2, t, 80 * h, 80 * h + 80), 2, "u%d" % h, "w2%d" % (2 * h + t))
            weigh(T.wp[:, NB + 80 * h:NB + 80 * h + 80], 2, "u%d" % (h + 2), "wp%d" % (2 + h))
        qz("w2", 0, 208, T.w2[:], "w20 w21 w22 w23", "w2q")
        if first:
            dma("Y", T.lwc[:].bitcast(dt.uint8), T.wc[:], "wp1", "wq")
            dma("Y", T.lws[:], T.ws[:], "wp1", "wsc")
            dma("Y", T.vt[:], T.v[:], "wp1", "vt")
            consts_tail()
        arrive(prv, "ap" + s, 2, "p" + s)
        for b in (3, 0, 1, 2):
            decode("p" + s, "p" + s, b, (1, 3, 4, 1)[b], plane(T.gp, b), "gp%d" % b)
            sc(plane(T.go, b), plane(T.gp, b).indirect(lv), "gp%d lv%s" % (b, s), "go%d" % b)
        if final:
            sc(T.onr[:], T.iot[:].indirect(ln), "iot ln" + s, "onr")
        def tile(name, src, h, R, W):
            qz(name, 128 * h, 128 * h + nq, src[:, 512 * h:512 * h + 4 * nq], R, W)

        def part(buf, h, t):
            return buf[:, 512 * h + t:512 * h + 4 * nv:4]

        def ys(h, t):
            return slice(NB * t + 80 * h, NB * t + 80 * h + nv)

        for k in range(SW):
            for h in chains:
                x, lb, ub = ("xs", 128 * h), 5 + h, (7, 0)[h] if SPLIT[0] else (7, 0)[k % 2]
                if k == 0 and FIRST[0]:
                    js = (h,) if SPLIT[0] else (0, 1)
                    for j in js:
                        tt(T.st[:, 512 * j:512 * j + 512:4], T.cot[:, 1024 * j:1024 * j + 512].indirect(sub("zl")), T.er[:], EQ,
                           " ".join("co%d%d ct%d%d" % (2 * j, t, 2 * j, t) for t in range(4)) + " zl er", "st%d0 zz%d" % (h, j))
                    qz("s2", 128 * h, 128 * (js[-1] + 1), T.st[:, 512 * h:512 * (js[-1] + 1)],
                       "st%d0 st%d1 st%d2 " % (h, h, h) + " ".join("zz%d" % j for j in js), "s2q%d" % h)
                    for j in js:
                        a = wide * j
                        mm(5 + j, 128, ("s2", 128 * j), ct(K0), True, True, "qK s2q%d" % h)
                        tt(T.xs[:, a:a + 320:4], ps[5 + j][:, 0:80], T.xs[:, a + 1:a + 320:4], MUL, "ps%d xw%d1 xs%d0" % (5 + j, j, h),
                           "xf%d" % j)
                    continue
                tile("xs", T.xs, h, "xs%d0 xs%d2 xw%d1 xw%d3 xf%d" % (h, h, h, h, h) + ("" if SPLIT[0] else " xw11 xw13 xf1"), "xq%d" % h)
                if k == SW - 1:
                    continue
                mm(lb, nq, ct(MX), x, True, True, "qMX xq%d" % h)
                w = "wp"
                tt(T.ys[:, ys(h, 0)], ps[lb][:, 0:nv], T[w][:, ys(h, 0)], A.min, "ps%d wp%d" % (lb, h) + ("" if SPLIT[0] else " wp1"), "ys%d0" % h)
                ts(part(T.xs, h, 0), T.ys[:, ys(h, 0)], 0.0, SIG, A.max, MUL, "ys%d0" % h, "xs%d0" % h)
                if k >= 7:
                    mm(ub, nq, ct(MX + 2), ("w2", 80 * h), True, False, "qMU_ w2q")
                    mm(ub, nq, ct(MX + 1), x, False, True, "qMU_ xq%d" % h)
                    tt(T.ys[:, ys(h, 1)], ps[ub][:, 0:nv], T.wp[:, ys(h, 1)], A.min, "ps%d wp2 wp3" % ub, "ys%d1" % h)
                    ts(part(T.xs, h, 2), T.ys[:, ys(h, 1)], 0.0, SIG, A.max, MUL, "ys%d1" % h, "xs%d2" % h)
        for h in chains:
            for t in range(2):
                bank = ((3, 4), (1, 2))[h][t]
                mm(bank, nq, ct(SS + 1 - t), ("xs", 128 * h), True, True, "qSS xq%d" % h)
                tt(part(T.st, h, 2 * t), ps[bank][:, 0:nv], T.ys[:, ys(h, t)], A.is_lt, "ps%d ys%d%d" % (bank, h, t), "st%d%d" % (h, 2 * t))
            tile("st", T.st, h, "st%d0 st%d1 st%d2" % (h, h, h), "sq%d" % h)
            mm(5 + h, nq, ct(FA), ("st", 128 * h), True, True, "qMU sq%d" % h)
            ts(part(T.st, h, 1), ps[5 + h][:, 0:nv], pc("th"), None, EQ, None, "ps%d _th" % (5 + h), "st%d1" % h)
            tile("s2", T.st, h, "st%d0 st%d1 st%d2" % (h, h, h), "s2q%d" % h)
        if final:
            qz("v", 0, 128, T.vt[:], "vt", "vq")
        places(MI, (3, 1), "mt", sub("hl" + s, 0, 32), "hl" + s)
        send(nxt, lh, hl, "ah" + s, "hl" + s)
        places(MU, (4, 2), "mt2", sub("mu", 0, 32), "mu")
        runs = ((0, 1), (1, 2)) if RUNS[r] == 2 else ((0, 2),)
        for hf, hi in runs:
            for b in range(4):
                mm(HB[hf][b], H * (hi - hf), et(b), (xq, H * hf), True, False, "qE " + xk)
        for b in range(4):
            (cp if PICK[0][b] == "V" else sc)(plane(T.vq, b), plane(T.vo, b).indirect(sub("mu")), "vo%d mu" % b, "vq%d" % b)
            if PICK[2][b] == "F":
                (cp if PICK[1][b] == "V" else sc)(plane(T.vg, b), plane(T.vq, b).indirect(pl), "vq%d pl%s" % (b, s), "vg%d" % b)
        if final:
            (cp if OLE[0] == "V" else sc)(T.wrow[:], T.onr[:].indirect(sub("mu")), "onr mu", "wrow")
        arrive(prv, "ah" + s, 1, "lh" + s)
        for b in range(4):
            if PICK[2][b] == "F":
                sc(plane(T.zp, b), plane(T.go, b).indirect(lh), "go%d lh%s" % (b, s), "zp%d" % b)
            else:
                tt(plane(T.zp, b), plane(T.go, b).indirect(lh), plane(T.vq, b), A.max, "go%d vq%d lh%s" % (b, b, s), "zp%d" % b)
            for lo, hi in ((0, 2),) if WHOLE[b] else ((0, 1), (1, 2)):
                out, src = slot(T.zt, b, H * lo, H * hi), plane(T.zp, b).indirect(sub("pl" + s, 10 * lo, 10 * hi))
                W = " ".join("zt%d%d" % (hf, b) for hf in range(lo, hi))
                if PICK[2][b] == "F":
                    tt(out, src, plane(T.vg, b, H * lo, H * hi), A.max, "zp%d vg%d pl%s" % (b, b, s), W)
                else:
                    (cp if PICK[2][b] == "V" else sc)(out, src, "zp%d pl%s" % (b, s), W)
        if final:
            (cp if OLE[1] == "V" else sc)(T.wro2[:], T.wrow[:].indirect(pl), "wrow pl" + s, "wro2")
            dma("Y", T.ol[:], T.wro2[0:128:16, :], "wro2", "")
        for hf, hi in runs:
            lo, n = H * hf, H * (hi - hf)
            qz("z", lo, lo + n, T.zt[:, 4 * lo:4 * (lo + n)], " ".join("zt%d%d" % (j, b) for j in range(hf, hi) for b in range(4)), "zq%d" % hf)
            for b in range(4):
                mm(HB[hf][b], n, ("lw", 128 * b), ("z", lo), False, True, "wq wsc zq%d" % hf)
        xq = "x%d" % (r + 1)
        for hf, hi in runs:
            lo, n, key = H * hf, H * (hi - hf), " ".join(xq + "ab"[j] for j in range(hf, hi))
            for b in range(4):
                o, bank, W = slot(T.xn, b, lo, lo + n), HB[hf][b], " ".join("xn%d%d" % (j, b) for j in range(hf, hi))
                if XN[hf][b] == "V":
                    ts(o, ps[bank][:, 0:n], 1.0 / 32, None, MUL, None, "ps%d" % bank, W)
                else:
                    act(o, ps[bank][:, 0:n], F.Copy, "ps%d" % bank, W, scale=1.0 / 32)
            qz(xq, lo, lo + n, T.xn[:, 4 * lo:4 * (lo + n)], " ".join("xn%d%d" % (j, b) for j in range(hf, hi) for b in range(4)), key)
            if final:
                mm(hf, n, ("v", 0), (xq, lo), True, True, "vq " + key)
                dma("Y", T.oc[:, 4 * lo:4 * (lo + n)], T[xq + "c"][:, lo:lo + n].bitcast(dt.uint8), key, "")
                (cp if hi == 2 or OUT[0] == "V" else sc)(T.sq[:, lo:lo + n], ps[hf][:, 0:n], "ps%d sq" % hf, "yb%d" % hf)
                dma("Y", T.y[:, lo:lo + n], T.sq[:, lo:lo + n], "yb%d" % hf, "")
        if not final:
            send_q(prv, xq, "n%d" % (r + 1), "an%d" % (r + 1), "%sa %sb" % (xq, xq))
    for k in range(4):
        dma(OUT[1] if k % 2 else "S", T.osc[4 * k:4 * k + 4, :], T[xq + "s"][32 * k:32 * k + 4, :], "%sa %sb" % (xq, xq), "")
    emit(g, T, ops)
